import numpy as np, ml_dtypes
CORES = [16,18,20,22]
N = 4
BF = ml_dtypes.bfloat16
def gentries(a):
    return np.ascontiguousarray(a.reshape(8, 16, -1).transpose(0, 2, 1)).reshape(8, -1)
def gtable(e):
    e = np.asarray(e); return np.ascontiguousarray(e.reshape(8, -1, 16).transpose(0, 2, 1)).reshape(128, -1).astype(np.int32)
C, K0, NQ, T, L, DS, SB = 4096, 128, 128, 3, 4, 1, 14
KM = K0 + T * NQ
def machine(rng, k, p, q):
    cl = rng.permutation(np.concatenate([np.arange(k), rng.integers(0, k, C - k)]))
    o = np.argsort(cl, kind="stable"); size = np.bincount(cl, minlength=k); first = np.add.accumulate(size) - size
    x = rng.integers(0, k, (16, k))[:, cl]; nx = o[first[x] + rng.integers(0, size[x])]
    out = rng.integers(0, 16, (16, k))[:, cl]
    out = np.where(rng.random((16, C)) < p, rng.integers(0, 16, (16, C)), out)
    nx = np.where(rng.random((16, C)) < q, rng.integers(0, C, (16, C)), nx)
    return nx, out, cl
def machines(rng):
    nx = np.empty((N, 8, 16, C), np.int64); out = np.empty((N, 8, 16, C), np.int64)
    for r in range(N):
        for g in range(8):
            p = float(rng.choice(np.array([0.004, 0.01, 0.03])))
            nx[r, g], out[r, g], cl = machine(rng, int(rng.choice(np.array([30, 80, 200, 500]))), p, 0.3 * p)
    return nx, out
def others(rng):
    return (rng.integers(0, C, (N, 8, K0)), rng.integers(0, 2 ** SB, (N, 8, T, NQ)), rng.integers(0, 16, (N, 8, T, NQ)),
            rng.integers(0, 16, (N, 8, 16, L)), rng.integers(0, 16, (N, 8, T, 16, L)))
def fresh(rng, ex):
    b = C // (T + 1); c = np.arange(C)
    nx = rng.integers(0, C, (16, C)); out = rng.integers(0, 16, (16, C)); nx[15] = c
    for d in range(3): out[d] = (c >> (4 * d)) & 15
    for t in range(T): nx[3 + t] = (t + 1) * b + rng.integers(0, b, C)
    ex[13:] = 15; ex[13:, L - 1] = np.arange(3)
    return nx, out, rng.integers(0, b, K0), np.repeat(3 + np.arange(T), NQ).reshape(T, NQ)
def pack(nx, out, bk, qs, qc, ex, zs):
    return {"mt": np.ascontiguousarray(np.roll((16 * nx + out).reshape(N, 128, C), DS, axis=0)).astype(np.int32),
            "bk": np.stack([gtable(a) for a in bk]), "qs": np.stack([gtable(a.reshape(8, -1)) for a in qs]), "qc": np.stack([gtable(a.reshape(8, -1)) for a in qc]),
            "ex": np.ascontiguousarray(ex.reshape(N, 128, L)).astype(np.int32), "zs": np.ascontiguousarray(zs.transpose(0, 1, 3, 2, 4)).reshape(N, 128, T * L).astype(np.int32)}
def setup_inputs(rng):
    nx, out = machines(rng)
    return pack(nx, out, *others(rng))
def setup_inputs_grow(rng):
    nx, out = machines(rng); bk, qs, qc, ex, zs = others(rng); c = np.arange(C); h = C // 2
    for r in range(N):
        o = rng.permutation(8)
        for g in o[:3]: nx[r, g], out[r, g], bk[r, g], qc[r, g] = fresh(rng, ex[r, g])
        g = o[2]; nx[r, g, 4:3 + T] = np.where(c >= C // (T + 1), c, nx[r, g, 4:3 + T])
        qs[r, g, 1:, :8] = 2 ** SB - 1 - np.arange(8) * (2 ** SB // (K0 + NQ))
        for g in o[3:6]:
            k = int(rng.integers(20, 61)); nx[r, g], out[r, g], cl = machine(rng, k, 0.0, 0.0)
            one = np.unique(cl, return_index=True)[1]
            bk[r, g] = rng.permutation(np.concatenate([one, rng.integers(0, C, K0 - k)]))
        g = o[5]
        nx[r, g, 15] = c; out[r, g, 15] = np.where(c < h, 3, 9); nx[r, g, 14, :h] = rng.integers(h, C, h)
        one = np.unique(cl[:h], return_index=True)[1]
        bk[r, g] = rng.permutation(np.concatenate([one, rng.integers(0, h, K0 - len(one))]))
        qc[r, g, 0] = 14; ex[r, g] = rng.integers(0, 14, (16, L)); zs[r, g, 0, int(rng.integers(1, 16))] = 15
    return pack(nx, out, bk, qs, qc, ex, zs)
def setup_inputs_near(rng):
    nx = np.empty((N, 8, 16, C), np.int64); out = np.empty((N, 8, 16, C), np.int64); bk, qs, qc, ex, zs = others(rng)
    for r in range(N):
        for g in range(8):
            x, y, cl = machine(rng, 40, 0.0, 0.0); y = np.minimum(np.maximum(y, 1), 14); x[15] = np.arange(C)
            c = np.flatnonzero(rng.random(C) < 0.5); a = rng.integers(0, 16, len(c)); b = (a + rng.integers(1, 16, len(c))) & 15
            y[a, c] += 1
            if (r + g) & 1: y[b, c] -= 1
            nx[r, g] = x; out[r, g] = y; ex[r, g] = 15; ex[r, g, :, L - 1] = rng.permutation(16)
    return pack(nx, out, bk, qs, qc, ex, zs)
def setup_inputs_alike(rng):
    nx, out = machines(rng); bk, qs, qc, ex, zs = others(rng)
    bk[:, ::2] = np.take_along_axis(rng.integers(0, C, (N, 4, 6)), rng.integers(0, 6, (N, 4, K0)), 2)
    zs = np.take_along_axis(zs, rng.integers(0, 5, (N, 8, T, 16))[..., None], 3)
    ex[:, 1::4] = np.repeat(ex[:, 1::4, :4], 4, axis=2)
    qs[:, 3] = rng.integers(0, 2 ** SB, 4)[rng.integers(0, 4, (N, T, NQ))]; qc[:, 3] = rng.integers(0, 16, 2)[rng.integers(0, 2, (N, T, NQ))]
    for r in range(N):
        nx[r, 5], out[r, 5], bk[r, 5], qc[r, 5] = fresh(rng, ex[r, 5])
        qs[r, 5] = rng.integers(0, 2 ** SB, 3)[rng.integers(0, 3, (T, NQ))]
    c = np.arange(C)
    nx[:, 7] = np.where(rng.random((N, 16, C)) < 0.1, 0, rng.integers(0, C, (N, 16, C))); nx[:, 7, 15] = c
    out[:, 7] = np.where((c == 0) | (c >= C // 2), 0, rng.integers(1, 16, (N, 16, C)))
    out[1::2, 7] = 15 - out[1::2, 7]
    bk[:, 7] = rng.integers(1, C // 2, (N, K0)); qc[:, 7] = rng.integers(0, 15, (N, T, NQ))
    ex[:, 7] = 15; ex[:, 7, :, L - 1] = np.argsort(rng.random((N, 16)), axis=-1)
    for r in range(N):
        if r & 2:
            nx[r, 7, 14] = np.where(rng.random(C) < 0.5, bk[r, 7][rng.integers(0, K0, C)], rng.integers(1, C // 2, C))
            qc[r, 7, 0] = 14; zs[r, 7, :, :, :L - 1] = 15
    return pack(nx, out, bk, qs, qc, ex, zs)
def setup_inputs_ends(rng):
    nx, out = machines(rng); bk, qs, qc, ex, zs = others(rng); e = np.array([0, C - 1]); l = np.array([0, 15])
    nx = np.where(rng.random(nx.shape) < 0.2, e[rng.integers(0, 2, nx.shape)], nx)
    qs[:, ::2] = np.array([0, 2 ** SB - 1])[rng.integers(0, 2, (N, 4, T, NQ))]
    qs[:, 1::2, 0] = (rng.integers(0, K0, (N, 4, NQ)) * (2 ** SB // K0) - rng.integers(0, 2, (N, 4, NQ))) & (2 ** SB - 1)
    qc[:, 1] = l[rng.integers(0, 2, (N, T, NQ))]; bk[:, 2] = e[rng.integers(0, 2, (N, K0))]; bk[:, :, 0] = 0; bk[:, :, K0 - 1] = C - 1
    ex[:, 4] = l[rng.integers(0, 2, (N, 16, L))]; zs[:, 4] = l[rng.integers(0, 2, (N, T, 16, L))]; ex[:, 5] = 15; zs[:, 7] = 0
    return pack(nx, out, bk, qs, qc, ex, zs)
def setup_inputs_spread(rng):
    a = rng.choice(np.array([1, 3, 8]), (N, 8, 1, 1)); b = rng.choice(np.array([1, 2, 6]), (N, 8, 1, 1))
    nx = (C * rng.random((N, 8, 16, C)) ** a).astype(np.int64); out = (16 * rng.random((N, 8, 16, C)) ** b).astype(np.int64)
    bk = (C * rng.random((N, 8, K0)) ** a[..., 0]).astype(np.int64); qs = (2 ** SB * rng.random((N, 8, T, NQ)) ** b).astype(np.int64)
    qc = (16 * rng.random((N, 8, T, NQ)) ** 2).astype(np.int64)
    ex = (16 * rng.random((N, 8, 16, L)) ** 2).astype(np.int64); zs = (16 * rng.random((N, 8, T, 16, L)) ** 2).astype(np.int64)
    return pack(nx, out, bk, qs, qc, ex, zs)
def check_inputs(d):
    bad = []
    for k, hi in (("mt", 16 * C - 1), ("bk", C - 1), ("qs", 2 ** SB - 1), ("qc", 15), ("ex", 15), ("zs", 15)):
        if np.min(d[k]) < 0 or np.max(d[k]) > hi: bad.append("range of " + k)
    return bad
def walk(tb, q, w):
    r = np.arange(N)[:, None, None, None]; g = np.arange(8)[None, :, None, None]; s = q[:, :, None, :]
    for i in range(L):
        v = tb[r, g, w[:, :, :, i][..., None], s]; s = v >> 4
    return v & 15
def reference(mt, bk, qs, qc, ex, zs):
    tb = np.roll(mt.astype(np.int64), -DS, axis=0).reshape(N, 8, 16, C)
    s_ = np.stack([gentries(a) for a in qs]).astype(np.int64).reshape(N, 8, T, NQ); c_ = np.stack([gentries(a) for a in qc]).astype(np.int64).reshape(N, 8, T, NQ)
    E = ex.astype(np.int64).reshape(N, 8, 16, L); Z = zs.astype(np.int64).reshape(N, 8, 16, T, L)
    kn = np.zeros((N, 8, KM), np.int64); rec = np.zeros((N, 8, 16, KM), np.int64); cnt = np.full((N, 8, 1), K0, np.int64)
    kn[:, :, :K0] = np.stack([gentries(a) for a in bk]); rec[..., :K0] = walk(tb, kn[:, :, :K0], E)
    r3 = np.arange(N)[:, None, None]; g3 = np.arange(8)[None, :, None]; ms = []
    for t in range(T):
        b = np.take_along_axis(kn, (s_[:, :, t] * cnt) >> SB, 2)
        q = tb[r3, g3, c_[:, :, t], b] >> 4
        rq = walk(tb, q, E)
        eq = np.broadcast_to((np.arange(KM) < cnt)[:, :, None, :], (N, 8, NQ, KM))
        for e in range(16): eq = eq & (rq[:, :, e, :, None] == rec[:, :, e, None, :])
        hit = np.any(eq, axis=3); new = (~hit).astype(np.int64)
        m = np.where(hit, np.argmax(eq, axis=3), cnt + np.add.accumulate(new, axis=2) - new)
        i, j, n = np.nonzero(new)
        kn[i, j, m[i, j, n]] = q[i, j, n]; rec[i, j, :, m[i, j, n]] = rq[i, j, :, n]
        cnt = cnt + np.add.reduce(new, axis=2)[..., None]; ms.append(m)
        zt = Z[:, :, :, t]
        differ = walk(tb, q, zt) != walk(tb, np.take_along_axis(kn, m, 2), zt)
        best = np.argmax(np.add.reduce(differ.astype(np.int64), axis=3), axis=2)
        E[:, :, t] = zt[r3[..., 0], g3[..., 0], best]
        rec[:, :, t] = walk(tb, kn, E[:, :, t:t + 1])[:, :, 0]
    rec = np.where((np.arange(KM) < cnt)[:, :, None, :], rec, -1)
    return {"ym": np.concatenate(ms, axis=2).astype(np.float32), "yr": rec.reshape(N, 128, KM).astype(np.float32), "ye": E.reshape(N, 128, L).astype(np.float32)}

@@ -1,0 +1,685 @@
+from concourse.mybir import AluOpType, AxisListType, ActivationFunctionType
+
+OP = AluOpType
+AF = ActivationFunctionType
+CWS = [256, 1024, 1024, 1024, 512, 256]
+NCH = len(CWS)
+OWS = [2048, 2048]
+C27 = 201326592.0
+C23 = 12582912.0
+EPS = 0.499969482421875
+PARTS = 4
+DIGITS = "0123456789abcdefghijklmnopqrstuvwxyzABCDEFGHIJKLMNOPQRSTUVWXYZ"
+ORDER = (
+    "1W2400083l040c020g0w060k0a0o0s203j0e3f3h2i2g2c2e2k4c7x0A3d2m"
+    "0i0E8h1Y2o7N2q2a4G8C2y2230342W322u2A0I2Y28262U2S360K0m2s2C2K"
+    "3r2I2M8j382H4p3N8d8f4i2E2O2Q7v0O8r4k1i4q4m4e2w584Q0q4K0u0U4O"
+    "4M0y0C1m0G0Q0M1u0W0S4S1k10121o4I1c161y1q0Y184U564y4w4A141e1s"
+    "1A5A1w1O1C1G3u3m1a4Y4C1K1g1I4u4W5C541E3p5y526A5c3E1Q5w3P5E4s"
+    "4g5G5a3a1M1S3t5I5O506E5K6G5Q3H603z6C3w5o5e5m5S3K1U639a5g5k5q"
+    "5s5i5W5Y423Q3S5U646c683C466S6j666I6M6a6Q3J6e6o6O6K6k709c6u6U"
+    "6W9e6g6Y6q74726m7c9g776s8Y3U9i9k6w3X786y7j407a7o7e7g9m7O9o7k"
+    "7ma23A3Z9r7S458O8K7WaW7qbm8F888H7t9saYa8aa8S8R7Q9uaha7alajaf"
+    "9wad9yb59A488m9C4a8M8I9094968W8Uamaqaub0aoas84ayawaCb2b6aAaE"
+    "aO86b88abh8Ba4baaGaIaK9E9GaSaQ9I92aUbcbiaMbObSbQbU7UbWbY5Nc0"
+    "9Kc6c89M4Ecc9Ocabobubec29Qcec4cobl7ycg8kcr9S9UbqcicA5u7YcFcC"
+    "cGbw9W9Ybsbya0bBbG8ucIdgcMdidkcKcOdB8obM98kybIbCckbKdGdmbFdC"
+    "dpcucmcQdqdEcScWcwdscUcYd07Adud3dPdwe2dzcydNdId4d6dcd9dbfsdQ"
+    "eodKdSdee4eqesdVfxdWeudY7Ce6e1ekewfueae9808xeeed8sey82fyehei"
+    "eEeReOeDeHeLeJeNeAfActfEeSfKemeW7EeUf0eYfCf4f2f8f6fcfofqfafe"
+    "kCfkfgfmfGfifM7GfWg0fYg2fIfQg4gag68zfOg87KgcgegggwgygkgigCgm"
+    "gogJgOfSgqfUlPgUlQgZh0gQgSgKgM7IhchbhCh6gsh2h4gEguhehMgGhEhg"
+    "h8gXhihkhGhmhIhohThqhKhOhshYi0gAi2huhzhxhQhUiyi4hAi6i9hWiilS"
+    "iAiailiCiEicifigkGimiGiuipjCiqiIixkBitiPiNiXiZiTj1iQiUjEiKkE"
+    "j6j2jMj8jaj4jijcjGjejkjmjgjojujwjqjsjyjIjAkakik6jKkkkojOjQk8"
+    "kukckPkUkekgjSjUjXkQkWjYk1kSkYk2kmkIkql0l3k5kskwl4lMl6kKl8la"
+    "lclelhltlulilwlklolqlylUlWlnlBlCkMlElGlJlKlYm0m2")
+SETS = [(1, 0), (2, 0), (1, 1), (2, 1), (1, 2), (1, 3), (2, 2), (2, 3)]
+BLOCKS, PAIR, WSET = 6, 8192, 2064
+
+F, B, H, I, U = "float32", "bfloat16", "float16", "int32", "uint16"
+SCRATCH = {}
+for _n, _w, _d in [
+        ("mti", 4096, I), ("wt", 4096, F), ("ob", 4096, B), ("xw", 4096, F), ("ow", 4096, B),
+        ("wd", 16, I), ("bki", 8, I), ("qsi", 24, I), ("qci", 24, I), ("pi", 8, I), ("ix", 24, F),
+        ("qg", 128, F), ("qm", 128, F), ("pg", 128, F), ("c16", 32, F), ("io640", 640, F), ("c8", 8, F),
+        ("blk", 128, B), ("eqm", 128, B), ("i128", 128, B), ("jb", 16, B), ("jj", 2048, B), ("nj", 128, B),
+        ("blkp", 128, B), ("tmp", 256, B), ("tmb", 128, B), ("pmx", 128, B), ("blkpp", 128, B), ("blki", 128, B), ("cst", 128, B),
+        ("b16", 128, B), ("d15", 128, B), ("low", 128, B), ("zb", 248, B), ("b8f", 16, F), ("keep", 384, B), ("cole", 16, F),
+        ("nlneg", 8, H), ("npm", 8, F), ("cnp", 8, F), ("neg1", 384, F), ("z8", 8, F), ("c15", 16, B),
+        ("wdf", 24, F), ("dd", 512, B), ("wrb", 512, B), ("dm", 128, B), ("msk", 128, B),
+        ("sel", PAIR + BLOCKS * WSET, B), ("st", 256, B), ("qcl", 24, U), ("lrow", 384, F), ("lm", 384, B), ("qsf", 24, F), ("bkl", 8, U),
+        ("ki", 8, I), ("kl", 8, U), ("qgt", 128, H), ("ql", 8, U), ("xi", 128, F), ("xl0", 128, U), ("xl1", 128, U), ("xk", 640, F),
+        ("y0", 2048, H), ("y1", 2048, H), ("y2", 2048, H), ("y3", 2048, H), ("g3", 8192, H), ("g4", 8192, B), ("gt", 2048, B),
+        ("l30", 128, U), ("l31", 128, U), ("l32", 128, U), ("l33", 128, U), ("lm3", 128, U),
+        ("l40", 128, U), ("l41", 128, U), ("l42", 128, U), ("l43", 128, U), ("l44", 128, U),
+        ("pz0", 512, F), ("pz1", 512, F), ("pz2", 512, F), ("pzn", 640, F), ("rr", 512, B), ("rn", 640, B), ("invn", 512, B), ("an", 256, B),
+        ("r2", 384, B), ("rq2", 128, B), ("lhb", 1024, B),
+        ("sc", 3072, F), ("nn", 8, F), ("vl", 8, F), ("uu", 8, H), ("inc", 8, H), ("ww", 8, H), ("mn", 8, H), ("ml", 8, U), ("cnt", 4, H),
+        ("pl", 24, U), ("num", 512, F), ("ymt", 384, F), ("inv", 128, B),
+        ("aq", 128, B), ("ne", 128, B), ("sm", 8, F), ("dd2", 16, B), ("oh", 4, F), ("ws", 4, B),
+        ("mk", 16, F), ("ya", 16, F), ("pw", 512, H), ("lw", 32, U), ("gw", 512, H), ("lw2", 32, U),
+        ("gz0", 512, B), ("gz1", 512, B), ("gz2", 512, B), ("yrt", 512, F)]:
+    SCRATCH[_n] = ("sbuf", [128, _w], _d)
+PSUM = ["pa0", "pa1", "pb0", "pb1", "pc0", "pc1", "pd0", "pe0"]
+for _n in PSUM:
+    SCRATCH[_n] = ("psum", [128, 512], F)
+SEMAPHORES = (["cv", "cs", "cp", "cg", "sent", "dex", "dzs", "dbk", "dqs", "dqc", "dym", "dyr", "dye"] + ["dmt%d" % h for h in range(NCH)]
+              + ["arr%d" % h for h in range(NCH + len(OWS))])
+CSEM = {"V": "cv", "S": "cs", "P": "cp", "G": "cg"}
+PLAN = {}
+
+
+def plan(ops):
+    out = []
+    for k in range(0, len(ORDER), 2):
+        c = 62 * DIGITS.index(ORDER[k]) + DIGITS.index(ORDER[k + 1])
+        out.append((c // 2, list(ops[c // 2]["alt"])[c % 2]))
+    return out
+
+
+def rank_program(g, core, T, topo):
+    rank = T.rank_of(core)
+    if rank is None:
+        return
+    queue = {"V": g.vector, "S": g.scalar, "P": g.tensor, "G": g, "Y": g.sync, "D": None}
+    ops = []
+    wrote, readers = {}, {}
+
+    def view(name, c0=0, c1=None, st=1):
+        if c1 is None:
+            c1 = SCRATCH[name][1][1]
+        ap = T[name][:, c0:c1] if st == 1 else T[name][:, c0:c1:st]
+        return (ap, name, c0, c1, (c1 - c0 + st - 1) // st)
+
+    def do(alt, reads, writes, free=False, tok=None, lat=0.0, dep=()):
+        i = len(ops)
+        deps, soft = set(dep), set()
+        for v in reads:
+            ps = v[1] in PSUM
+            for (a, b, j) in wrote.get(v[1], []):
+                if a < v[3] and v[2] < b:
+                    deps.add(j)
+                elif ps:
+                    soft.add(j)
+            if ps:
+                soft.update(j for (a, b, j) in readers.get(v[1], []))
+        for v in writes:
+            ps = v[1] in PSUM
+            for (a, b, j) in wrote.get(v[1], []):
+                if ps:
+                    soft.add(j)
+                elif a < v[3] and v[2] < b and not (free and ops[j]["free"]):
+                    deps.add(j)
+            for (a, b, j) in readers.get(v[1], []):
+                if a < v[3] and v[2] < b:
+                    deps.add(j)
+                elif ps:
+                    soft.add(j)
+        ops.append({"alt": alt, "lat": lat, "deps": deps, "soft": soft - deps, "tok": tok, "free": free, "run": None,
+                    "nm": writes[0][1] if writes else "-"})
+        for v in writes:
+            if not free:
+                for d in (wrote, readers):
+                    d[v[1]] = [r for r in d.get(v[1], []) if not (v[2] <= r[0] and r[1] <= v[3])]
+            wrote.setdefault(v[1], []).append((v[2], v[3], i))
+        for v in reads:
+            readers.setdefault(v[1], []).append((v[2], v[3], i))
+        return i
+
+    chains = {}
+
+    def chain(q, i):
+        if q in chains:
+            ops[i]["soft"].add(chains[q])
+        chains[q] = i
+
+    def flight(i, out, us, tok, lat):
+        j = do({"D": (None, (0, 0, 0, 0, us, 0))}, [], out, tok=tok, lat=lat, dep=[i])
+        chain("D", j)
+
+    def dma(q, out, in_ap, sem, us):
+        i = do({q: (lambda e: e.dma_start(out[0], in_ap).then_inc(T.sem[sem], 16), (0.1, 0, 0, 0))}, [], [], tok=())
+        chain(q, i)
+        flight(i, [out], us, (sem, 16), 2.0)
+
+    def sca(s):
+        return [s] if isinstance(s, tuple) else []
+
+    def val(s):
+        return s[0] if isinstance(s, tuple) else s
+
+    def two(*vs):
+        return all(SCRATCH[v[1]][2] in (B, H, U) for v in vs)
+
+    def dv(n, half=False):
+        return (0.03, max(64, n * (0.5 if half else 1.0)), 0, 0)
+
+    def ind(v, idx):
+        return v[0] if idx is None else v[0].indirect(idx[0])
+
+    def lst(idx):
+        return [] if idx is None else [idx]
+
+    def a_ts(out, in0, s1, op0, s2=None, op1=None, idx=None):
+        i0 = ind(in0, idx)
+        w = dv(out[4], two(out, in0)) if idx is None else (0.05, 0, out[4], 0)
+        if op1 is None:
+            return (lambda e: e.tensor_scalar(out[0], i0, val(s1), None, op0), w)
+        return (lambda e: e.tensor_scalar(out[0], i0, val(s1), val(s2), op0, op1), w)
+
+    def a_act(out, in_, scale=1.0, bias=0.0, func=AF.Identity, idx=None):
+        i0 = ind(in_, idx)
+        return (lambda e: e.activation(out[0], i0, func, bias=val(bias), scale=val(scale)),
+                (0.065, 0, out[4], 0) if idx else (0.065, out[4], 0, 0))
+
+    def a_cp(out, in_, idx=None):
+        i0 = ind(in_, idx)
+        return (lambda e: e.tensor_copy(out[0], i0), dv(out[4], two(out, in_)) if idx is None else (0.05, 0, out[4], 0))
+
+    def ts(out, in0, s1, op0, s2=None, op1=None, free=False, idx=None):
+        do({"V": a_ts(out, in0, s1, op0, s2, op1, idx)}, [in0] + sca(s1) + sca(s2) + lst(idx), [out], free)
+
+    def tt(out, in0, in1, op, idx=None):
+        i0 = ind(in0, idx)
+        w = (0.05, 0, out[4], 0) if idx else dv(out[4] * (1 if in0[1] in PSUM or in1[1] in PSUM else 2))
+        do({"V": (lambda e: e.tensor_tensor(out[0], i0, in1[0], op), w)}, [in0, in1] + lst(idx), [out])
+
+    def cp(out, in_, idx=None):
+        do({"V": a_cp(out, in_, idx)}, [in_] + lst(idx), [out])
+
+    def fill(out, c):
+        do({"V": (lambda e: e.memset(out[0], c), dv(out[4], two(out)))}, [], [out])
+
+    def scatter(win, idx, in_):
+        do({"V": (lambda e: e.tensor_copy(win[0].indirect(idx[0]), in_[0]), (0.05, 0, 2 * in_[4], 0))}, [in_, idx], [win])
+
+    def scan(out, d0, d1, init, op0, op1):
+        do({"V": (lambda e: e.tensor_tensor_scan(out[0], d0[0], d1[0], init, op0, op1), dv(out[4]))}, [d0, d1], [out])
+
+    def reduce(out, in_, op):
+        do({"V": (lambda e: e.tensor_reduce(out[0], in_[0], AxisListType.X, op), dv(in_[4]))}, [in_], [out])
+
+    def act(out, in_, scale=1.0, bias=0.0, func=AF.Identity, idx=None):
+        do({"S": a_act(out, in_, scale, bias, func, idx)}, [in_] + sca(scale) + sca(bias) + lst(idx), [out])
+
+    def move(out, in_, idx=None):
+        do({"S": a_act(out, in_, idx=idx), "V": a_cp(out, in_, idx)}, [in_] + lst(idx), [out])
+
+    def scale(out, in_, col, free=False, idx=None):
+        do({"S": a_act(out, in_, col, idx=idx), "V": a_ts(out, in_, col, OP.mult, idx=idx)}, [in_, col] + lst(idx), [out], free)
+
+    def lin(out, in_, s, b=0.0):
+        do({"V": a_ts(out, in_, s, OP.mult, b, OP.add), "S": a_act(out, in_, s, b)}, [in_] + sca(s) + sca(b), [out])
+
+    def step(out, idx):
+        do({"S": a_act(out, xw, 0.0625, -C23 - 2048.0, idx=idx), "V": a_ts(out, xw, 0.0625, OP.mult, -C23 - 2048.0, OP.add, idx=idx)},
+           [xw, idx], [out])
+
+    def mms(out, pairs, f=1, parts=1):
+        n = len(pairs)
+        for m in range(parts):
+            lo, hi = n * m // parts, n * (m + 1) // parts
+
+            def fn(e, lo=lo, hi=hi):
+                for k in range(lo, hi):
+                    r = e.matmul(out[0], pairs[k][0][0], pairs[k][1][0], k == 0, k == n - 1)
+                return r
+            do({"P": (fn, (0, 0, 0, f * (hi - lo) * max(64, out[4])))}, [p for pr in pairs[lo:hi] for p in pr], [out])
+
+    def iota(out, pattern, base=0, cm=0):
+        if out[1] == "pi":
+            fn = lambda e: e.iota(out[0], pattern, base, cm)
+        else:
+            fn = lambda e: e.iota(out[0], pattern, base, cm, allow_small_or_imprecise_dtypes=True)
+        return do({"G": (fn, (0.13, 2 * out[4], 0, 0))}, [], [out])
+
+    def const(v, c=0):
+        do({"G": (lambda e: e.iota(v[0], [[0, v[4]]], c, 0, allow_small_or_imprecise_dtypes=True), (0.13, 2 * v[4], 0, 0)),
+            "V": (lambda e: e.memset(v[0], float(c)), dv(v[4], two(v)))}, [], [v])
+
+    def zeros(name, c):
+        for a in range(c, c + 2048, 512):
+            const(view(name, a, a + 512))
+
+    c0 = [sum(CWS[:h]) for h in range(NCH)]
+    dma("S", view("wd", 0, 4), T.ex[:], "dex", 0.1)
+    dma("S", view("wd", 4, 16), T.zs[:], "dzs", 0.1)
+    for h in range(NCH):
+        dma("Y", view("mti", c0[h], c0[h] + CWS[h]), T.mt[:, c0[h]:c0[h] + CWS[h]], "dmt%d" % h, 5.2 * CWS[h] / 4096)
+    dma("S", view("bki"), T.bk[:], "dbk", 0.1)
+    dma("S", view("qci"), T.qc[:], "dqc", 0.1)
+    dma("S", view("qsi"), T.qs[:], "dqs", 0.1)
+
+    dst = T.cores[(rank - 1) % len(T.cores)]
+    rid, pid, _ = topo.addr(dst)
+    emask = topo.mask(core, dst)
+    neng = len(topo.engines(core, dst))
+
+    def send(out, v, us, h):
+        i = do({"G": (lambda e: e.remote_dma(out[0], v[0], T.sem["arr%d" % h], T.sem.sent, pid, rid, emask),
+                      (0, 0, 0, 0, 1.0, 0 if h else 1))}, [v], [], tok=())
+        chain("G", i)
+        flight(i, [out], us, ("arr%d" % h, neng), 1.0)
+    for h in range(NCH):
+        a, b = c0[h], c0[h] + CWS[h]
+        ts(view("wt", a, b), view("mti", a, b), -7.5, OP.add, C27, OP.add)
+        send(view("xw", a, b), view("wt", a, b), 5.2 * CWS[h] / 4096, h)
+    for k in range(8):
+        a = 512 * k
+        bank = view(("pc0", "pc1", "pb0", "pb1")[k % 4])
+        act(bank, view("wt", a, a + 512), bias=-C27)
+        tt(view("ob", a, a + 512), view("mti", a, a + 512), bank, OP.subtract)
+    for h in range(len(OWS)):
+        a = sum(OWS[:h])
+        send(view("ow", a, a + OWS[h]), view("ob", a, a + OWS[h]), 2.6 * OWS[h] / 4096, NCH + h)
+
+    iota(view("pi", 0, 1), [[0, 1]], 0, 1)
+    iota(view("qg"), [[1, 8], [0, 16]])
+    iota(view("qm"), [[0, 8], [1, 16]], 1)
+    iota(view("c16", 0, 16), [[16, 16]], 1)
+    iota(view("pg"), [[0, 16], [1, 8]])
+    iota(view("c8"), [[16, 8]])
+    iota(view("c16", 16, 32), [[-1, 16]], 15)
+    iota(view("io640"), [[1, 640]])
+    pi = view("pi", 0, 1)
+    ts(view("pi", 4, 5), pi, 15, OP.bitwise_and)
+    ts(view("pi", 5, 6), pi, 4, OP.arith_shift_right)
+    ts(view("pi", 6, 7), pi, 7, OP.bitwise_and)
+    ts(view("pi", 7, 8), pi, 3, OP.arith_shift_right)
+    cp(view("ix", 0, 4), view("pi", 4, 8))
+
+    def ix(k):
+        return view("ix", k, k + 1)
+    A_, G_, PG_, PI_ = ix(0), ix(1), ix(2), ix(3)
+    A1, PI1, A15 = ix(4), ix(5), ix(7)
+    ts(A1, A_, 1.0, OP.add)
+    ts(view("blk"), view("qg"), G_, OP.is_equal)
+    ts(view("eqm"), view("qm"), A1, OP.is_equal)
+    tt(view("i128"), view("eqm"), view("blk"), OP.mult)
+    ts(view("b8f", 0, 8), view("pg", 0, 8), G_, OP.is_equal)
+    ts(view("b8f", 8, 16), view("b8f", 0, 8), -2048.0, OP.mult)
+    cp(view("wdf", 0, 16), view("wd"))
+    ts(view("wdf", 16, 20), view("wdf", 0, 16, 4), 16.0, OP.mult, 1.0, OP.add)
+    tt(view("wdf", 20, 24), view("wdf", 16, 20), view("wdf", 1, 16, 4), OP.add)
+    ts(view("cole"), view("c16", 0, 16), A_, OP.add)
+    for k in range(4):
+        scale(view("dd", 128 * k, 128 * k + 128), view("i128"), view("wdf", 20 + k, 21 + k))
+    mms(view("pa0"), [(view("blk"), view("dd"))])
+    act(view("wrb"), view("pa0"))
+    for k in range(8):
+        c = 4 * SETS[k][1] + 1 + SETS[k][0]
+        scale(view("dm", 16 * k, 16 * k + 16), view("eqm", 0, 16), view("wdf", c, c + 1))
+    mms(view("pa1", 0, 128), [(view("blk"), view("dm"))])
+    ts(view("msk"), view("pa1", 0, 128), A_, OP.is_equal)
+
+    def block(kind, s):
+        return PAIR + WSET * SETS.index((kind, s))
+
+    def sel(kind, s, i, w=128):
+        if kind:
+            c = block(kind, s) + 128 * i
+        else:
+            c = 2048 + 384 * i + 128 * (s - 1) if s else 128 * i
+        return view("sel", c, c + w)
+
+    def build0(s, w):
+        for i in range(16):
+            ts(sel(0, s, i, w), view("wrb", 128 * s, 128 * s + w), view("cole", i, i + 1), OP.is_equal, free=True)
+
+    def spread(buf, lo, hi, first, last, st):
+        for k in range(8):
+            scale(view(buf, first(k), last(k), st), view("msk", 16 * lo, 16 * hi), view("b8f", k, k + 1), free=True)
+
+    def build(lo, hi):
+        spread("sel", lo, hi, lambda k: PAIR + WSET * lo + 16 * k, lambda k: PAIR + WSET * (hi - 1) + 129 * 15 + 16 * k + 1, 129)
+
+    def buildS():
+        spread("st", BLOCKS, 8, lambda k: k, lambda k: 256, 8)
+
+    def jj(i):
+        return view("jj", 128 * i, 128 * i + 128)
+
+    zeros("jj", 0)
+    zeros("sel", PAIR)
+    zeros("sel", PAIR + WSET)
+    const(view("neg1"), -1)
+    for k in range(2, BLOCKS):
+        zeros("sel", PAIR + WSET * k)
+    const(view("rn"), -1)
+    const(view("pzn"))
+    fill(view("jb"), 1.0)
+    for k in range(8):
+        scale(view("jj", 16 * k, 2048, 129), view("jb"), view("b8f", k, k + 1), free=True)
+
+    cp(view("bkl"), view("bki"))
+    cp(view("qcl"), view("qci"))
+    ts(view("qsf"), view("qsi"), 1.0 / 16384, OP.mult)
+    act(view("lrow"), view("io640"), idx=view("qcl"))
+    ts(view("lm"), view("lrow"), A_, OP.is_equal)
+    const(view("xk", 128, 640))
+    const(view("cnt", 0, 1), 128)
+    build0(0, 128)
+    build(0, 2)
+    iota(view("cst"), [[16, 16], [0, 8]], 1)
+
+    def consts():
+        lin(PI1, PI_, 1.0, 1.0)
+        lin(A15, A_, -1.0, 15.0)
+        for t in range(3):
+            ts(ix(8 + t), A_, float(t), OP.not_equal)
+            ts(ix(12 + t), A_, float(t), OP.is_equal)
+        ts(ix(11), A_, 3.0, OP.is_ge)
+        const(view("z8"))
+        const(view("zb"))
+        ts(view("zb", 120, 128), view("pg", 0, 8), G_, OP.is_equal)
+        ts(view("blki"), view("pg"), G_, OP.is_equal)
+        ts(view("blkpp"), view("pg"), PG_, OP.is_equal)
+        ts(view("blkp"), view("qg"), PG_, OP.is_equal)
+        ts(view("cst"), view("cst"), A_, OP.add)
+        tt(view("cst"), view("cst"), view("blki"), OP.mult)
+        ts(view("cst"), view("cst"), -1.0, OP.add)
+        ts(view("tmp", 0, 128), view("qm"), PI1, OP.is_equal)
+        tt(view("pmx"), view("tmp", 0, 128), view("blkp"), OP.mult)
+        ts(view("tmp", 128, 256), view("qm"), PI1, OP.is_gt, -1.0, OP.add)
+        tt(view("tmb"), view("tmp", 128, 256), view("blkp"), OP.mult)
+        lin(view("npm"), view("c8"), 1.0, PI_)
+        lin(view("cnp"), view("npm"), 1.0, -511.0)
+        lin(view("sm", 4, 5), A_, -1.0, 639.0)
+        lin(view("nlneg"), view("c8"), -1.0, view("sm", 4, 5))
+        tt(view("c15"), view("eqm", 0, 16), view("c16", 16, 32), OP.mult)
+        const(view("b16"), 16)
+        scale(view("d15"), view("i128"), A15)
+        lin(view("low"), view("blk"), 256.0, -256.0)
+        tt(view("low"), view("low"), view("d15"), OP.add)
+        for t in range(3):
+            scale(view("keep", 128 * t, 128 * t + 128), view("i128"), ix(8 + t))
+        lin(view("nj"), jj(2), -2.0)
+        move(view("num", 0, 128), view("io640", 0, 128))
+
+    xw, ow = view("xw"), view("ow")
+    rot = {"g3": 0, "g4": 0}
+
+    def buf(kind):
+        k = 1024 * (rot[kind] % 8)
+        rot[kind] += 1
+        return view(kind, k, k + 1024)
+
+    def pl(t):
+        return view("pl", 8 * t, 8 * t + 8)
+
+    def lookup(t):
+        if t == 0:
+            ts(view("ki"), view("qsf", 0, 8), 128.0, OP.mult, -EPS, OP.add)
+        else:
+            ts(view("ki"), view("qsf", 8 * t, 8 * t + 8), view("pd0", 8, 9), OP.mult, -EPS, OP.add)
+        cp(view("kl"), view("ki"))
+        if t:
+            scatter(view("xk"), pl(t - 1), view("xi"))
+        tt(view("qgt"), view("xk") if t else view("xk", 0, 128), view("lm", 128 * t, 128 * t + 128), OP.mult, idx=view("kl"))
+        mms(view("pa0", 0, 8), [(jj(i), view("qgt", i, 128, 16)) for i in range(16)])
+        ts(view("ql"), view("pa0", 0, 8), 2048.0, OP.add)
+
+    def pass1(b):
+        lst_ = view("bkl") if b == 0 else view("ql")
+        ts(view("xl%d" % (b % 2)), xw, 0.0625, OP.mult, -C23, OP.add, idx=lst_)
+        step(view("xk", 0, 128) if b == 0 else view("xi"), lst_)
+
+    def pass2(b):
+        for h in (0, 1):
+            step(view("y%d" % b, 1024 * h, 1024 * h + 1024), view("xl%d" % (b % 2), 64 * h, 64 * h + 64))
+
+    def psel_x(b, out):
+        for h in (0, 1):
+            bank = view("pa%d" % h, 0, 64)
+            mms(bank, [(sel(0, 0, a), view("y%d" % b, 1024 * h + a, 1024 * h + 1024, 16)) for a in range(16)])
+            ts(view(out, 64 * h, 64 * h + 64), bank, 2048.0, OP.add)
+
+    def psel_z(b, z, n=1):
+        for k in range(n):
+            mms(view("pe0", 128 * k, 128 * k + 128), [(sel(0, 1 + z, a), view("y%d" % (b + k), a, 2048, 16)) for a in range(16)], 1, PARTS)
+        move(view("pz%d" % z, 128 * b, 128 * b + 128 * n), view("pe0", 0, 128 * n))
+
+    def p3(s, src, out, slow=0):
+        for h in (0, 1):
+            bank = view(("pa%d" % h, "pb%d" % h, "pe0")[slow], 64 * h, 64 * h + 64)
+            g3 = buf("g3")
+            w = 32 if slow == 2 else 64
+            for a in range(0, 64, w):
+                step(view("g3", g3[2] + 16 * a, g3[2] + 16 * (a + w)), view(src, 64 * h + a, 64 * h + a + w))
+            mms(bank, [(sel(1, s, e), view("g3", g3[2] + e, g3[3], 16)) for e in range(16)])
+            ts(view(out, 64 * h, 64 * h + 64), bank, 2048.0, OP.add)
+
+    def p4g(h, src):
+        g4 = buf("g4")
+        move(g4, ow, idx=view(src, 64 * h, 64 * h + 64))
+        return g4
+
+    def p4s(h, g4, extra=(), skip=-1, s=0):
+        bank = view("pb%d" % h, 0, 64)
+        mms(bank, [(sel(2, s, e), view("g4", g4[2] + e, g4[3], 16)) for e in range(16) if e != skip] + list(extra))
+        return bank
+
+    def p4z(s, src, w=64):
+        for a in range(0, 128, w):
+            move(view("gt", 16 * a, 16 * (a + w)), ow, idx=view(src, a, a + w))
+        bank, m = view("pb%d" % (s % 2), 0, 128), 128 * (s - 2)
+
+        def fn(e):
+            for k in range(16):
+                r = e.matmul(T[bank[1]][:, k:128:16], T.gt[:, k:2048:16], T.st[:, m + 8 * k:m + 8 * k + 8], True, True)
+            return r
+        do({"P": (fn, (0, 0, 0, 16 * 64))}, [view("gt"), view("st", m, m + 128)], [bank])
+        return bank
+
+    def evac_r(b, h, bank):
+        move(view("rr", 128 * b + 64 * h, 128 * b + 64 * h + 64), bank)
+
+    def compare(t):
+        b, L = t + 1, 128 * (t + 1)
+        q = view("rr", 128 * b, 128 * b + 128)
+        act(view("r2", 0, L), view("rr", 0, L), scale=32.0, func=AF.Square)
+        act(view("rq2"), q, scale=32.0, func=AF.Square)
+        for k in range(8):
+            scale(view("lhb", k, 1024, 8), q, view("b8f", 8 + k, 9 + k), free=True)
+        for c in range(8):
+            bank = view(("pc0", "pc1", "pa1")[c % 3], 0, L)
+            mms(bank, [(view("blki"), view("r2", 0, L)), (view("lhb", 128 * c, 128 * c + 128), view("rr", 0, L))])
+            scan(view("sc", 384 * c, 384 * c + L), bank, view("neg1", 0, L), 8000000.0, OP.min, OP.add)
+        mms(view("pd0", 0, 8), [(view("zb", 120 - 8 * i, 248 - 8 * i), view("rq2", i, 128, 16)) for i in range(16)])
+        act(view("nn"), view("pd0", 0, 8), scale=-1.0)
+
+    def append(t):
+        L, b = 128 * (t + 1), t + 1
+        last = (T.sc[:, L - 1::384], "sc", 0, 3072, 8)
+        tt(view("uu"), last, view("nn"), OP.is_ge)
+        scan(view("inc"), view("uu"), view("z8"), 0.0, OP.add, OP.add)
+        tt(view("vl"), last, view("nn"), OP.subtract)
+        tt(view("ww"), view("uu"), view("cnp"), OP.mult)
+        mms(view("pd0", 8, 9), [(view("i128"), view("cnt", t, t + 1)), (view("blkp"), view("inc", 7, 8))])
+        mms(view("pd0", 0, 8), [(view("blkp"), view("inc")), (view("tmb"), view("uu")), (view("i128"), view("nlneg")), (view("pmx"), view("ww"))])
+        if t < 2:
+            mms(view("pd0", 9, 10), [(view("blkpp"), view("inc", 7, 8))])
+        tt(view("mn"), view("vl"), view("npm"), OP.min)
+        mms(view("pc0", 0, 8), [(view("pmx"), view("mn"))])
+        cp(pl(t), view("pd0", 0, 8))
+        if t < 2:
+            lookup(t + 1)
+            move(view("cnt", t + 1, t + 2), view("pd0", 8, 9))
+            ts(view("cnp"), view("cnp"), view("pd0", 9, 10), OP.add)
+        ts(view("ml"), view("pc0", 0, 8), float(L), OP.add)
+        nb = view("num", 128 * b, 128 * b + 128)
+        move(nb, view("io640"), idx=pl(t))
+        move(view("ymt", 128 * t, 128 * t + 128), view("num", 0, 128 * b + 128), idx=view("ml"))
+        if t:
+            ts(view("lm3"), view("pz%d" % t, 0, L + 128), 2048.0, OP.add, idx=view("ml"))
+        else:
+            tt(view("ne"), view("an"), view("aq"), OP.not_equal, idx=view("ml"))
+        if t < 2:
+            q = view("rr", 128 * b, 128 * b + 128)
+            ts(view("inv"), nb, 512.0, OP.is_ge, 16.0, OP.mult)
+            tt(q, q, view("inv"), OP.max)
+        else:
+            ts(view("invn"), view("io640", 0, 512), view("pd0", 8, 9), OP.is_ge)
+            move(view("pzn", 0, 128), view("pz2", 0, 128))
+            move(view("rn", 0, 128), view("rr", 0, 128))
+            for k in range(3):
+                scatter(view("pzn"), pl(k), view("pz2", 128 * k + 128, 128 * k + 256))
+                scatter(view("rn"), pl(k), view("rr", 128 * k + 128, 128 * k + 256))
+
+    def winner(t):
+        mx = view("sm", 1, 2)
+        if t:
+            sc = view("pd0", 48, 49)
+            mms(view("pd0", 64, 192), [(view("blk"), view("low")), (view("b16"), view("ne"))])
+            mms(sc, [(view("d15"), view("jb", 0, 1)), (view("ne"), view("b16", 0, 1))])
+            reduce(mx, view("pd0", 64, 192), OP.max)
+        else:
+            dc, sc = view("sm", 0, 1), view("sm", 2, 3)
+            reduce(dc, view("ne"), OP.add)
+            ts(view("dd2"), view("eqm", 0, 16), dc, OP.mult, 16.0, OP.mult)
+            mms(view("pd0", 16, 32), [(view("blk"), view("dd2")), (view("blk"), view("c15"))])
+            ts(sc, dc, 16.0, OP.mult, A15, OP.add)
+            reduce(mx, view("pd0", 16, 32), OP.max)
+        oh = view("oh", t, t + 1)
+        ts(oh, sc, mx, OP.is_equal)
+        scale(view("ws"), view("wdf", 4 * t + 4, 4 * t + 8), oh)
+        mms(view("pd0", 32, 36), [(view("blk"), view("ws"))])
+        ts(view("mk", 2 * t, 2 * t + 2), view("pd0", 34, 36), A_, OP.is_equal)
+        lin(view("mk", 8 + t, 9 + t), view("mk", 2 * t, 2 * t + 1), 0.0625)
+        lin(view("mk", 12 + t, 13 + t), view("mk", 2 * t, 2 * t + 1), -C23 - 2048.0)
+        if t == 0:
+            ts(view("mk", 15, 16), view("pd0", 32, 33), 16.0, OP.mult, view("pd0", 33, 34), OP.add)
+        scale(view("ya", 4 * t, 4 * t + 4), view("pd0", 32, 36), ix(12 + t))
+
+    def wpass(t, c0, c1, src):
+        n = (c1 - c0) // 16
+        h = (c1 - c0) // (2 if n > 16 else 1)
+        for a in range(c0, c1, h):
+            scale(view("pw", a, a + h), view(src, a, a + h), view("oh", t, t + 1))
+        bank, bank2 = view("pc0", 0, n), view("pc1", 0, n)
+        mms(bank, [(jj(i), view("pw", c0 + i, c1, 16)) for i in range(16)])
+        lw, lw2 = view("lw", 0, n), view("lw2", 0, n)
+        ts(lw, bank, 2048.0, OP.add)
+        m16, mb = view("mk", 8 + t, 9 + t), view("mk", 12 + t, 13 + t)
+        for a in range(0, c1 - c0, h):
+            o, li = view("gw", a, a + h), view("lw", a // 16, (a + h) // 16)
+            do({"S": a_act(o, xw, m16, mb, idx=li), "V": a_ts(o, xw, -C27 - 32768.0, OP.add, m16, OP.mult, idx=li)}, [xw, m16, mb, li], [o])
+        mms(bank2, [(jj(i), view("gw", i, c1 - c0, 16)) for i in range(16)])
+        ts(lw2, bank2, 2048.0, OP.add)
+        for a in range(0, c1 - c0, h):
+            scale(view("gz%d" % t, c0 + a, c0 + a + h), ow, view("mk", 2 * t + 1, 2 * t + 2), idx=view("lw2", a // 16, (a + h) // 16))
+
+    def rupdate(t):
+        L = 128 * (t + 2)
+        bank = view("pc0", 0, L)
+        mms(bank, [(view("keep", 128 * t, 128 * t + 128), view("rr", 0, L)), (jj(t), view("gz%d" % t, 0, L))])
+        move(view("rr", 0, L), bank)
+
+    pass1(0)
+    lookup(0)
+    pass1(1)
+    pass2(0)
+    psel_x(0, "l30")
+    pass2(1)
+    psel_x(1, "l31")
+    p3(0, "l30", "l40")
+    p3(0, "l31", "l41")
+    build0(1, 384)
+    for b in (0, 1):
+        for h in (0, 1):
+            evac_r(b, h, p4s(h, p4g(h, "l4%d" % b)))
+    consts()
+    build(2, BLOCKS)
+    buildS()
+    for z in range(3):
+        psel_z(0, z, 2)
+    compare(0)
+    for b, x in ((1, 2), (0, 3)):
+        ts(view("l3%d" % x), view("pz0", 128 * b, 128 * b + 128), 2048.0, OP.add)
+        p3(1, "l3%d" % x, "l4%d" % (x if x == 2 else 4), 1)
+        for h in (0, 1):
+            c = 128 * b + 64 * h
+            move(view("an", c, c + 64), p4s(h, p4g(h, "l4%d" % (x if x == 2 else 4)), s=1))
+    move(view("aq"), view("an", 128, 256))
+    for t in range(3):
+        b = t + 2
+        append(t)
+        if t:
+            p3(1 + t, "lm3", "l43")
+        if t < 2:
+            pass1(b)
+            pass2(b)
+            psel_x(b, "l31")
+        if t:
+            tt(view("ne"), p4z(1 + t, "l43"), view("aq"), OP.not_equal)
+        winner(t)
+        if t < 2:
+            for z in range(t, 2):
+                psel_z(b, z)
+            p3(0, "l31", "l41")
+        if t == 0:
+            scale(view("gz0", 0, 256), view("an"), view("oh", 0, 1))
+            wpass(0, 256, 384, "pz0")
+        else:
+            wpass(t, 0, 512, "pzn" if t == 2 else "pz1")
+        if t == 2:
+            break
+        gs = [p4g(h, "l41") for h in (0, 1)]
+        rupdate(t)
+        for h in (0, 1):
+            c = 128 * b + 64 * h
+            evac_r(b, h, p4s(h, gs[h], [(jj(t), view("gz%d" % t, c, c + 64))], t))
+        if t == 0:
+            ts(view("sel", 0, 2048, 16), view("cst"), view("mk", 15, 16), OP.is_equal)
+            for k in (1, 2):
+                ts(view("sel", block(k, 0), block(k, 0) + 128, 16), view("b8f", 0, 8), view("mk", k - 1, k), OP.mult)
+        psel_z(b, 2)
+        compare(t + 1)
+        ts(view("l32"), view("pz%d" % (t + 1), 128 * b, 128 * b + 128), 2048.0, OP.add)
+        p3(2 + t, "l32", "l42", 2)
+        move(view("aq"), p4z(2 + t, "l42", 32))
+
+    ends = []
+
+    def out(dst_ap, src_ap, v, sem):
+        do({"Y": (lambda e: e.dma_start(dst_ap, src_ap).then_inc(T.sem[sem], 16), (0.1, 0, 0, 0))}, [v], [], lat=2.0, tok=())
+        ends.append(sem)
+    out(T.ym[:], T.ymt[::16, :], view("ymt"), "dym")
+    yet = view("ya", 12, 16)
+    scale(yet, view("wdf", 0, 4), ix(11))
+    for t in range(3):
+        tt(yet, yet, view("ya", 4 * t, 4 * t + 4), OP.add)
+    out(T.ye[:], T.ya[:, 12:16], yet, "dye")
+    mms(view("pc0"), [(view("keep", 256, 384), view("rn", 0, 512)), (view("nj"), view("invn")), (jj(2), view("gz2"))])
+    ts(view("yrt"), view("pc0"), -1.0, OP.max)
+    out(T.yr[:], T.yrt[:], view("yrt"), "dyr")
+
+    PLAN["ops"], PLAN["p"] = ops, plan(ops)
+    pos = {q: 0 for q in queue}
+    seen = {q: {} for q in queue}
+    for i, q in PLAN["p"]:
+        ops[i]["run"] = q
+    for i, q in PLAN["p"]:
+        o = ops[i]
+        if q == "D":
+            continue
+        want = {}
+        for d in o["deps"] | set(d for d in o["soft"] if ops[d]["run"] != q):
+            if ops[d]["tok"]:
+                s, n = ops[d]["tok"]
+                want[s] = max(want.get(s, 0), n)
+        for s in sorted(want):
+            if seen[q].get(s, 0) < want[s]:
+                queue[q].wait_ge(T.sem[s], want[s])
+                seen[q][s] = want[s]
+        r = o["alt"][q][0](queue[q])
+        if o["tok"] is None:
+            pos[q] += 1
+            r.then_inc(T.sem[CSEM[q]], 1)
+            o["tok"] = (CSEM[q], pos[q])
+    for s in ends:
+        g.sync.wait_ge(T.sem[s], 16)
+    g.wait_ge(T.sem.sent, (NCH + len(OWS)) * neng)
+    for q in sorted(CSEM):
+        g.wait_ge(T.sem[CSEM[q]], pos[q])

@@ -2,206 +2,201 @@ from concourse.mybir import AluOpType, AxisListType, ActivationFunctionType
 
 OP = AluOpType
 AF = ActivationFunctionType
-CWS = [256, 1024, 1024, 1024, 512, 256]
+CWS = [512] * 7 + [384, 128]
 NCH = len(CWS)
-OWS = [2048, 2048]
 C27 = 201326592.0
 C23 = 12582912.0
 EPS = 0.499969482421875
 PARTS = 4
+WSET, WCMP = 2064, 272
+NBUF = 14
+WIDE, FINE = 64, 32
 DIGITS = "0123456789abcdefghijklmnopqrstuvwxyzABCDEFGHIJKLMNOPQRSTUVWXYZ"
-ORDER = (
-    "1W2400083l040c020g0w060k0a0o0s203j0e3f3h2i2g2c2e2k4c7x0A3d2m"
-    "0i0E8h1Y2o7N2q2a4G8C2y2230342W322u2A0I2Y28262U2S360K0m2s2C2K"
-    "3r2I2M8j382H4p3N8d8f4i2E2O2Q7v0O8r4k1i4q4m4e2w584Q0q4K0u0U4O"
-    "4M0y0C1m0G0Q0M1u0W0S4S1k10121o4I1c161y1q0Y184U564y4w4A141e1s"
-    "1A5A1w1O1C1G3u3m1a4Y4C1K1g1I4u4W5C541E3p5y526A5c3E1Q5w3P5E4s"
-    "4g5G5a3a1M1S3t5I5O506E5K6G5Q3H603z6C3w5o5e5m5S3K1U639a5g5k5q"
-    "5s5i5W5Y423Q3S5U646c683C466S6j666I6M6a6Q3J6e6o6O6K6k709c6u6U"
-    "6W9e6g6Y6q74726m7c9g776s8Y3U9i9k6w3X786y7j407a7o7e7g9m7O9o7k"
-    "7ma23A3Z9r7S458O8K7WaW7qbm8F888H7t9saYa8aa8S8R7Q9uaha7alajaf"
-    "9wad9yb59A488m9C4a8M8I9094968W8Uamaqaub0aoas84ayawaCb2b6aAaE"
-    "aO86b88abh8Ba4baaGaIaK9E9GaSaQ9I92aUbcbiaMbObSbQbU7UbWbY5Nc0"
-    "9Kc6c89M4Ecc9Ocabobubec29Qcec4cobl7ycg8kcr9S9UbqcicA5u7YcFcC"
-    "cGbw9W9Ybsbya0bBbG8ucIdgcMdidkcKcOdB8obM98kybIbCckbKdGdmbFdC"
-    "dpcucmcQdqdEcScWcwdscUcYd07Adud3dPdwe2dzcydNdId4d6dcd9dbfsdQ"
-    "eodKdSdee4eqesdVfxdWeudY7Ce6e1ekewfueae9808xeeed8sey82fyehei"
-    "eEeReOeDeHeLeJeNeAfActfEeSfKemeW7EeUf0eYfCf4f2f8f6fcfofqfafe"
-    "kCfkfgfmfGfifM7GfWg0fYg2fIfQg4gag68zfOg87KgcgegggwgygkgigCgm"
-    "gogJgOfSgqfUlPgUlQgZh0gQgSgKgM7IhchbhCh6gsh2h4gEguhehMgGhEhg"
-    "h8gXhihkhGhmhIhohThqhKhOhshYi0gAi2huhzhxhQhUiyi4hAi6i9hWiilS"
-    "iAiailiCiEicifigkGimiGiuipjCiqiIixkBitiPiNiXiZiTj1iQiUjEiKkE"
-    "j6j2jMj8jaj4jijcjGjejkjmjgjojujwjqjsjyjIjAkakik6jKkkkojOjQk8"
-    "kukckPkUkekgjSjUjXkQkWjYk1kSkYk2kmkIkql0l3k5kskwl4lMl6kKl8la"
-    "lclelhltlulilwlklolqlylUlWlnlBlCkMlElGlJlKlYm0m2")
-SETS = [(1, 0), (2, 0), (1, 1), (2, 1), (1, 2), (1, 3), (2, 2), (2, 3)]
-BLOCKS, PAIR, WSET = 6, 8192, 2064
+ORDER = "1Q2C036d7s5D2500091N0f37302F0l0r3Q222k6f1W6i341T2P2U0x0D061Z7h2Y2h2e5X71637b0J3A2J7m5U0P0V392r602n0c113N2M0i6V2z140o2t171a0u3J7k1d1g2S2w78411j3Y4E4g446D0A280G6l3D3G474a4d7H4w5n4y5R0M7q5k1p1v4j1B0Y0S7y7K5O1H7v7B4B4p3x4s7N7Q4m1s1m4H5F7T6Y553r7W3l3u7F883i8b4K3c1y828e8l586r858U8X7Z8h8t663V1K90934Q9f8n748w978q3S9i991E3f8z4U8F6G4W8D9l9c9o5b8I9G9J9M6o4N6M9s9P4Z3o9Sdm5q529V9Y6udta1a45e6Ja89u9A8L6S9ycx5M8O6P5hdpdv6xdB9DcAcEbrbD5I8RbxcNcGbJcJbobbbGbebzb8cQbhbtcldycf5zbRbLc9bkcrc369bUcobXc6cic0ccbOcu5wcScVeedEdHdKd1encYda5tekeqd8etd4eweCeFeLdNdQaaeIdgeOdXeReUehfYaddTg4agezf36A2bape5dkg8e9ddeceYajdZe2fff6gaf9gdgmfiflgggjfrfcgKfofufxgNgQgTgWgwgZgp7dfAfDfGhwhzhCf0htfJg1gygsamfNgBhFhRgEashUhIfPgIhLh2h5h8avayhchOaBjBjIfVjEici3i7hXi1iyifiEivaEisiNiHiKiBjQfSjKjTjNiiilioiPiSj1j4iViYk2jpjsjdjgjvjyj7jajjhejmkkk5jWknjZaHkqktkbkFl9lllrkwkzkCkIhhkLlAaTk8lplEaWkRlukOlGaKlxlPkUlJlSkXlNl0mvmyaZb2kekhhklWaNaQmClYm1i9spmEb6lcmHnem4ssm7mal3l6mdmKmNmhnhnknnnJmjntmQmTn0mmnqnLnOnRlfmWmplimtn2nXnUhnn5nbn9nwnzo0o3o9nCnGo7pTpZhrpXsvocoiooomosofsCp5q2p2ouoWq5oZoToKsEoxoAoMoDoPppsHpsqbpNpQpvpypjpmq8qnp7papdpgoHqkqeqhpHpKpBpEqFqUr6qqqCqtqwrfrlqIrjrvrorrrxrJrAqLqOqRrHrDqXrPrNqzrSsKr9rcrVrYsys1s4s7sbsRthsdsgsmtzsNsjsTsWsZt3t5t8tktftbtnr0r3tqtttwtFtC"
 
 F, B, H, I, U = "float32", "bfloat16", "float16", "int32", "uint16"
 SCRATCH = {}
 for _n, _w, _d in [
-        ("mti", 4096, I), ("wt", 4096, F), ("ob", 4096, B), ("xw", 4096, F), ("ow", 4096, B),
-        ("wd", 16, I), ("bki", 8, I), ("qsi", 24, I), ("qci", 24, I), ("pi", 8, I), ("ix", 24, F),
-        ("qg", 128, F), ("qm", 128, F), ("pg", 128, F), ("c16", 32, F), ("io640", 640, F), ("c8", 8, F),
-        ("blk", 128, B), ("eqm", 128, B), ("i128", 128, B), ("jb", 16, B), ("jj", 2048, B), ("nj", 128, B),
-        ("blkp", 128, B), ("tmp", 256, B), ("tmb", 128, B), ("pmx", 128, B), ("blkpp", 128, B), ("blki", 128, B), ("cst", 128, B),
-        ("b16", 128, B), ("d15", 128, B), ("low", 128, B), ("zb", 248, B), ("b8f", 16, F), ("keep", 384, B), ("cole", 16, F),
-        ("nlneg", 8, H), ("npm", 8, F), ("cnp", 8, F), ("neg1", 384, F), ("z8", 8, F), ("c15", 16, B),
-        ("wdf", 24, F), ("dd", 512, B), ("wrb", 512, B), ("dm", 128, B), ("msk", 128, B),
-        ("sel", PAIR + BLOCKS * WSET, B), ("st", 256, B), ("qcl", 24, U), ("lrow", 384, F), ("lm", 384, B), ("qsf", 24, F), ("bkl", 8, U),
-        ("ki", 8, I), ("kl", 8, U), ("qgt", 128, H), ("ql", 8, U), ("xi", 128, F), ("xl0", 128, U), ("xl1", 128, U), ("xk", 640, F),
-        ("y0", 2048, H), ("y1", 2048, H), ("y2", 2048, H), ("y3", 2048, H), ("g3", 8192, H), ("g4", 8192, B), ("gt", 2048, B),
-        ("l30", 128, U), ("l31", 128, U), ("l32", 128, U), ("l33", 128, U), ("lm3", 128, U),
-        ("l40", 128, U), ("l41", 128, U), ("l42", 128, U), ("l43", 128, U), ("l44", 128, U),
-        ("pz0", 512, F), ("pz1", 512, F), ("pz2", 512, F), ("pzn", 640, F), ("rr", 512, B), ("rn", 640, B), ("invn", 512, B), ("an", 256, B),
+        ("mti", 4096, I), ("xw", 4096, F), ("ow", 4096, B), ("inp", 72, I), ("inl", 72, I), ("inu", 48, U),
+        ("res", 1024, F), ("resl", 896, F), ("fin", 36, F), ("finl", 36, F), ("cap", 36, F),
+        ("pi", 8, I), ("ix", 24, F), ("qg", 128, B), ("pg", 128, B), ("io640", 640, F), ("c24", 24, F), ("cc", WCMP, F), ("ee", WCMP, B),
+        ("one", 128, B), ("blk", 128, B), ("eye", 16, B), ("i128", 128, B), ("zj", 144, B), ("blkp", 128, B), ("tlo", 128, B),
+        ("pmx", 128, B), ("blkpp", 128, B), ("blki", 128, B), ("b16", 128, B), ("d15", 128, B), ("low", 128, B), ("zb", 248, B),
+        ("b8f", 8, F), ("keep", 384, B), ("nlneg", 8, H), ("own", 24, F), ("cnp", 8, F), ("neg1", 384, F), ("z8", 8, F), ("c15", 16, B),
+        ("k32", 32, F), ("w16", 640, B), ("wdb", 16, B), ("code", 8, F), ("cb", 512, H), ("cmp", 12 * WCMP, B),
+        ("lm", 384, B), ("qsf", 24, F), ("ki", 8, I), ("kl", 8, U), ("qgt", 128, H), ("ql", 8, U), ("xi", 256, F),
+        ("xl", 512, U), ("xk", 640, F), ("yy", 8192, H), ("gb", 2048 * NBUF, H), ("ls", 128 * 20, U),
+        ("pz0", 384, F), ("pz1", 512, F), ("pz2", 512, F), ("pzn", 640, F), ("rr", 512, B), ("an", 256, B),
         ("r2", 384, B), ("rq2", 128, B), ("lhb", 1024, B),
-        ("sc", 3072, F), ("nn", 8, F), ("vl", 8, F), ("uu", 8, H), ("inc", 8, H), ("ww", 8, H), ("mn", 8, H), ("ml", 8, U), ("cnt", 4, H),
-        ("pl", 24, U), ("num", 512, F), ("ymt", 384, F), ("inv", 128, B),
-        ("aq", 128, B), ("ne", 128, B), ("sm", 8, F), ("dd2", 16, B), ("oh", 4, F), ("ws", 4, B),
-        ("mk", 16, F), ("ya", 16, F), ("pw", 512, H), ("lw", 32, U), ("gw", 512, H), ("lw2", 32, U),
-        ("gz0", 512, B), ("gz1", 512, B), ("gz2", 512, B), ("yrt", 512, F)]:
+        ("sc", 3072, F), ("nn", 8, F), ("top", 8, F), ("uu", 8, H), ("inc", 10, H), ("ww", 8, H), ("mn", 8, H), ("ml", 8, U),
+        ("cnt", 4, H), ("pl", 24, U), ("num", 512, F), ("aq", 128, B), ("ne", 128, B), ("sm", 8, F), ("dd2", 16, B),
+        ("oh", 4, F), ("ws", 12, B), ("mk", 16, F), ("pw", 512, H), ("lw", 32, U), ("gw", 512, H), ("lw2", 32, U),
+        ("gz0", 384, B), ("gz1", 512, B), ("gz2", 512, B)]:
     SCRATCH[_n] = ("sbuf", [128, _w], _d)
-PSUM = ["pa0", "pa1", "pb0", "pb1", "pc0", "pc1", "pd0", "pe0"]
-for _n in PSUM:
+SCRATCH["sel"] = ("sbuf", [128, 12, WSET], B)
+BANKS = ["bank%d" % _k for _k in range(8)]
+for _n in BANKS:
     SCRATCH[_n] = ("psum", [128, 512], F)
-SEMAPHORES = (["cv", "cs", "cp", "cg", "sent", "dex", "dzs", "dbk", "dqs", "dqc", "dym", "dyr", "dye"] + ["dmt%d" % h for h in range(NCH)]
-              + ["arr%d" % h for h in range(NCH + len(OWS))])
+SEMAPHORES = (["cv", "cs", "cp", "cg", "sent", "din", "din2", "ain", "ares", "afin", "dym", "dyr", "dy2", "dye"]
+              + ["dmt%d" % h for h in range(NCH)] + ["wave%d" % h for h in range(4)] + ["dz%d" % h for h in range(3, 9)])
 CSEM = {"V": "cv", "S": "cs", "P": "cp", "G": "cg"}
 PLAN = {}
 
 
 def plan(ops):
-    out = []
-    for k in range(0, len(ORDER), 2):
-        c = 62 * DIGITS.index(ORDER[k]) + DIGITS.index(ORDER[k + 1])
-        out.append((c // 2, list(ops[c // 2]["alt"])[c % 2]))
-    return out
+    code = [62 * DIGITS.index(ORDER[k]) + DIGITS.index(ORDER[k + 1]) for k in range(0, len(ORDER), 2)]
+    if len(code) != len(ops):
+        code = [3 * i for i in range(len(ops))]
+    order = [(x // 3, list(ops[x // 3]["alt"])[x % 3]) for x in code]
+    users, bank_of, extra = {}, {}, {}
+    for i, o in enumerate(ops):
+        users.setdefault(o["ps"], []).append(i)
+    togo, held, through = [0] * 8, [None] * 8, [0] * 8
+    for n, (i, q) in enumerate(order):
+        v = ops[i]["ps"]
+        if v is not None:
+            if v not in bank_of:
+                k = min([k for k in range(8) if not togo[k]], key=lambda k: through[k])
+                extra[i] = users[held[k]] if held[k] else []
+                held[k], bank_of[v], togo[k] = v, k, len(users[v])
+            togo[bank_of[v]] -= 1
+            through[bank_of[v]] = n
+    return order, bank_of, extra
 
 
 def rank_program(g, core, T, topo):
     rank = T.rank_of(core)
     if rank is None:
         return
-    queue = {"V": g.vector, "S": g.scalar, "P": g.tensor, "G": g, "Y": g.sync, "D": None}
+    queue = {"V": g.vector, "S": g.scalar, "P": g.tensor, "G": g, "Y": g.sync}
     ops = []
     wrote, readers = {}, {}
+    nps = [0]
 
     def view(name, c0=0, c1=None, st=1):
         if c1 is None:
             c1 = SCRATCH[name][1][1]
-        ap = T[name][:, c0:c1] if st == 1 else T[name][:, c0:c1:st]
-        return (ap, name, c0, c1, (c1 - c0 + st - 1) // st)
+        return (name, c0, c1, st, (c1 - c0 + st - 1) // st)
 
-    def do(alt, reads, writes, free=False, tok=None, lat=0.0, dep=()):
+    def psum():
+        nps[0] += 1
+        return "#%d" % nps[0]
+
+    def inps(v):
+        return v[0][0] == "#"
+
+    def ap(v):
+        if v[0] == "sel":
+            k = v[1] // WSET
+            return T.sel[:, k, v[1] - k * WSET:v[2] - k * WSET:v[3]]
+        t = T[BANKS[PLAN["p"][1][v[0]]]] if inps(v) else T[v[0]]
+        return t[:, v[1]:v[2]] if v[3] == 1 else t[:, v[1]:v[2]:v[3]]
+
+    def do(alt, reads, writes, free=False, after=()):
         i = len(ops)
-        deps, soft = set(dep), set()
+        deps, soft = set(), set(after)
         for v in reads:
-            ps = v[1] in PSUM
-            for (a, b, j) in wrote.get(v[1], []):
-                if a < v[3] and v[2] < b:
+            for (a, b, j) in wrote.get(v[0], []):
+                if a < v[2] and v[1] < b:
                     deps.add(j)
-                elif ps:
+                elif inps(v):
                     soft.add(j)
-            if ps:
-                soft.update(j for (a, b, j) in readers.get(v[1], []))
+            if inps(v):
+                soft.update(j for (a, b, j) in readers.get(v[0], []))
         for v in writes:
-            ps = v[1] in PSUM
-            for (a, b, j) in wrote.get(v[1], []):
-                if ps:
+            for (a, b, j) in wrote.get(v[0], []):
+                if inps(v):
                     soft.add(j)
-                elif a < v[3] and v[2] < b and not (free and ops[j]["free"]):
+                elif a < v[2] and v[1] < b and not (free and ops[j]["free"]):
                     deps.add(j)
-            for (a, b, j) in readers.get(v[1], []):
-                if a < v[3] and v[2] < b:
+            for (a, b, j) in readers.get(v[0], []):
+                if a < v[2] and v[1] < b:
                     deps.add(j)
-                elif ps:
+                elif inps(v):
                     soft.add(j)
-        ops.append({"alt": alt, "lat": lat, "deps": deps, "soft": soft - deps, "tok": tok, "free": free, "run": None,
-                    "nm": writes[0][1] if writes else "-"})
+        ps = [v[0] for v in list(reads) + list(writes) if inps(v)]
+        ops.append({"alt": alt, "deps": deps, "soft": soft - deps, "free": free, "ps": ps[0] if ps else None,
+                    "nm": writes[0][0] if writes else "-"})
         for v in writes:
             if not free:
                 for d in (wrote, readers):
-                    d[v[1]] = [r for r in d.get(v[1], []) if not (v[2] <= r[0] and r[1] <= v[3])]
-            wrote.setdefault(v[1], []).append((v[2], v[3], i))
+                    d[v[0]] = [r for r in d.get(v[0], []) if not (v[1] <= r[0] and r[1] <= v[2])]
+            wrote.setdefault(v[0], []).append((v[1], v[2], i))
         for v in reads:
-            readers.setdefault(v[1], []).append((v[2], v[3], i))
+            readers.setdefault(v[0], []).append((v[1], v[2], i))
         return i
 
-    chains = {}
-
-    def chain(q, i):
-        if q in chains:
-            ops[i]["soft"].add(chains[q])
-        chains[q] = i
-
-    def flight(i, out, us, tok, lat):
-        j = do({"D": (None, (0, 0, 0, 0, us, 0))}, [], out, tok=tok, lat=lat, dep=[i])
-        chain("D", j)
-
-    def dma(q, out, in_ap, sem, us):
-        i = do({q: (lambda e: e.dma_start(out[0], in_ap).then_inc(T.sem[sem], 16), (0.1, 0, 0, 0))}, [], [], tok=())
-        chain(q, i)
-        flight(i, [out], us, (sem, 16), 2.0)
+    def a_dma(pairs, sem, us):
+        def fn(e):
+            for o, i in pairs:
+                e.dma_start(o, i).then_inc(T.sem[sem], 16)
+        return (fn, (0.08 * len(pairs), 0, 0, 0, 0, us, 1), (sem, 16 * len(pairs)))
 
     def sca(s):
         return [s] if isinstance(s, tuple) else []
 
     def val(s):
-        return s[0] if isinstance(s, tuple) else s
+        return ap(s) if isinstance(s, tuple) else s
 
     def two(*vs):
-        return all(SCRATCH[v[1]][2] in (B, H, U) for v in vs)
+        return all(not inps(v) and SCRATCH[v[0]][2] in (B, H, U) for v in vs)
 
     def dv(n, half=False):
-        return (0.03, max(64, n * (0.5 if half else 1.0)), 0, 0)
+        return (0.03, max(64, n * (0.5 if half else 1.0)), 0, 0, 0, 0, 0)
+
+    def dg(n):
+        return (0.05, 0, n, 0, 0, 0, 0)
 
     def ind(v, idx):
-        return v[0] if idx is None else v[0].indirect(idx[0])
+        return ap(v) if idx is None else ap(v).indirect(ap(idx))
 
     def lst(idx):
         return [] if idx is None else [idx]
 
     def a_ts(out, in0, s1, op0, s2=None, op1=None, idx=None):
-        i0 = ind(in0, idx)
-        w = dv(out[4], two(out, in0)) if idx is None else (0.05, 0, out[4], 0)
+        w = dv(out[4], two(out, in0)) if idx is None else dg(out[4])
         if op1 is None:
-            return (lambda e: e.tensor_scalar(out[0], i0, val(s1), None, op0), w)
-        return (lambda e: e.tensor_scalar(out[0], i0, val(s1), val(s2), op0, op1), w)
+            return (lambda e: e.tensor_scalar(ap(out), ind(in0, idx), val(s1), None, op0), w, None)
+        return (lambda e: e.tensor_scalar(ap(out), ind(in0, idx), val(s1), val(s2), op0, op1), w, None)
 
     def a_act(out, in_, scale=1.0, bias=0.0, func=AF.Identity, idx=None):
-        i0 = ind(in_, idx)
-        return (lambda e: e.activation(out[0], i0, func, bias=val(bias), scale=val(scale)),
-                (0.065, 0, out[4], 0) if idx else (0.065, out[4], 0, 0))
+        return (lambda e: e.activation(ap(out), ind(in_, idx), func, bias=val(bias), scale=val(scale)),
+                (0.065, 0, out[4], 0, 0, 0, 0) if idx else (0.065, out[4], 0, 0, 0, 0, 0), None)
 
     def a_cp(out, in_, idx=None):
-        i0 = ind(in_, idx)
-        return (lambda e: e.tensor_copy(out[0], i0), dv(out[4], two(out, in_)) if idx is None else (0.05, 0, out[4], 0))
+        return (lambda e: e.tensor_copy(ap(out), ind(in_, idx)), dv(out[4], two(out, in_)) if idx is None else dg(out[4]), None)
 
-    def ts(out, in0, s1, op0, s2=None, op1=None, free=False, idx=None):
-        do({"V": a_ts(out, in0, s1, op0, s2, op1, idx)}, [in0] + sca(s1) + sca(s2) + lst(idx), [out], free)
+    def a_iota(out, pattern, base=0, cm=0):
+        if SCRATCH[out[0]][2] == I:
+            fn = lambda e: e.iota(ap(out), pattern, base, cm)
+        else:
+            fn = lambda e: e.iota(ap(out), pattern, base, cm, allow_small_or_imprecise_dtypes=True)
+        return (fn, (0.13, 2 * out[4], 0, 0, 0, 0, 0), None)
+
+    def a_fill(v, c):
+        return (lambda e: e.memset(ap(v), float(c)), dv(v[4], two(v)), None)
+
+    def ts(out, in0, s1, op0, s2=None, op1=None, idx=None):
+        do({"V": a_ts(out, in0, s1, op0, s2, op1, idx)}, [in0] + sca(s1) + sca(s2) + lst(idx), [out])
 
     def tt(out, in0, in1, op, idx=None):
-        i0 = ind(in0, idx)
-        w = (0.05, 0, out[4], 0) if idx else dv(out[4] * (1 if in0[1] in PSUM or in1[1] in PSUM else 2))
-        do({"V": (lambda e: e.tensor_tensor(out[0], i0, in1[0], op), w)}, [in0, in1] + lst(idx), [out])
+        w = dg(out[4]) if idx else dv(out[4] * (1 if inps(in0) or inps(in1) else 2))
+        do({"V": (lambda e: e.tensor_tensor(ap(out), ind(in0, idx), ap(in1), op), w, None)}, [in0, in1] + lst(idx), [out])
 
-    def cp(out, in_, idx=None):
-        do({"V": a_cp(out, in_, idx)}, [in_] + lst(idx), [out])
-
-    def fill(out, c):
-        do({"V": (lambda e: e.memset(out[0], c), dv(out[4], two(out)))}, [], [out])
+    def cp(out, in_):
+        do({"V": a_cp(out, in_)}, [in_], [out])
 
     def scatter(win, idx, in_):
-        do({"V": (lambda e: e.tensor_copy(win[0].indirect(idx[0]), in_[0]), (0.05, 0, 2 * in_[4], 0))}, [in_, idx], [win])
+        do({"V": (lambda e: e.tensor_copy(ap(win).indirect(ap(idx)), ap(in_)), (0.05, 0, 0, in_[4], 0, 0, 0), None)}, [in_, idx], [win])
 
     def scan(out, d0, d1, init, op0, op1):
-        do({"V": (lambda e: e.tensor_tensor_scan(out[0], d0[0], d1[0], init, op0, op1), dv(out[4]))}, [d0, d1], [out])
+        do({"V": (lambda e: e.tensor_tensor_scan(ap(out), ap(d0), ap(d1), val(init), op0, op1), dv(out[4]), None)}, [d0, d1] + sca(init), [out])
 
     def reduce(out, in_, op):
-        do({"V": (lambda e: e.tensor_reduce(out[0], in_[0], AxisListType.X, op), dv(in_[4]))}, [in_], [out])
+        do({"V": (lambda e: e.tensor_reduce(ap(out), ap(in_), AxisListType.X, op), dv(in_[4]), None)}, [in_], [out])
 
-    def act(out, in_, scale=1.0, bias=0.0, func=AF.Identity, idx=None):
-        do({"S": a_act(out, in_, scale, bias, func, idx)}, [in_] + sca(scale) + sca(bias) + lst(idx), [out])
+    def act(out, in_, scale=1.0, bias=0.0, func=AF.Identity):
+        do({"S": a_act(out, in_, scale, bias, func)}, [in_] + sca(scale) + sca(bias), [out])
 
     def move(out, in_, idx=None):
         do({"S": a_act(out, in_, idx=idx), "V": a_cp(out, in_, idx)}, [in_] + lst(idx), [out])
@@ -216,470 +211,419 @@ def rank_program(g, core, T, topo):
         do({"S": a_act(out, xw, 0.0625, -C23 - 2048.0, idx=idx), "V": a_ts(out, xw, 0.0625, OP.mult, -C23 - 2048.0, OP.add, idx=idx)},
            [xw, idx], [out])
 
-    def mms(out, pairs, f=1, parts=1):
+    def mms(out, pairs, parts=1):
         n = len(pairs)
         for m in range(parts):
             lo, hi = n * m // parts, n * (m + 1) // parts
 
             def fn(e, lo=lo, hi=hi):
                 for k in range(lo, hi):
-                    r = e.matmul(out[0], pairs[k][0][0], pairs[k][1][0], k == 0, k == n - 1)
+                    r = e.matmul(ap(out), ap(pairs[k][0]), ap(pairs[k][1]), k == 0, k == n - 1)
                 return r
-            do({"P": (fn, (0, 0, 0, f * (hi - lo) * max(64, out[4])))}, [p for pr in pairs[lo:hi] for p in pr], [out])
+            do({"P": (fn, (0, 0, 0, 0, (hi - lo) * max(64, out[4]), 0, 0), None)}, [p for pr in pairs[lo:hi] for p in pr], [out])
 
     def iota(out, pattern, base=0, cm=0):
-        if out[1] == "pi":
-            fn = lambda e: e.iota(out[0], pattern, base, cm)
-        else:
-            fn = lambda e: e.iota(out[0], pattern, base, cm, allow_small_or_imprecise_dtypes=True)
-        return do({"G": (fn, (0.13, 2 * out[4], 0, 0))}, [], [out])
+        do({"G": a_iota(out, pattern, base, cm)}, [], [out])
+
+    def select(out, in_, pattern, op, fill, base, cm):
+        do({"G": (lambda e: e.affine_select(ap(out), ap(in_), pattern, op, float(fill), base, cm), (0.17, 2 * out[4], 0, 0, 0, 0, 0), None)},
+           [in_], [out])
 
     def const(v, c=0):
-        do({"G": (lambda e: e.iota(v[0], [[0, v[4]]], c, 0, allow_small_or_imprecise_dtypes=True), (0.13, 2 * v[4], 0, 0)),
-            "V": (lambda e: e.memset(v[0], float(c)), dv(v[4], two(v)))}, [], [v])
+        do({"G": a_iota(v, [[0, v[4]]], c), "V": a_fill(v, c)}, [], [v])
 
-    def zeros(name, c):
-        for a in range(c, c + 2048, 512):
-            const(view(name, a, a + 512))
+    nrk = len(T.cores)
+    sent = [0]
 
-    c0 = [sum(CWS[:h]) for h in range(NCH)]
-    dma("S", view("wd", 0, 4), T.ex[:], "dex", 0.1)
-    dma("S", view("wd", 4, 16), T.zs[:], "dzs", 0.1)
+    def send(dst, out, v, sem, us, kind, share=1):
+        rid, pid, _ = topo.addr(dst)
+        eng = topo.engines(core, dst)[::share]
+        sent[0] += len(eng)
+        do({"G": (lambda e: e.remote_dma(ap(out), ap(v), T.sem[sem], T.sem.sent, pid, rid, sum(1 << k for k in eng)),
+                  (0.3, 0, 0, 0, 0, us, kind), (sem, len(eng)))}, [v], [out])
+    owner, learner = T.cores[(rank + 1) % nrk], T.cores[(rank - 1) % nrk]
+
+    do({"S": a_dma([(T.inp[:, 0:4], T.ex[:]), (T.inp[:, 4:16], T.zs[:]), (T.inp[:, 48:72], T.qs[:])], "din", 0.1)},
+       [], [view("inp", 0, 16), view("inp", 48, 72)])
+    last = [do({"Y": a_dma([(T.inp[:, 16:24], T.bk[:]), (T.inp[:, 24:48], T.qc[:])], "din2", 0.1)}, [], [view("inp", 16, 48)])]
+    send(owner, view("inl"), view("inp"), "ain", 0.2, 3, 4)
+    xw, ow = view("xw"), view("ow")
+    a = 0
     for h in range(NCH):
-        dma("Y", view("mti", c0[h], c0[h] + CWS[h]), T.mt[:, c0[h]:c0[h] + CWS[h]], "dmt%d" % h, 5.2 * CWS[h] / 4096)
-    dma("S", view("bki"), T.bk[:], "dbk", 0.1)
-    dma("S", view("qci"), T.qc[:], "dqc", 0.1)
-    dma("S", view("qsi"), T.qs[:], "dqs", 0.1)
-
-    dst = T.cores[(rank - 1) % len(T.cores)]
-    rid, pid, _ = topo.addr(dst)
-    emask = topo.mask(core, dst)
-    neng = len(topo.engines(core, dst))
-
-    def send(out, v, us, h):
-        i = do({"G": (lambda e: e.remote_dma(out[0], v[0], T.sem["arr%d" % h], T.sem.sent, pid, rid, emask),
-                      (0, 0, 0, 0, 1.0, 0 if h else 1))}, [v], [], tok=())
-        chain("G", i)
-        flight(i, [out], us, ("arr%d" % h, neng), 1.0)
-    for h in range(NCH):
-        a, b = c0[h], c0[h] + CWS[h]
-        ts(view("wt", a, b), view("mti", a, b), -7.5, OP.add, C27, OP.add)
-        send(view("xw", a, b), view("wt", a, b), 5.2 * CWS[h] / 4096, h)
-    for k in range(8):
-        a = 512 * k
-        bank = view(("pc0", "pc1", "pb0", "pb1")[k % 4])
-        act(bank, view("wt", a, a + 512), bias=-C27)
-        tt(view("ob", a, a + 512), view("mti", a, a + 512), bank, OP.subtract)
-    for h in range(len(OWS)):
-        a = sum(OWS[:h])
-        send(view("ow", a, a + OWS[h]), view("ob", a, a + OWS[h]), 2.6 * OWS[h] / 4096, NCH + h)
-
-    iota(view("pi", 0, 1), [[0, 1]], 0, 1)
-    iota(view("qg"), [[1, 8], [0, 16]])
-    iota(view("qm"), [[0, 8], [1, 16]], 1)
-    iota(view("c16", 0, 16), [[16, 16]], 1)
-    iota(view("pg"), [[0, 16], [1, 8]])
-    iota(view("c8"), [[16, 8]])
-    iota(view("c16", 16, 32), [[-1, 16]], 15)
-    iota(view("io640"), [[1, 640]])
-    pi = view("pi", 0, 1)
-    ts(view("pi", 4, 5), pi, 15, OP.bitwise_and)
-    ts(view("pi", 5, 6), pi, 4, OP.arith_shift_right)
-    ts(view("pi", 6, 7), pi, 7, OP.bitwise_and)
-    ts(view("pi", 7, 8), pi, 3, OP.arith_shift_right)
-    cp(view("ix", 0, 4), view("pi", 4, 8))
+        b = a + CWS[h]
+        last = [do({"Y": a_dma([(T.mti[:, a:b], T.mt[:, a:b])], "dmt%d" % h, 5.2 * CWS[h] / 4096)}, [], [view("mti", a, b)], after=last)]
+        ts(view("xw", a, b), view("mti", a, b), -7.5, OP.add, C27, OP.add)
+        a = b
+    for a in range(0, 4096, 512):
+        bank = view(psum(), 0, 512)
+        act(bank, view("xw", a, a + 512), bias=-C27)
+        tt(view("ow", a, a + 512), view("mti", a, a + 512), bank, OP.subtract)
 
     def ix(k):
         return view("ix", k, k + 1)
-    A_, G_, PG_, PI_ = ix(0), ix(1), ix(2), ix(3)
-    A1, PI1, A15 = ix(4), ix(5), ix(7)
-    ts(A1, A_, 1.0, OP.add)
+    A_, PG2, G_, PI_, G16, A15, A32 = ix(0), ix(1), ix(2), ix(3), ix(4), ix(5), ix(6)
+    iota(view("pi", 0, 1), [[0, 1]], 0, 1)
+    iota(view("pi", 1, 2), [[0, 1]], 0, 2)
+    ts(view("pi", 4, 6), view("pi", 0, 2), 15, OP.bitwise_and)
+    ts(view("pi", 6, 8), view("pi", 0, 2), 4, OP.arith_shift_right)
+    cp(view("ix", 0, 4), view("pi", 4, 8))
+    iota(view("qg"), [[1, 8], [0, 16]])
+    iota(view("ee"), [[1, 17], [0, 16]])
+    iota(view("cc"), [[0, 17], [16, 16]], 1, 1)
+    iota(view("io640"), [[1, 640]])
     ts(view("blk"), view("qg"), G_, OP.is_equal)
-    ts(view("eqm"), view("qm"), A1, OP.is_equal)
-    tt(view("i128"), view("eqm"), view("blk"), OP.mult)
-    ts(view("b8f", 0, 8), view("pg", 0, 8), G_, OP.is_equal)
-    ts(view("b8f", 8, 16), view("b8f", 0, 8), -2048.0, OP.mult)
-    cp(view("wdf", 0, 16), view("wd"))
-    ts(view("wdf", 16, 20), view("wdf", 0, 16, 4), 16.0, OP.mult, 1.0, OP.add)
-    tt(view("wdf", 20, 24), view("wdf", 16, 20), view("wdf", 1, 16, 4), OP.add)
-    ts(view("cole"), view("c16", 0, 16), A_, OP.add)
-    for k in range(4):
-        scale(view("dd", 128 * k, 128 * k + 128), view("i128"), view("wdf", 20 + k, 21 + k))
-    mms(view("pa0"), [(view("blk"), view("dd"))])
-    act(view("wrb"), view("pa0"))
-    for k in range(8):
-        c = 4 * SETS[k][1] + 1 + SETS[k][0]
-        scale(view("dm", 16 * k, 16 * k + 16), view("eqm", 0, 16), view("wdf", c, c + 1))
-    mms(view("pa1", 0, 128), [(view("blk"), view("dm"))])
-    ts(view("msk"), view("pa1", 0, 128), A_, OP.is_equal)
-
-    def block(kind, s):
-        return PAIR + WSET * SETS.index((kind, s))
-
-    def sel(kind, s, i, w=128):
-        if kind:
-            c = block(kind, s) + 128 * i
-        else:
-            c = 2048 + 384 * i + 128 * (s - 1) if s else 128 * i
-        return view("sel", c, c + w)
-
-    def build0(s, w):
-        for i in range(16):
-            ts(sel(0, s, i, w), view("wrb", 128 * s, 128 * s + w), view("cole", i, i + 1), OP.is_equal, free=True)
-
-    def spread(buf, lo, hi, first, last, st):
-        for k in range(8):
-            scale(view(buf, first(k), last(k), st), view("msk", 16 * lo, 16 * hi), view("b8f", k, k + 1), free=True)
-
-    def build(lo, hi):
-        spread("sel", lo, hi, lambda k: PAIR + WSET * lo + 16 * k, lambda k: PAIR + WSET * (hi - 1) + 129 * 15 + 16 * k + 1, 129)
-
-    def buildS():
-        spread("st", BLOCKS, 8, lambda k: k, lambda k: 256, 8)
+    ts(view("ee"), view("ee"), A_, OP.is_equal)
+    iota(view("eye"), [[1, 16]])
+    ts(view("eye"), view("eye"), A_, OP.is_equal)
+    lin(G16, G_, 16.0, 1.0)
+    const(view("zj"))
+    ts(view("zj", 15, 143, 16), view("qg", 0, 128, 16), G_, OP.is_equal)
+    ts(view("b8f"), view("qg", 0, 128, 16), G_, OP.is_equal, -2048.0, OP.mult)
 
     def jj(i):
-        return view("jj", 128 * i, 128 * i + 128)
+        return view("zj", 15 - i, 143 - i)
 
-    zeros("jj", 0)
-    zeros("sel", PAIR)
-    zeros("sel", PAIR + WSET)
-    const(view("neg1"), -1)
-    for k in range(2, BLOCKS):
-        zeros("sel", PAIR + WSET * k)
-    const(view("rn"), -1)
-    const(view("pzn"))
-    fill(view("jb"), 1.0)
-    for k in range(8):
-        scale(view("jj", 16 * k, 2048, 129), view("jb"), view("b8f", k, k + 1), free=True)
+    def sel(kind, s, i):
+        c = WSET * (3 * s + kind)
+        return view("sel", c + i, c + 2048, 16)
 
-    cp(view("bkl"), view("bki"))
-    cp(view("qcl"), view("qci"))
-    ts(view("qsf"), view("qsi"), 1.0 / 16384, OP.mult)
-    act(view("lrow"), view("io640"), idx=view("qcl"))
-    ts(view("lm"), view("lrow"), A_, OP.is_equal)
-    const(view("xk", 128, 640))
+    def whole(k0, k1=None):
+        return [view("sel", WSET * k, WSET * k + WSET) for k in range(k0, k1 or k0 + 1)]
+    first = view("sel", 0, WSET // 4)
+    do({"V": a_fill(first, 0)}, [], [first])
+    for a in range(WSET // 4, 3 * WSET, WSET // 4):
+        v = view("sel", a, a + WSET // 4)
+        do({"V": a_fill(v, 0), "S": a_act(v, first)}, [first], [v])
+    for a in range(9 * WSET, 12 * WSET, WSET // 4):
+        iota(view("sel", a, a + WSET // 4), [[0, WSET // 4]])
+    for s in range(4):
+        const(view("cmp", WCMP * (3 * s + 1), WCMP * (3 * s + 3)))
+    cp(view("inu"), view("inl", 0, 48))
+    ts(view("code", 0, 4), view("inl", 0, 16, 4), 16.0, OP.mult, G16, OP.add)
+    tt(view("code", 4, 8), view("code", 0, 4), view("inl", 1, 16, 4), OP.add)
+
+    def wave(n, k0, k1):
+        last[0] = do({"Y": a_dma([(T.sel[16 * k:16 * k + 16, k0:k1, 256 * k:256 * k + WCMP], T.cmp[16 * k:16 * k + 16, WCMP * k0:WCMP * k1])
+                                  for k in range(8)], "wave%d" % n, 0.15 * (k1 - k0))},
+                     [view("cmp", WCMP * k0, WCMP * k1)], whole(k0, k1), after=last)
+    for s in range(4):
+        c = 3 * WCMP * s
+        for k in range(3 * s, 3 * s + 3) if s in (1, 2) else ():
+            do({"Y": a_dma([(T.sel[:, k, :], T.sel[:, 11, :])], "dz%d" % k, 1.32)}, whole(11), whole(k), after=last)
+        scale(view("cb", 128 * s, 128 * s + 128), view("blk"), view("code", 4 + s, 5 + s))
+        bank = view(psum(), 0, WCMP)
+        mms(bank, [(view("cb", 128 * s, 128 * s + 128), view("ee"))])
+        tt(view("cmp", c, c + WCMP), bank, view("cc"), OP.is_equal)
+        move(view("cmp", c + WCMP, c + 3 * WCMP, 17), view("eye"), idx=view("inu", 4 * s + 2, 4 * s + 4))
+        if s != 2:
+            wave(min(s, 2), 3 * min(s, 2), 3 * s + 3)
+
+    move(view("lm"), view("eye"), idx=view("inu", 24, 48))
+    ts(view("qsf", 8, 24), view("inl", 56, 72), 1.0 / 16384, OP.mult)
+    cp(view("wdb"), view("inl", 0, 16))
+    for a in range(512, 1024, 256):
+        const(view("res", a, a + 256), -1)
+    for a in range(128, 640, 256):
+        const(view("pzn", a, a + 256))
+        const(view("xk", a, a + 256))
     const(view("cnt", 0, 1), 128)
-    build0(0, 128)
-    build(0, 2)
-    iota(view("cst"), [[16, 16], [0, 8]], 1)
+    const(view("inc", 0, 2))
+    const(view("neg1"), -1)
+    const(view("z8"))
+    const(view("zb"))
+    const(view("one"), 1)
+    const(view("b16"), 16)
+    const(view("cap", 32, 36), 16)
+    const(view("w16", 0, 512))
+    const(view("w16", 512, 640), 16)
+    iota(view("pg"), [[0, 16], [2, 8]])
+    iota(view("c24"), [[16, 24]], 128)
+    iota(view("c15"), [[-1, 16]], 15)
+    iota(view("d15"), [[0, 8], [-1, 16]], 15)
+    select(view("i128"), view("one"), [[-1, 128]], OP.is_equal, 0, 0, 1)
+    select(view("d15"), view("d15"), [[-1, 128]], OP.is_equal, 0, 0, 1)
+    select(view("low"), view("d15"), [[-16, 8], [0, 16]], OP.is_ge, -256, 0, 1)
+    select(view("low"), view("low"), [[16, 8], [0, 16]], OP.is_ge, -256, 15, -1)
+    select(view("blki"), view("one"), [[0, 16], [-16, 8]], OP.is_ge, 0, 0, 1)
+    select(view("blki"), view("blki"), [[0, 16], [16, 8]], OP.is_ge, 0, 15, -1)
+    select(view("pmx"), view("one"), [[-1, 8], [-8, 16]], OP.is_equal, 0, 0, 1)
+    for t in range(2):
+        select(view("keep", 128 * t, 128 * t + 128), view("i128"), [[0, 8], [1, 16]], OP.not_equal, 0, -t, 0)
+    select(view("keep", 256, 384), view("i128"), [[0, 8], [1, 16]], OP.is_ge, 0, -3, 0)
+    ts(view("zb", 120, 128), view("qg", 0, 128, 16), G_, OP.is_equal)
+    ts(view("blkpp"), view("pg"), PG2, OP.is_equal)
+    ts(view("blkp"), view("qg"), 2.0, OP.mult, PG2, OP.is_equal)
+    select(view("tlo"), view("blkp"), [[1, 8], [8, 16]], OP.is_gt, 0, 0, -1)
+    lin(A15, A_, -1.0, 15.0)
+    lin(A32, A_, 32.0)
+    lin(view("k32"), view("io640", 0, 32), 1.0, A32)
+    lin(view("own"), view("c24"), 1.0, PI_)
+    lin(view("cnp"), view("own", 0, 8), 1.0, -639.0)
+    lin(view("sm", 4, 5), A_, -1.0, 767.0)
+    lin(view("nlneg"), view("c24", 0, 8), -1.0, view("sm", 4, 5))
+    iota(view("num", 0, 128), [[1, 128]])
 
-    def consts():
-        lin(PI1, PI_, 1.0, 1.0)
-        lin(A15, A_, -1.0, 15.0)
-        for t in range(3):
-            ts(ix(8 + t), A_, float(t), OP.not_equal)
-            ts(ix(12 + t), A_, float(t), OP.is_equal)
-        ts(ix(11), A_, 3.0, OP.is_ge)
-        const(view("z8"))
-        const(view("zb"))
-        ts(view("zb", 120, 128), view("pg", 0, 8), G_, OP.is_equal)
-        ts(view("blki"), view("pg"), G_, OP.is_equal)
-        ts(view("blkpp"), view("pg"), PG_, OP.is_equal)
-        ts(view("blkp"), view("qg"), PG_, OP.is_equal)
-        ts(view("cst"), view("cst"), A_, OP.add)
-        tt(view("cst"), view("cst"), view("blki"), OP.mult)
-        ts(view("cst"), view("cst"), -1.0, OP.add)
-        ts(view("tmp", 0, 128), view("qm"), PI1, OP.is_equal)
-        tt(view("pmx"), view("tmp", 0, 128), view("blkp"), OP.mult)
-        ts(view("tmp", 128, 256), view("qm"), PI1, OP.is_gt, -1.0, OP.add)
-        tt(view("tmb"), view("tmp", 128, 256), view("blkp"), OP.mult)
-        lin(view("npm"), view("c8"), 1.0, PI_)
-        lin(view("cnp"), view("npm"), 1.0, -511.0)
-        lin(view("sm", 4, 5), A_, -1.0, 639.0)
-        lin(view("nlneg"), view("c8"), -1.0, view("sm", 4, 5))
-        tt(view("c15"), view("eqm", 0, 16), view("c16", 16, 32), OP.mult)
-        const(view("b16"), 16)
-        scale(view("d15"), view("i128"), A15)
-        lin(view("low"), view("blk"), 256.0, -256.0)
-        tt(view("low"), view("low"), view("d15"), OP.add)
-        for t in range(3):
-            scale(view("keep", 128 * t, 128 * t + 128), view("i128"), ix(8 + t))
-        lin(view("nj"), jj(2), -2.0)
-        move(view("num", 0, 128), view("io640", 0, 128))
+    turn = {"gb": 0, "ls": 0}
 
-    xw, ow = view("xw"), view("ow")
-    rot = {"g3": 0, "g4": 0}
-
-    def buf(kind):
-        k = 1024 * (rot[kind] % 8)
-        rot[kind] += 1
-        return view(kind, k, k + 1024)
+    def fresh(name, w):
+        k = w * (turn[name] % (SCRATCH[name][1][1] // w))
+        turn[name] += 1
+        return k
 
     def pl(t):
         return view("pl", 8 * t, 8 * t + 8)
 
-    def lookup(t):
+    def lookup(t, cnt):
         if t == 0:
-            ts(view("ki"), view("qsf", 0, 8), 128.0, OP.mult, -EPS, OP.add)
+            ts(view("ki"), view("inl", 48, 56), 1.0 / 128, OP.mult, -EPS, OP.add)
         else:
-            ts(view("ki"), view("qsf", 8 * t, 8 * t + 8), view("pd0", 8, 9), OP.mult, -EPS, OP.add)
+            ts(view("ki"), view("qsf", 8 * t, 8 * t + 8), cnt, OP.mult, -EPS, OP.add)
         cp(view("kl"), view("ki"))
         if t:
-            scatter(view("xk"), pl(t - 1), view("xi"))
+            scatter(view("xk"), pl(t - 1), view("xi", 128 * t - 128, 128 * t))
         tt(view("qgt"), view("xk") if t else view("xk", 0, 128), view("lm", 128 * t, 128 * t + 128), OP.mult, idx=view("kl"))
-        mms(view("pa0", 0, 8), [(jj(i), view("qgt", i, 128, 16)) for i in range(16)])
-        ts(view("ql"), view("pa0", 0, 8), 2048.0, OP.add)
+        bank = view(psum(), 0, 8)
+        mms(bank, [(jj(i), view("qgt", i, 128, 16)) for i in range(16)])
+        ts(view("ql"), bank, 2048.0, OP.add)
 
-    def pass1(b):
-        lst_ = view("bkl") if b == 0 else view("ql")
-        ts(view("xl%d" % (b % 2)), xw, 0.0625, OP.mult, -C23, OP.add, idx=lst_)
-        step(view("xk", 0, 128) if b == 0 else view("xi"), lst_)
-
-    def pass2(b):
+    def pass12(b):
+        lst_ = view("inu", 16, 24) if b == 0 else view("ql")
+        ts(view("xl", 128 * b, 128 * b + 128), xw, 0.0625, OP.mult, -C23, OP.add, idx=lst_)
+        if b < 3:
+            step(view("xk", 0, 128) if b == 0 else view("xi", 128 * b - 128, 128 * b), lst_)
         for h in (0, 1):
-            step(view("y%d" % b, 1024 * h, 1024 * h + 1024), view("xl%d" % (b % 2), 64 * h, 64 * h + 64))
+            c = 2048 * b + 1024 * h
+            step(view("yy", c, c + 1024), view("xl", 128 * b + 64 * h, 128 * b + 64 * h + 64))
 
-    def psel_x(b, out):
+    def psel_x(b):
+        out = fresh("ls", 128)
         for h in (0, 1):
-            bank = view("pa%d" % h, 0, 64)
-            mms(bank, [(sel(0, 0, a), view("y%d" % b, 1024 * h + a, 1024 * h + 1024, 16)) for a in range(16)])
-            ts(view(out, 64 * h, 64 * h + 64), bank, 2048.0, OP.add)
+            bank, c = view(psum(), 0, 64), 2048 * b + 1024 * h
+            mms(bank, [(sel(0, 0, a), view("yy", c + a, c + 1024, 16)) for a in range(16)])
+            ts(view("ls", out + 64 * h, out + 64 * h + 64), bank, 2048.0, OP.add)
+        return out
 
-    def psel_z(b, z, n=1):
-        for k in range(n):
-            mms(view("pe0", 128 * k, 128 * k + 128), [(sel(0, 1 + z, a), view("y%d" % (b + k), a, 2048, 16)) for a in range(16)], 1, PARTS)
-        move(view("pz%d" % z, 128 * b, 128 * b + 128 * n), view("pe0", 0, 128 * n))
+    def psel_z(b, z):
+        bank = view(psum(), 0, 128)
+        mms(bank, [(sel(0, 1 + z, a), view("yy", 2048 * b + a, 2048 * b + 2048, 16)) for a in range(16)], PARTS)
+        move(view("pz%d" % z, 128 * b, 128 * b + 128), bank)
 
-    def p3(s, src, out, slow=0):
+    def zlist(z, c, idx=None):
+        out = fresh("ls", 128)
+        ts(view("ls", out, out + 128), view("pz%d" % z, 0 if idx else c, c + 128), 2048.0, OP.add, idx=idx)
+        return out
+
+    def p3(s, src, w):
+        out, gb = fresh("ls", 128), fresh("gb", 2048)
         for h in (0, 1):
-            bank = view(("pa%d" % h, "pb%d" % h, "pe0")[slow], 64 * h, 64 * h + 64)
-            g3 = buf("g3")
-            w = 32 if slow == 2 else 64
+            bank, c = view(psum(), 0, 64), gb + 1024 * h
             for a in range(0, 64, w):
-                step(view("g3", g3[2] + 16 * a, g3[2] + 16 * (a + w)), view(src, 64 * h + a, 64 * h + a + w))
-            mms(bank, [(sel(1, s, e), view("g3", g3[2] + e, g3[3], 16)) for e in range(16)])
-            ts(view(out, 64 * h, 64 * h + 64), bank, 2048.0, OP.add)
+                step(view("gb", c + 16 * a, c + 16 * (a + w)), view("ls", src + 64 * h + a, src + 64 * h + a + w))
+            mms(bank, [(sel(1, s, e), view("gb", c + e, c + 1024, 16)) for e in range(16)])
+            ts(view("ls", out + 64 * h, out + 64 * h + 64), bank, 2048.0, OP.add)
+        return out
 
-    def p4g(h, src):
-        g4 = buf("g4")
-        move(g4, ow, idx=view(src, 64 * h, 64 * h + 64))
-        return g4
-
-    def p4s(h, g4, extra=(), skip=-1, s=0):
-        bank = view("pb%d" % h, 0, 64)
-        mms(bank, [(sel(2, s, e), view("g4", g4[2] + e, g4[3], 16)) for e in range(16) if e != skip] + list(extra))
-        return bank
-
-    def p4z(s, src, w=64):
+    def walk(s, src, w):
+        src, gb = p3(s, src, w), fresh("gb", 2048)
         for a in range(0, 128, w):
-            move(view("gt", 16 * a, 16 * (a + w)), ow, idx=view(src, a, a + w))
-        bank, m = view("pb%d" % (s % 2), 0, 128), 128 * (s - 2)
+            move(view("gb", gb + 16 * a, gb + 16 * (a + w)), ow, idx=view("ls", src + a, src + a + w))
+        return gb
+
+    def p4s(gb, out, c0, s, t=-1):
+        for h in (0, 1):
+            bank, c, o = view(psum(), 0, 64), gb + 1024 * h, c0 + 64 * h
+            mms(bank, [(sel(2, s, e), view("gb", c + e, c + 1024, 16)) for e in range(16) if e != t]
+                + ([(jj(t), view("gz%d" % t, o, o + 64))] if t >= 0 else []))
+            move(view(out, o, o + 64), bank)
+
+    def p4z(s, gb):
+        bank, c = psum(), WSET * (3 * s + 2)
 
         def fn(e):
             for k in range(16):
-                r = e.matmul(T[bank[1]][:, k:128:16], T.gt[:, k:2048:16], T.st[:, m + 8 * k:m + 8 * k + 8], True, True)
+                r = e.matmul(ap(view(bank, k, 128, 16)), ap(view("gb", gb + k, gb + 2048, 16)), ap(view("sel", c + 17 * k, c + 2048, 256)), True, True)
             return r
-        do({"P": (fn, (0, 0, 0, 16 * 64))}, [view("gt"), view("st", m, m + 128)], [bank])
-        return bank
-
-    def evac_r(b, h, bank):
-        move(view("rr", 128 * b + 64 * h, 128 * b + 64 * h + 64), bank)
+        do({"P": (fn, (0, 0, 0, 0, 16 * 64, 0, 0), None)}, [view("gb", gb, gb + 2048)] + whole(3 * s + 2), [view(bank, 0, 128)])
+        return view(bank, 0, 128)
 
     def compare(t):
         b, L = t + 1, 128 * (t + 1)
         q = view("rr", 128 * b, 128 * b + 128)
         act(view("r2", 0, L), view("rr", 0, L), scale=32.0, func=AF.Square)
         act(view("rq2"), q, scale=32.0, func=AF.Square)
+        bank = view(psum(), 0, 8)
+        mms(bank, [(view("zb", 120 - 8 * i, 248 - 8 * i), view("rq2", i, 128, 16)) for i in range(16)])
+        tt(view("top"), view("own", 8 * t, 8 * t + 8), bank, OP.subtract)
+        lin(view("nn"), bank, -1.0)
         for k in range(8):
-            scale(view("lhb", k, 1024, 8), q, view("b8f", 8 + k, 9 + k), free=True)
+            scale(view("lhb", k, 1024, 8), q, view("b8f", k, k + 1), free=True)
         for c in range(8):
-            bank = view(("pc0", "pc1", "pa1")[c % 3], 0, L)
+            bank = view(psum(), 0, L)
             mms(bank, [(view("blki"), view("r2", 0, L)), (view("lhb", 128 * c, 128 * c + 128), view("rr", 0, L))])
-            scan(view("sc", 384 * c, 384 * c + L), bank, view("neg1", 0, L), 8000000.0, OP.min, OP.add)
-        mms(view("pd0", 0, 8), [(view("zb", 120 - 8 * i, 248 - 8 * i), view("rq2", i, 128, 16)) for i in range(16)])
-        act(view("nn"), view("pd0", 0, 8), scale=-1.0)
+            scan(view("sc", 384 * c, 384 * c + L), bank, view("neg1", 0, L), view("top", c, c + 1), OP.min, OP.add)
 
     def append(t):
-        L, b = 128 * (t + 1), t + 1
-        last = (T.sc[:, L - 1::384], "sc", 0, 3072, 8)
-        tt(view("uu"), last, view("nn"), OP.is_ge)
-        scan(view("inc"), view("uu"), view("z8"), 0.0, OP.add, OP.add)
-        tt(view("vl"), last, view("nn"), OP.subtract)
+        L = 128 * (t + 1)
+        least = view("sc", L - 1, 3072, 384)
+        bank = psum()
+        cnt, tot = view(bank, 8, 9), view("inc", 9, 10)
+        tt(view("uu"), least, view("nn"), OP.is_ge)
+        tt(view("mn"), least, view("nn"), OP.subtract)
+        scan(view("inc", 2, 10), view("uu"), view("z8"), 0.0, OP.add, OP.add)
         tt(view("ww"), view("uu"), view("cnp"), OP.mult)
-        mms(view("pd0", 8, 9), [(view("i128"), view("cnt", t, t + 1)), (view("blkp"), view("inc", 7, 8))])
-        mms(view("pd0", 0, 8), [(view("blkp"), view("inc")), (view("tmb"), view("uu")), (view("i128"), view("nlneg")), (view("pmx"), view("ww"))])
+        mms(cnt, [(view("i128"), view("cnt", t, t + 1)), (view("blkp"), tot)])
+        mms(view(bank, 0, 8), [(view("blkp"), view("inc", 1, 9)), (view("tlo"), view("uu")), (view("i128"), view("nlneg")), (view("pmx"), view("ww"))])
         if t < 2:
-            mms(view("pd0", 9, 10), [(view("blkpp"), view("inc", 7, 8))])
-        tt(view("mn"), view("vl"), view("npm"), OP.min)
-        mms(view("pc0", 0, 8), [(view("pmx"), view("mn"))])
-        cp(pl(t), view("pd0", 0, 8))
+            mms(view(bank, 9, 10), [(view("blkpp"), tot)])
+        mb = view(psum(), 0, 8)
+        mms(mb, [(view("pmx"), view("mn"))])
+        cp(pl(t), view(bank, 0, 8))
         if t < 2:
-            lookup(t + 1)
-            move(view("cnt", t + 1, t + 2), view("pd0", 8, 9))
-            ts(view("cnp"), view("cnp"), view("pd0", 9, 10), OP.add)
-        ts(view("ml"), view("pc0", 0, 8), float(L), OP.add)
-        nb = view("num", 128 * b, 128 * b + 128)
-        move(nb, view("io640"), idx=pl(t))
-        move(view("ymt", 128 * t, 128 * t + 128), view("num", 0, 128 * b + 128), idx=view("ml"))
-        if t:
-            ts(view("lm3"), view("pz%d" % t, 0, L + 128), 2048.0, OP.add, idx=view("ml"))
+            lookup(t + 1, cnt)
+            move(view("cnt", t + 1, t + 2), cnt)
+            ts(view("cnp"), view("cnp"), view(bank, 9, 10), OP.add)
         else:
-            tt(view("ne"), view("an"), view("aq"), OP.not_equal, idx=view("ml"))
+            ts(view("cap", 0, 32), view("k32"), cnt, OP.is_lt)
+            lin(view("cap", 0, 32), view("cap", 0, 32), 17.0, -1.0)
+        ts(view("ml"), mb, float(L), OP.add)
+        move(view("num", L, L + 128), view("io640"), idx=pl(t))
+        move(view("res", 128 * t, 128 * t + 128), view("num", 0, L + 128), idx=view("ml"))
         if t < 2:
-            q = view("rr", 128 * b, 128 * b + 128)
-            ts(view("inv"), nb, 512.0, OP.is_ge, 16.0, OP.mult)
-            tt(q, q, view("inv"), OP.max)
-        else:
-            ts(view("invn"), view("io640", 0, 512), view("pd0", 8, 9), OP.is_ge)
-            move(view("pzn", 0, 128), view("pz2", 0, 128))
-            move(view("rn", 0, 128), view("rr", 0, 128))
-            for k in range(3):
-                scatter(view("pzn"), pl(k), view("pz2", 128 * k + 128, 128 * k + 256))
-                scatter(view("rn"), pl(k), view("rr", 128 * k + 128, 128 * k + 256))
+            q = view("rr", L, L + 128)
+            tt(q, view("w16"), q, OP.max, idx=pl(t))
+
+    def in_order(win, src):
+        move(view(win[0], win[1], win[1] + 128), view(src, 0, 128))
+        for k in range(3):
+            scatter(win, pl(k), view(src, 128 * k + 128, 128 * k + 256))
 
     def winner(t):
-        mx = view("sm", 1, 2)
+        mx, bank = view("sm", 1, 2), psum()
         if t:
-            sc = view("pd0", 48, 49)
-            mms(view("pd0", 64, 192), [(view("blk"), view("low")), (view("b16"), view("ne"))])
-            mms(sc, [(view("d15"), view("jb", 0, 1)), (view("ne"), view("b16", 0, 1))])
-            reduce(mx, view("pd0", 64, 192), OP.max)
+            sc = view(bank, 128, 129)
+            mms(view(bank, 0, 128), [(view("blk"), view("low")), (view("b16"), view("ne"))])
+            mms(sc, [(view("d15"), view("one", 0, 1)), (view("ne"), view("b16", 0, 1))])
+            reduce(mx, view(bank, 0, 128), OP.max)
         else:
             dc, sc = view("sm", 0, 1), view("sm", 2, 3)
             reduce(dc, view("ne"), OP.add)
-            ts(view("dd2"), view("eqm", 0, 16), dc, OP.mult, 16.0, OP.mult)
-            mms(view("pd0", 16, 32), [(view("blk"), view("dd2")), (view("blk"), view("c15"))])
+            ts(view("dd2"), view("eye"), dc, OP.mult, 16.0, OP.mult)
+            mms(view(bank, 0, 16), [(view("blk"), view("dd2")), (view("i128"), view("c15"))])
             ts(sc, dc, 16.0, OP.mult, A15, OP.add)
-            reduce(mx, view("pd0", 16, 32), OP.max)
-        oh = view("oh", t, t + 1)
+            reduce(mx, view(bank, 0, 16), OP.max)
+        oh, ws, bank = view("oh", t, t + 1), view("ws", 4 * t, 4 * t + 4), psum()
         ts(oh, sc, mx, OP.is_equal)
-        scale(view("ws"), view("wdf", 4 * t + 4, 4 * t + 8), oh)
-        mms(view("pd0", 32, 36), [(view("blk"), view("ws"))])
-        ts(view("mk", 2 * t, 2 * t + 2), view("pd0", 34, 36), A_, OP.is_equal)
-        lin(view("mk", 8 + t, 9 + t), view("mk", 2 * t, 2 * t + 1), 0.0625)
-        lin(view("mk", 12 + t, 13 + t), view("mk", 2 * t, 2 * t + 1), -C23 - 2048.0)
+        scale(ws, view("wdb", 4 * t + 4, 4 * t + 8), oh)
+        mms(view(bank, 0, 4), [(view("blk"), ws)])
+        ts(view("mk", 8 + t, 9 + t), view(bank, 2, 3), A_, OP.is_equal, 0.0625, OP.mult)
+        ts(view("mk", t, t + 1), view(bank, 3, 4), A_, OP.is_equal)
+        lin(view("mk", 12 + t, 13 + t), view("mk", 8 + t, 9 + t), -C27 - 32768.0)
         if t == 0:
-            ts(view("mk", 15, 16), view("pd0", 32, 33), 16.0, OP.mult, view("pd0", 33, 34), OP.add)
-        scale(view("ya", 4 * t, 4 * t + 4), view("pd0", 32, 36), ix(12 + t))
+            ts(view("mk", 15, 16), view(bank, 0, 1), 16.0, OP.mult, view(bank, 1, 2), OP.add)
+            ts(view("cmp", WCMP, 3 * WCMP, WCMP), view(bank, 2, 4), A_, OP.is_equal)
+            ts(view("cmp", 0, 16), view("cc", 0, 16), G16, OP.subtract, view("mk", 15, 16), OP.is_equal)
 
     def wpass(t, c0, c1, src):
         n = (c1 - c0) // 16
         h = (c1 - c0) // (2 if n > 16 else 1)
         for a in range(c0, c1, h):
             scale(view("pw", a, a + h), view(src, a, a + h), view("oh", t, t + 1))
-        bank, bank2 = view("pc0", 0, n), view("pc1", 0, n)
+        bank, bank2 = view(psum(), 0, n), view(psum(), 0, n)
         mms(bank, [(jj(i), view("pw", c0 + i, c1, 16)) for i in range(16)])
-        lw, lw2 = view("lw", 0, n), view("lw2", 0, n)
-        ts(lw, bank, 2048.0, OP.add)
+        ts(view("lw", 0, n), bank, 2048.0, OP.add)
         m16, mb = view("mk", 8 + t, 9 + t), view("mk", 12 + t, 13 + t)
         for a in range(0, c1 - c0, h):
             o, li = view("gw", a, a + h), view("lw", a // 16, (a + h) // 16)
             do({"S": a_act(o, xw, m16, mb, idx=li), "V": a_ts(o, xw, -C27 - 32768.0, OP.add, m16, OP.mult, idx=li)}, [xw, m16, mb, li], [o])
         mms(bank2, [(jj(i), view("gw", i, c1 - c0, 16)) for i in range(16)])
-        ts(lw2, bank2, 2048.0, OP.add)
+        ts(view("lw2", 0, n), bank2, 2048.0, OP.add)
         for a in range(0, c1 - c0, h):
-            scale(view("gz%d" % t, c0 + a, c0 + a + h), ow, view("mk", 2 * t + 1, 2 * t + 2), idx=view("lw2", a // 16, (a + h) // 16))
+            scale(view("gz%d" % t, c0 + a, c0 + a + h), ow, view("mk", t, t + 1), idx=view("lw2", a // 16, (a + h) // 16))
 
     def rupdate(t):
         L = 128 * (t + 2)
-        bank = view("pc0", 0, L)
+        bank = view(psum(), 0, L)
         mms(bank, [(view("keep", 128 * t, 128 * t + 128), view("rr", 0, L)), (jj(t), view("gz%d" % t, 0, L))])
         move(view("rr", 0, L), bank)
 
-    pass1(0)
-    lookup(0)
-    pass1(1)
-    pass2(0)
-    psel_x(0, "l30")
-    pass2(1)
-    psel_x(1, "l31")
-    p3(0, "l30", "l40")
-    p3(0, "l31", "l41")
-    build0(1, 384)
+    pass12(0)
+    lookup(0, None)
+    pass12(1)
     for b in (0, 1):
-        for h in (0, 1):
-            evac_r(b, h, p4s(h, p4g(h, "l4%d" % b)))
-    consts()
-    build(2, BLOCKS)
-    buildS()
+        p4s(walk(0, psel_x(b), WIDE), "rr", 128 * b, 0)
     for z in range(3):
-        psel_z(0, z, 2)
+        for b in (0, 1):
+            psel_z(b, z)
     compare(0)
-    for b, x in ((1, 2), (0, 3)):
-        ts(view("l3%d" % x), view("pz0", 128 * b, 128 * b + 128), 2048.0, OP.add)
-        p3(1, "l3%d" % x, "l4%d" % (x if x == 2 else 4), 1)
-        for h in (0, 1):
-            c = 128 * b + 64 * h
-            move(view("an", c, c + 64), p4s(h, p4g(h, "l4%d" % (x if x == 2 else 4)), s=1))
+    for b in (1, 0):
+        p4s(walk(1, zlist(0, 128 * b), FINE), "an", 128 * b, 1)
     move(view("aq"), view("an", 128, 256))
     for t in range(3):
         b = t + 2
         append(t)
         if t:
-            p3(1 + t, "lm3", "l43")
-        if t < 2:
-            pass1(b)
-            pass2(b)
-            psel_x(b, "l31")
-        if t:
-            tt(view("ne"), p4z(1 + t, "l43"), view("aq"), OP.not_equal)
+            tt(view("ne"), p4z(1 + t, walk(1 + t, zlist(t, 128 * (t + 1), view("ml")), FINE)), view("aq"), OP.not_equal)
+        else:
+            tt(view("ne"), view("an"), view("aq"), OP.not_equal, idx=view("ml"))
         winner(t)
-        if t < 2:
-            for z in range(t, 2):
-                psel_z(b, z)
-            p3(0, "l31", "l41")
+        if t == 2:
+            break
+        pass12(b)
+        gs = walk(0, psel_x(b), WIDE)
+        for z in range(t, 3):
+            psel_z(b, z)
         if t == 0:
             scale(view("gz0", 0, 256), view("an"), view("oh", 0, 1))
             wpass(0, 256, 384, "pz0")
         else:
-            wpass(t, 0, 512, "pzn" if t == 2 else "pz1")
-        if t == 2:
-            break
-        gs = [p4g(h, "l41") for h in (0, 1)]
+            wpass(1, 0, 512, "pz1")
         rupdate(t)
-        for h in (0, 1):
-            c = 128 * b + 64 * h
-            evac_r(b, h, p4s(h, gs[h], [(jj(t), view("gz%d" % t, c, c + 64))], t))
+        p4s(gs, "rr", 128 * b, 0, t)
         if t == 0:
-            ts(view("sel", 0, 2048, 16), view("cst"), view("mk", 15, 16), OP.is_equal)
-            for k in (1, 2):
-                ts(view("sel", block(k, 0), block(k, 0) + 128, 16), view("b8f", 0, 8), view("mk", k - 1, k), OP.mult)
-        psel_z(b, 2)
+            wave(3, 0, 3)
         compare(t + 1)
-        ts(view("l32"), view("pz%d" % (t + 1), 128 * b, 128 * b + 128), 2048.0, OP.add)
-        p3(2 + t, "l32", "l42", 2)
-        move(view("aq"), p4z(2 + t, "l42", 32))
+        move(view("aq"), p4z(2 + t, walk(2 + t, zlist(t + 1, 128 * b), FINE)))
+    in_order(view("pzn"), "pz2")
+    in_order(view("res", 384, 1024), "rr")
+    wpass(2, 0, 512, "pzn")
 
-    ends = []
+    send(learner, view("resl"), view("res", 0, 896), "ares", 1.2, 2)
+    bank = psum()
+    mms(view(bank, 32, 36), [(view("keep", 256, 384), view("wdb", 0, 4))] + [(jj(t), view("ws", 4 * t, 4 * t + 4)) for t in range(3)])
+    mms(view(bank, 0, 32), [(jj(i), view("gz2", 32 * i, 32 * i + 32)) for i in range(16)])
+    tt(view("fin"), view(bank, 0, 36), view("cap"), OP.min)
+    send(learner, view("finl"), view("fin"), "afin", 0.1, 2)
+    do({"Y": a_dma([(T.ym[:], T.resl[::16, 0:384])], "dym", 0.1)}, [view("resl")], [])
+    i = do({"Y": a_dma([(T.yr[:], T.resl[:, 384:896])], "dyr", 0.7)}, [view("resl")], [])
+    j = do({"Y": a_dma([(T.yr[2::16, :], T.finl[:, 0:32])], "dy2", 0.1)}, [view("finl")], [])
+    ops[j]["deps"].add(i)
+    do({"S": a_dma([(T.ye[:], T.finl[:, 32:36])], "dye", 0.1)}, [view("finl")], [])
 
-    def out(dst_ap, src_ap, v, sem):
-        do({"Y": (lambda e: e.dma_start(dst_ap, src_ap).then_inc(T.sem[sem], 16), (0.1, 0, 0, 0))}, [v], [], lat=2.0, tok=())
-        ends.append(sem)
-    out(T.ym[:], T.ymt[::16, :], view("ymt"), "dym")
-    yet = view("ya", 12, 16)
-    scale(yet, view("wdf", 0, 4), ix(11))
-    for t in range(3):
-        tt(yet, yet, view("ya", 4 * t, 4 * t + 4), OP.add)
-    out(T.ye[:], T.ya[:, 12:16], yet, "dye")
-    mms(view("pc0"), [(view("keep", 256, 384), view("rn", 0, 512)), (view("nj"), view("invn")), (jj(2), view("gz2"))])
-    ts(view("yrt"), view("pc0"), -1.0, OP.max)
-    out(T.yr[:], T.yrt[:], view("yrt"), "dyr")
-
-    PLAN["ops"], PLAN["p"] = ops, plan(ops)
-    pos = {q: 0 for q in queue}
+    if "p" not in PLAN:
+        PLAN["ops"] = ops
+        PLAN["p"] = plan(ops)
+    order, _, extra = PLAN["p"]
+    pos = dict.fromkeys(queue, 0)
     seen = {q: {} for q in queue}
-    for i, q in PLAN["p"]:
-        ops[i]["run"] = q
-    for i, q in PLAN["p"]:
+    run, tok = dict(order), {}
+    for i, q in order:
         o = ops[i]
-        if q == "D":
-            continue
         want = {}
-        for d in o["deps"] | set(d for d in o["soft"] if ops[d]["run"] != q):
-            if ops[d]["tok"]:
-                s, n = ops[d]["tok"]
-                want[s] = max(want.get(s, 0), n)
+        for d in list(o["deps"]) + [d for d in o["soft"] if run[d] != q] + [d for d in extra.get(i, []) if run[d] + q != "PP"]:
+            s, n = tok[d]
+            want[s] = max(want.get(s, 0), n)
         for s in sorted(want):
             if seen[q].get(s, 0) < want[s]:
                 queue[q].wait_ge(T.sem[s], want[s])
                 seen[q][s] = want[s]
         r = o["alt"][q][0](queue[q])
-        if o["tok"] is None:
+        tok[i] = o["alt"][q][2]
+        if tok[i] is None:
             pos[q] += 1
             r.then_inc(T.sem[CSEM[q]], 1)
-            o["tok"] = (CSEM[q], pos[q])
-    for s in ends:
+            tok[i] = (CSEM[q], pos[q])
+    for s in ("dym", "dy2", "dye"):
         g.sync.wait_ge(T.sem[s], 16)
-    g.wait_ge(T.sem.sent, (NCH + len(OWS)) * neng)
+    g.wait_ge(T.sem.sent, sent[0])
     for q in sorted(CSEM):
         g.wait_ge(T.sem[CSEM[q]], pos[q])

@@ -4,41 +4,41 @@ OP = AluOpType
 AF = ActivationFunctionType
 CWS = [512] * 7 + [384, 128]
 NCH = len(CWS)
-C27 = 201326592.0
-C23 = 12582912.0
 EPS = 0.499969482421875
 PARTS = 4
 WSET, WCMP = 2064, 272
-NBUF = 14
+NBUF = 12
 WIDE, FINE = 64, 32
+SETS = [(1, 0), (2, 0), (0, 1), (1, 1), (2, 1), (0, 2), (0, 3), (1, 2), (2, 2), (1, 3), (2, 3)]
 DIGITS = "0123456789abcdefghijklmnopqrstuvwxyzABCDEFGHIJKLMNOPQRSTUVWXYZ"
-ORDER = "1Q2C036d7s5D2500091N0f37302F0l0r3Q222k6f1W6i341T2P2U0x0D061Z7h2Y2h2e5X71637b0J3A2J7m5U0P0V392r602n0c113N2M0i6V2z140o2t171a0u3J7k1d1g2S2w78411j3Y4E4g446D0A280G6l3D3G474a4d7H4w5n4y5R0M7q5k1p1v4j1B0Y0S7y7K5O1H7v7B4B4p3x4s7N7Q4m1s1m4H5F7T6Y553r7W3l3u7F883i8b4K3c1y828e8l586r858U8X7Z8h8t663V1K90934Q9f8n748w978q3S9i991E3f8z4U8F6G4W8D9l9c9o5b8I9G9J9M6o4N6M9s9P4Z3o9Sdm5q529V9Y6udta1a45e6Ja89u9A8L6S9ycx5M8O6P5hdpdv6xdB9DcAcEbrbD5I8RbxcNcGbJcJbobbbGbebzb8cQbhbtcldycf5zbRbLc9bkcrc369bUcobXc6cic0ccbOcu5wcScVeedEdHdKd1encYda5tekeqd8etd4eweCeFeLdNdQaaeIdgeOdXeReUehfYaddTg4agezf36A2bape5dkg8e9ddeceYajdZe2fff6gaf9gdgmfiflgggjfrfcgKfofufxgNgQgTgWgwgZgp7dfAfDfGhwhzhCf0htfJg1gygsamfNgBhFhRgEashUhIfPgIhLh2h5h8avayhchOaBjBjIfVjEici3i7hXi1iyifiEivaEisiNiHiKiBjQfSjKjTjNiiilioiPiSj1j4iViYk2jpjsjdjgjvjyj7jajjhejmkkk5jWknjZaHkqktkbkFl9lllrkwkzkCkIhhkLlAaTk8lplEaWkRlukOlGaKlxlPkUlJlSkXlNl0mvmyaZb2kekhhklWaNaQmClYm1i9spmEb6lcmHnem4ssm7mal3l6mdmKmNmhnhnknnnJmjntmQmTn0mmnqnLnOnRlfmWmplimtn2nXnUhnn5nbn9nwnzo0o3o9nCnGo7pTpZhrpXsvocoiooomosofsCp5q2p2ouoWq5oZoToKsEoxoAoMoDoPppsHpsqbpNpQpvpypjpmq8qnp7papdpgoHqkqeqhpHpKpBpEqFqUr6qqqCqtqwrfrlqIrjrvrorrrxrJrAqLqOqRrHrDqXrPrNqzrSsKr9rcrVrYsys1s4s7sbsRthsdsgsmtzsNsjsTsWsZt3t5t8tktftbtnr0r3tqtttwtFtC"
+ORDER = "1s032k22001R1K3a2F092Y1p0f2V0l1v6o2o370r2D1y2R1E2J1C2t2x2M252z0c0i117m7C0o0u0x140D2b282e0J1W6r067q1H2h3377175X1a1Z0A1d0G0M7v1g30661T3m1j3o7W1N3s0P0V3i5A0S4q3u0Z4s4O2Q5w522s7K3y6l7N4v3G4j3S414C4Z3D4m7Z6P827a553P4g445R3J3V3M7z3A4y4a474E7R4d3Y867t887T586x4Q8h3f8k6J8q8cdg8f8u968o9c8G9a1m8wcfci4Hclco8I6f9g9r9jdj8Mcs8z5b6Admdp9l8C694T8P717d7g8R6M9u909x9p9Bcy6D8Ucv5e9DcA5hcD7F5qcG5U9G9M8X5F9S94cKcM9K4X6icT9Pb9b6dtblbfaTbcbobi5naWbr63dyaZaQdwbRcQc3bzd2cVb3bt9V9YbU60bwbLc6dBc9bO6ubCcc7HbFbXc03cbI74ekcYdLd4dad8eqewetdEezeCdIdTa7aaad4LendNeJeL5OeFeOdR5DeReUdXam6ceXdee5f7dZa1fWeig1ape2e9ebef6Y6Sg5f9f1agfiflg7gafogmfvgd5k5tfrfxgggkfAgvgTgWgZh2f3gpgzh6fDgtfQffh8gBfGa47jgIfJhIgKgFhbhehhfMhMhGgNhOhlhRgRhVi0hXjRasjThn5LfZicifk5i6iafSjWi3iuiW6GiQaBiriNixfciHiZj2iTiKja6Vii5IjgakjsiAk0iDjmjdjjk3jvjpjEjyjHo6jBj4kejKj7k8jNkbkzaEaHkRkwavkokhkCljlvkFlAlMkIilkLlykOaKlDkUkXl0lGl3lKlPkklSl6lVlZl9hqhthwaOmFm1azmHm4hzmLkqkum7sImalmlomNmdhCmgmTmQmjnznCmZmWn3mmipmpnFmBnInLsKnbn5n8msmvo9mynfnhlrodlcnOogoinknroloonRnnnwovnUnXoDoro1nuqioxqeoHoJoNoAlfoSpqphpnoPpep8pkqkpbp5oVsNquoYqnpKpNpEq2pHpWq8p2pyq5pZqCpsqrqFqbpBpvpQpTqwqAqXqUqIo4rcrorxr0r3r6r9rErArQrGrMrJrSrgqLrZs1rVsUs8s4sQrrsWqOqRsasdrusZt5sgsjsmrispt8sFssrmt2svsytztbsBtCtftlthtntqtwtutFtItLtOtRtUtX"
 
 F, B, H, I, U = "float32", "bfloat16", "float16", "int32", "uint16"
 SCRATCH = {}
 for _n, _w, _d in [
-        ("mti", 4096, I), ("xw", 4096, F), ("ow", 4096, B), ("inp", 72, I), ("inl", 72, I), ("inu", 48, U),
+        ("mti", 4096, I), ("xw", 4096, I), ("ow", 4096, I), ("inp", 72, I), ("inl", 72, I), ("inu", 48, U),
         ("res", 1024, F), ("resl", 896, F), ("fin", 36, F), ("finl", 36, F), ("cap", 36, F),
         ("pi", 8, I), ("ix", 24, F), ("qg", 128, B), ("pg", 128, B), ("io640", 640, F), ("c24", 24, F), ("cc", WCMP, F), ("ee", WCMP, B),
         ("one", 128, B), ("blk", 128, B), ("eye", 16, B), ("i128", 128, B), ("zj", 144, B), ("blkp", 128, B), ("tlo", 128, B),
         ("pmx", 128, B), ("blkpp", 128, B), ("blki", 128, B), ("b16", 128, B), ("d15", 128, B), ("low", 128, B), ("zb", 248, B),
         ("b8f", 8, F), ("keep", 384, B), ("nlneg", 8, H), ("own", 24, F), ("cnp", 8, F), ("neg1", 384, F), ("z8", 8, F), ("c15", 16, B),
-        ("k32", 32, F), ("w16", 640, B), ("wdb", 16, B), ("code", 8, F), ("cb", 512, H), ("cmp", 12 * WCMP, B),
-        ("lm", 384, B), ("qsf", 24, F), ("ki", 8, I), ("kl", 8, U), ("qgt", 128, H), ("ql", 8, U), ("xi", 256, F),
+        ("k32", 32, F), ("w16", 640, B), ("wdb", 16, B), ("code", 8, F), ("cb", 512, H), ("cmp", 11 * WCMP, B),
+        ("ex0", 2048, B), ("row", 128, H), ("cst", 128, F),
+        ("lm", 384, B), ("qsf", 24, F), ("kl", 8, U), ("qgt", 128, H), ("ql", 8, U), ("xi", 256, F),
         ("xl", 512, U), ("xk", 640, F), ("yy", 8192, H), ("gb", 2048 * NBUF, H), ("ls", 128 * 20, U),
-        ("pz0", 384, F), ("pz1", 512, F), ("pz2", 512, F), ("pzn", 640, F), ("rr", 512, B), ("an", 256, B),
-        ("r2", 384, B), ("rq2", 128, B), ("lhb", 1024, B),
+        ("pw0", 384, H), ("pw1", 512, H), ("pw2", 512, H), ("zo", 144, B), ("pz1", 384, F), ("pz2", 512, F), ("pzn", 640, F),
+        ("rr", 512, B), ("an", 256, B), ("r2", 384, B), ("rq2", 128, B), ("lhb", 1024, B),
         ("sc", 3072, F), ("nn", 8, F), ("top", 8, F), ("uu", 8, H), ("inc", 10, H), ("ww", 8, H), ("mn", 8, H), ("ml", 8, U),
         ("cnt", 4, H), ("pl", 24, U), ("num", 512, F), ("aq", 128, B), ("ne", 128, B), ("sm", 8, F), ("dd2", 16, B),
-        ("oh", 4, F), ("ws", 12, B), ("mk", 16, F), ("pw", 512, H), ("lw", 32, U), ("gw", 512, H), ("lw2", 32, U),
+        ("oh", 4, F), ("ws", 12, B), ("mk", 16, F), ("lw", 32, U), ("gw", 512, H), ("lw2", 32, U),
         ("gz0", 384, B), ("gz1", 512, B), ("gz2", 512, B)]:
     SCRATCH[_n] = ("sbuf", [128, _w], _d)
-SCRATCH["sel"] = ("sbuf", [128, 12, WSET], B)
+SCRATCH["sel"] = ("sbuf", [128, len(SETS), WSET], B)
 BANKS = ["bank%d" % _k for _k in range(8)]
 for _n in BANKS:
     SCRATCH[_n] = ("psum", [128, 512], F)
 SEMAPHORES = (["cv", "cs", "cp", "cg", "sent", "din", "din2", "ain", "ares", "afin", "dym", "dyr", "dy2", "dye"]
-              + ["dmt%d" % h for h in range(NCH)] + ["wave%d" % h for h in range(4)] + ["dz%d" % h for h in range(3, 9)])
+              + ["dmt%d" % h for h in range(NCH)] + ["wave%d" % h for h in range(4)] + ["dz%d" % h for h in range(len(SETS))])
 CSEM = {"V": "cv", "S": "cs", "P": "cp", "G": "cg"}
 PLAN = {}
 
@@ -116,7 +116,7 @@ def rank_program(g, core, T, topo):
                     soft.add(j)
         ps = [v[0] for v in list(reads) + list(writes) if inps(v)]
         ops.append({"alt": alt, "deps": deps, "soft": soft - deps, "free": free, "ps": ps[0] if ps else None,
-                    "nm": writes[0][0] if writes else "-"})
+                    "nm": writes[0][:2] if writes else ("-", 0)})
         for v in writes:
             if not free:
                 for d in (wrote, readers):
@@ -176,15 +176,12 @@ def rank_program(g, core, T, topo):
     def a_fill(v, c):
         return (lambda e: e.memset(ap(v), float(c)), dv(v[4], two(v)), None)
 
-    def ts(out, in0, s1, op0, s2=None, op1=None, idx=None):
-        do({"V": a_ts(out, in0, s1, op0, s2, op1, idx)}, [in0] + sca(s1) + sca(s2) + lst(idx), [out])
+    def ts(out, in0, s1, op0, s2=None, op1=None):
+        do({"V": a_ts(out, in0, s1, op0, s2, op1)}, [in0] + sca(s1) + sca(s2), [out])
 
     def tt(out, in0, in1, op, idx=None):
         w = dg(out[4]) if idx else dv(out[4] * (1 if inps(in0) or inps(in1) else 2))
         do({"V": (lambda e: e.tensor_tensor(ap(out), ind(in0, idx), ap(in1), op), w, None)}, [in0, in1] + lst(idx), [out])
-
-    def cp(out, in_):
-        do({"V": a_cp(out, in_)}, [in_], [out])
 
     def scatter(win, idx, in_):
         do({"V": (lambda e: e.tensor_copy(ap(win).indirect(ap(idx)), ap(in_)), (0.05, 0, 0, in_[4], 0, 0, 0), None)}, [in_, idx], [win])
@@ -204,12 +201,14 @@ def rank_program(g, core, T, topo):
     def scale(out, in_, col, free=False, idx=None):
         do({"S": a_act(out, in_, col, idx=idx), "V": a_ts(out, in_, col, OP.mult, idx=idx)}, [in_, col] + lst(idx), [out], free)
 
-    def lin(out, in_, s, b=0.0):
-        do({"V": a_ts(out, in_, s, OP.mult, b, OP.add), "S": a_act(out, in_, s, b)}, [in_] + sca(s) + sca(b), [out])
+    def lin(out, in_, s, b=0.0, idx=None):
+        do({"V": a_ts(out, in_, s, OP.mult, b, OP.add, idx), "S": a_act(out, in_, s, b, idx=idx)}, [in_] + sca(s) + sca(b) + lst(idx), [out])
 
     def step(out, idx):
-        do({"S": a_act(out, xw, 0.0625, -C23 - 2048.0, idx=idx), "V": a_ts(out, xw, 0.0625, OP.mult, -C23 - 2048.0, OP.add, idx=idx)},
-           [xw, idx], [out])
+        lin(out, xw, 1.0, -2048.0, idx)
+
+    def states(out, in_, idx=None):
+        lin(out, in_, 1.0, 2048.0, idx)
 
     def mms(out, pairs, parts=1):
         n = len(pairs)
@@ -229,8 +228,11 @@ def rank_program(g, core, T, topo):
         do({"G": (lambda e: e.affine_select(ap(out), ap(in_), pattern, op, float(fill), base, cm), (0.17, 2 * out[4], 0, 0, 0, 0, 0), None)},
            [in_], [out])
 
-    def const(v, c=0):
-        do({"G": a_iota(v, [[0, v[4]]], c), "V": a_fill(v, c)}, [], [v])
+    def const(v, c=0, early=False):
+        alt = {"G": a_iota(v, [[0, v[4]]], c)}
+        if early:
+            alt["V"] = a_fill(v, c)
+        do(alt, [], [v])
 
     nrk = len(T.cores)
     sent = [0]
@@ -252,12 +254,11 @@ def rank_program(g, core, T, topo):
     for h in range(NCH):
         b = a + CWS[h]
         last = [do({"Y": a_dma([(T.mti[:, a:b], T.mt[:, a:b])], "dmt%d" % h, 5.2 * CWS[h] / 4096)}, [], [view("mti", a, b)], after=last)]
-        ts(view("xw", a, b), view("mti", a, b), -7.5, OP.add, C27, OP.add)
+        x, v = view("xw", a, b), view("mti", a, b)
+        do({"S": a_act(x, v, 0.0625, -0.46875), "V": a_ts(x, v, 4, OP.arith_shift_right)}, [v], [x])
         a = b
     for a in range(0, 4096, 512):
-        bank = view(psum(), 0, 512)
-        act(bank, view("xw", a, a + 512), bias=-C27)
-        tt(view("ow", a, a + 512), view("mti", a, a + 512), bank, OP.subtract)
+        ts(view("ow", a, a + 512), view("mti", a, a + 512), 15, OP.bitwise_and)
 
     def ix(k):
         return view("ix", k, k + 1)
@@ -266,17 +267,19 @@ def rank_program(g, core, T, topo):
     iota(view("pi", 1, 2), [[0, 1]], 0, 2)
     ts(view("pi", 4, 6), view("pi", 0, 2), 15, OP.bitwise_and)
     ts(view("pi", 6, 8), view("pi", 0, 2), 4, OP.arith_shift_right)
-    cp(view("ix", 0, 4), view("pi", 4, 8))
+    move(view("ix", 0, 4), view("pi", 4, 8))
     iota(view("qg"), [[1, 8], [0, 16]])
     iota(view("ee"), [[1, 17], [0, 16]])
     iota(view("cc"), [[0, 17], [16, 16]], 1, 1)
     iota(view("io640"), [[1, 640]])
+    const(view("one"), 1, True)
+    select(view("i128"), view("one"), [[-1, 128]], OP.is_equal, 0, 0, 1)
     ts(view("blk"), view("qg"), G_, OP.is_equal)
     ts(view("ee"), view("ee"), A_, OP.is_equal)
     iota(view("eye"), [[1, 16]])
     ts(view("eye"), view("eye"), A_, OP.is_equal)
     lin(G16, G_, 16.0, 1.0)
-    const(view("zj"))
+    const(view("zj"), 0, True)
     ts(view("zj", 15, 143, 16), view("qg", 0, 128, 16), G_, OP.is_equal)
     ts(view("b8f"), view("qg", 0, 128, 16), G_, OP.is_equal, -2048.0, OP.mult)
 
@@ -284,7 +287,9 @@ def rank_program(g, core, T, topo):
         return view("zj", 15 - i, 143 - i)
 
     def sel(kind, s, i):
-        c = WSET * (3 * s + kind)
+        if kind == s == 0:
+            return view("ex0", 128 * i, 128 * i + 128)
+        c = WSET * SETS.index((kind, s))
         return view("sel", c + i, c + 2048, 16)
 
     def whole(k0, k1=None):
@@ -293,34 +298,49 @@ def rank_program(g, core, T, topo):
     do({"V": a_fill(first, 0)}, [], [first])
     for a in range(WSET // 4, 3 * WSET, WSET // 4):
         v = view("sel", a, a + WSET // 4)
-        do({"V": a_fill(v, 0), "S": a_act(v, first)}, [first], [v])
-    for a in range(9 * WSET, 12 * WSET, WSET // 4):
-        iota(view("sel", a, a + WSET // 4), [[0, WSET // 4]])
+        do({"V": a_fill(v, 0), "S": a_act(v, first), "G": a_iota(v, [[0, v[4]]])}, [first], [v])
+    for a in range(10 * WSET, 11 * WSET, WSET // 4):
+        const(view("sel", a, a + WSET // 4), 0, True)
     for s in range(4):
-        const(view("cmp", WCMP * (3 * s + 1), WCMP * (3 * s + 3)))
-    cp(view("inu"), view("inl", 0, 48))
-    ts(view("code", 0, 4), view("inl", 0, 16, 4), 16.0, OP.mult, G16, OP.add)
+        c = WCMP * SETS.index((1, s))
+        const(view("cmp", c, c + 2 * WCMP), 0, s < 2)
+    move(view("inu"), view("inl", 0, 48))
+    lin(view("code", 0, 4), view("inl", 0, 16, 4), 16.0, G16)
     tt(view("code", 4, 8), view("code", 0, 4), view("inl", 1, 16, 4), OP.add)
 
     def wave(n, k0, k1):
         last[0] = do({"Y": a_dma([(T.sel[16 * k:16 * k + 16, k0:k1, 256 * k:256 * k + WCMP], T.cmp[16 * k:16 * k + 16, WCMP * k0:WCMP * k1])
                                   for k in range(8)], "wave%d" % n, 0.15 * (k1 - k0))},
                      [view("cmp", WCMP * k0, WCMP * k1)], whole(k0, k1), after=last)
+
+    def zeros(*sets):
+        for k in sets:
+            do({"Y": a_dma([(T.sel[:, k, :], T.sel[:, 10, :])], "dz%d" % k, 1.32)}, whole(10), whole(k), after=last)
     for s in range(4):
-        c = 3 * WCMP * s
-        for k in range(3 * s, 3 * s + 3) if s in (1, 2) else ():
-            do({"Y": a_dma([(T.sel[:, k, :], T.sel[:, 11, :])], "dz%d" % k, 1.32)}, whole(11), whole(k), after=last)
-        scale(view("cb", 128 * s, 128 * s + 128), view("blk"), view("code", 4 + s, 5 + s))
-        bank = view(psum(), 0, WCMP)
-        mms(bank, [(view("cb", 128 * s, 128 * s + 128), view("ee"))])
-        tt(view("cmp", c, c + WCMP), bank, view("cc"), OP.is_equal)
-        move(view("cmp", c + WCMP, c + 3 * WCMP, 17), view("eye"), idx=view("inu", 4 * s + 2, 4 * s + 4))
-        if s != 2:
-            wave(min(s, 2), 3 * min(s, 2), 3 * s + 3)
+        cb, d = view("cb", 128 * s, 128 * s + 128), WCMP * SETS.index((1, s))
+        scale(cb, view("blk"), view("code", 4 + s, 5 + s))
+        if s:
+            bank, c = view(psum(), 0, WCMP), WCMP * SETS.index((0, s))
+            mms(bank, [(cb, view("ee"))])
+            tt(view("cmp", c, c + WCMP), bank, view("cc"), OP.is_equal)
+        else:
+            bank = view(psum(), 0, 128)
+            mms(bank, [(cb, view("i128"))])
+            move(view("row"), bank)
+            for a in range(16):
+                ts(sel(0, 0, a), view("row"), view("cc", a, a + 1), OP.is_equal)
+        move(view("cmp", d, d + 2 * WCMP, 17), view("eye"), idx=view("inu", 4 * s + 2, 4 * s + 4))
+    zeros(3, 4)
+    wave(0, 0, 3)
+    wave(1, 3, 5)
+    zeros(5, 6)
+    wave(2, 5, 7)
+    zeros(7, 8, 9)
+    wave(3, 7, 11)
 
     move(view("lm"), view("eye"), idx=view("inu", 24, 48))
-    ts(view("qsf", 8, 24), view("inl", 56, 72), 1.0 / 16384, OP.mult)
-    cp(view("wdb"), view("inl", 0, 16))
+    lin(view("qsf", 8, 24), view("inl", 56, 72), 1.0 / 16384)
+    move(view("wdb"), view("inl", 0, 16))
     for a in range(512, 1024, 256):
         const(view("res", a, a + 256), -1)
     for a in range(128, 640, 256):
@@ -331,7 +351,6 @@ def rank_program(g, core, T, topo):
     const(view("neg1"), -1)
     const(view("z8"))
     const(view("zb"))
-    const(view("one"), 1)
     const(view("b16"), 16)
     const(view("cap", 32, 36), 16)
     const(view("w16", 0, 512))
@@ -340,7 +359,6 @@ def rank_program(g, core, T, topo):
     iota(view("c24"), [[16, 24]], 128)
     iota(view("c15"), [[-1, 16]], 15)
     iota(view("d15"), [[0, 8], [-1, 16]], 15)
-    select(view("i128"), view("one"), [[-1, 128]], OP.is_equal, 0, 0, 1)
     select(view("d15"), view("d15"), [[-1, 128]], OP.is_equal, 0, 0, 1)
     select(view("low"), view("d15"), [[-16, 8], [0, 16]], OP.is_ge, -256, 0, 1)
     select(view("low"), view("low"), [[16, 8], [0, 16]], OP.is_ge, -256, 15, -1)
@@ -354,6 +372,9 @@ def rank_program(g, core, T, topo):
     ts(view("blkpp"), view("pg"), PG2, OP.is_equal)
     ts(view("blkp"), view("qg"), 2.0, OP.mult, PG2, OP.is_equal)
     select(view("tlo"), view("blkp"), [[1, 8], [8, 16]], OP.is_gt, 0, 0, -1)
+    iota(view("cst"), [[16, 16], [0, 8]], 1, 1)
+    select(view("cst"), view("cst"), [[0, 16], [-16, 8]], OP.is_ge, -1, 0, 1)
+    select(view("cst"), view("cst"), [[0, 16], [16, 8]], OP.is_ge, -1, 15, -1)
     lin(A15, A_, -1.0, 15.0)
     lin(A32, A_, 32.0)
     lin(view("k32"), view("io640", 0, 32), 1.0, A32)
@@ -375,58 +396,57 @@ def rank_program(g, core, T, topo):
 
     def lookup(t, cnt):
         if t == 0:
-            ts(view("ki"), view("inl", 48, 56), 1.0 / 128, OP.mult, -EPS, OP.add)
+            ts(view("kl"), view("inl", 48, 56), 1.0 / 128, OP.mult, -EPS, OP.add)
         else:
-            ts(view("ki"), view("qsf", 8 * t, 8 * t + 8), cnt, OP.mult, -EPS, OP.add)
-        cp(view("kl"), view("ki"))
-        if t:
+            ts(view("kl"), view("qsf", 8 * t, 8 * t + 8), cnt, OP.mult, -EPS, OP.add)
             scatter(view("xk"), pl(t - 1), view("xi", 128 * t - 128, 128 * t))
         tt(view("qgt"), view("xk") if t else view("xk", 0, 128), view("lm", 128 * t, 128 * t + 128), OP.mult, idx=view("kl"))
         bank = view(psum(), 0, 8)
         mms(bank, [(jj(i), view("qgt", i, 128, 16)) for i in range(16)])
-        ts(view("ql"), bank, 2048.0, OP.add)
+        states(view("ql"), bank)
 
     def pass12(b):
         lst_ = view("inu", 16, 24) if b == 0 else view("ql")
-        ts(view("xl", 128 * b, 128 * b + 128), xw, 0.0625, OP.mult, -C23, OP.add, idx=lst_)
+        move(view("xl", 128 * b, 128 * b + 128), xw, lst_)
         if b < 3:
             step(view("xk", 0, 128) if b == 0 else view("xi", 128 * b - 128, 128 * b), lst_)
-        for h in (0, 1):
-            c = 2048 * b + 1024 * h
-            step(view("yy", c, c + 1024), view("xl", 128 * b + 64 * h, 128 * b + 64 * h + 64))
+        for a in range(128 * b, 128 * b + 128, WIDE):
+            step(view("yy", 16 * a, 16 * (a + WIDE)), view("xl", a, a + WIDE))
 
     def psel_x(b):
         out = fresh("ls", 128)
         for h in (0, 1):
             bank, c = view(psum(), 0, 64), 2048 * b + 1024 * h
             mms(bank, [(sel(0, 0, a), view("yy", c + a, c + 1024, 16)) for a in range(16)])
-            ts(view("ls", out + 64 * h, out + 64 * h + 64), bank, 2048.0, OP.add)
+            states(view("ls", out + 64 * h, out + 64 * h + 64), bank)
         return out
 
-    def psel_z(b, z):
-        bank = view(psum(), 0, 128)
+    def psel_z(b, z, buf=None, walks=False):
+        bank, out = view(psum(), 0, 128), None
         mms(bank, [(sel(0, 1 + z, a), view("yy", 2048 * b + a, 2048 * b + 2048, 16)) for a in range(16)], PARTS)
-        move(view("pz%d" % z, 128 * b, 128 * b + 128), bank)
-
-    def zlist(z, c, idx=None):
-        out = fresh("ls", 128)
-        ts(view("ls", out, out + 128), view("pz%d" % z, 0 if idx else c, c + 128), 2048.0, OP.add, idx=idx)
+        if walks:
+            out = fresh("ls", 128)
+            states(view("ls", out, out + 128), bank)
+        if buf:
+            move(view(buf, 128 * b, 128 * b + 128), bank)
         return out
 
-    def p3(s, src, w):
-        out, gb = fresh("ls", 128), fresh("gb", 2048)
+    def matched(t):
+        out = fresh("ls", 128)
+        states(view("ls", out, out + 128), view("pz%d" % t, 0, 128 * t + 256), view("ml"))
+        return out
+
+    def walk(s, src, w):
+        mid, gb = fresh("ls", 128), fresh("gb", 2048)
         for h in (0, 1):
             bank, c = view(psum(), 0, 64), gb + 1024 * h
             for a in range(0, 64, w):
                 step(view("gb", c + 16 * a, c + 16 * (a + w)), view("ls", src + 64 * h + a, src + 64 * h + a + w))
             mms(bank, [(sel(1, s, e), view("gb", c + e, c + 1024, 16)) for e in range(16)])
-            ts(view("ls", out + 64 * h, out + 64 * h + 64), bank, 2048.0, OP.add)
-        return out
-
-    def walk(s, src, w):
-        src, gb = p3(s, src, w), fresh("gb", 2048)
+            states(view("ls", mid + 64 * h, mid + 64 * h + 64), bank)
+        gb = fresh("gb", 2048)
         for a in range(0, 128, w):
-            move(view("gb", gb + 16 * a, gb + 16 * (a + w)), ow, idx=view("ls", src + a, src + a + w))
+            move(view("gb", gb + 16 * a, gb + 16 * (a + w)), ow, idx=view("ls", mid + a, mid + a + w))
         return gb
 
     def p4s(gb, out, c0, s, t=-1):
@@ -437,13 +457,13 @@ def rank_program(g, core, T, topo):
             move(view(out, o, o + 64), bank)
 
     def p4z(s, gb):
-        bank, c = psum(), WSET * (3 * s + 2)
+        bank, c = psum(), WSET * SETS.index((2, s))
 
         def fn(e):
             for k in range(16):
                 r = e.matmul(ap(view(bank, k, 128, 16)), ap(view("gb", gb + k, gb + 2048, 16)), ap(view("sel", c + 17 * k, c + 2048, 256)), True, True)
             return r
-        do({"P": (fn, (0, 0, 0, 0, 16 * 64, 0, 0), None)}, [view("gb", gb, gb + 2048)] + whole(3 * s + 2), [view(bank, 0, 128)])
+        do({"P": (fn, (0, 0, 0, 0, 16 * 64, 0, 0), None)}, [view("gb", gb, gb + 2048)] + whole(c // WSET), [view(bank, 0, 128)])
         return view(bank, 0, 128)
 
     def compare(t):
@@ -477,7 +497,7 @@ def rank_program(g, core, T, topo):
             mms(view(bank, 9, 10), [(view("blkpp"), tot)])
         mb = view(psum(), 0, 8)
         mms(mb, [(view("pmx"), view("mn"))])
-        cp(pl(t), view(bank, 0, 8))
+        move(pl(t), view(bank, 0, 8))
         if t < 2:
             lookup(t + 1, cnt)
             move(view("cnt", t + 1, t + 2), cnt)
@@ -485,7 +505,7 @@ def rank_program(g, core, T, topo):
         else:
             ts(view("cap", 0, 32), view("k32"), cnt, OP.is_lt)
             lin(view("cap", 0, 32), view("cap", 0, 32), 17.0, -1.0)
-        ts(view("ml"), mb, float(L), OP.add)
+        lin(view("ml"), mb, 1.0, float(L))
         move(view("num", L, L + 128), view("io640"), idx=pl(t))
         move(view("res", 128 * t, 128 * t + 128), view("num", 0, L + 128), idx=view("ml"))
         if t < 2:
@@ -509,36 +529,31 @@ def rank_program(g, core, T, topo):
             reduce(dc, view("ne"), OP.add)
             ts(view("dd2"), view("eye"), dc, OP.mult, 16.0, OP.mult)
             mms(view(bank, 0, 16), [(view("blk"), view("dd2")), (view("i128"), view("c15"))])
-            ts(sc, dc, 16.0, OP.mult, A15, OP.add)
+            lin(sc, dc, 16.0, A15)
             reduce(mx, view(bank, 0, 16), OP.max)
         oh, ws, bank = view("oh", t, t + 1), view("ws", 4 * t, 4 * t + 4), psum()
         ts(oh, sc, mx, OP.is_equal)
         scale(ws, view("wdb", 4 * t + 4, 4 * t + 8), oh)
         mms(view(bank, 0, 4), [(view("blk"), ws)])
-        ts(view("mk", 8 + t, 9 + t), view(bank, 2, 3), A_, OP.is_equal, 0.0625, OP.mult)
-        ts(view("mk", t, t + 1), view(bank, 3, 4), A_, OP.is_equal)
-        lin(view("mk", 12 + t, 13 + t), view("mk", 8 + t, 9 + t), -C27 - 32768.0)
+        ts(view("mk", 4 * t, 4 * t + 2), view(bank, 2, 4), A_, OP.is_equal)
+        ts(view("mk", 4 * t + 2, 4 * t + 3), view(bank, 2, 3), A_, OP.is_equal, -2048.0, OP.mult)
+        scale(view("zo"), view("zj"), oh)
         if t == 0:
             ts(view("mk", 15, 16), view(bank, 0, 1), 16.0, OP.mult, view(bank, 1, 2), OP.add)
-            ts(view("cmp", WCMP, 3 * WCMP, WCMP), view(bank, 2, 4), A_, OP.is_equal)
-            ts(view("cmp", 0, 16), view("cc", 0, 16), G16, OP.subtract, view("mk", 15, 16), OP.is_equal)
 
-    def wpass(t, c0, c1, src):
+    def wpass(t, c0, c1):
         n = (c1 - c0) // 16
         h = (c1 - c0) // (2 if n > 16 else 1)
-        for a in range(c0, c1, h):
-            scale(view("pw", a, a + h), view(src, a, a + h), view("oh", t, t + 1))
         bank, bank2 = view(psum(), 0, n), view(psum(), 0, n)
-        mms(bank, [(jj(i), view("pw", c0 + i, c1, 16)) for i in range(16)])
-        ts(view("lw", 0, n), bank, 2048.0, OP.add)
-        m16, mb = view("mk", 8 + t, 9 + t), view("mk", 12 + t, 13 + t)
+        mms(bank, [(view("zo", 15 - i, 143 - i), view("pw%d" % t, c0 + i, c1, 16)) for i in range(16)])
+        states(view("lw", 0, n), bank)
+        mk, mb = view("mk", 4 * t, 4 * t + 1), view("mk", 4 * t + 2, 4 * t + 3)
         for a in range(0, c1 - c0, h):
-            o, li = view("gw", a, a + h), view("lw", a // 16, (a + h) // 16)
-            do({"S": a_act(o, xw, m16, mb, idx=li), "V": a_ts(o, xw, -C27 - 32768.0, OP.add, m16, OP.mult, idx=li)}, [xw, m16, mb, li], [o])
+            lin(view("gw", a, a + h), xw, mk, mb, view("lw", a // 16, (a + h) // 16))
         mms(bank2, [(jj(i), view("gw", i, c1 - c0, 16)) for i in range(16)])
-        ts(view("lw2", 0, n), bank2, 2048.0, OP.add)
+        states(view("lw2", 0, n), bank2)
         for a in range(0, c1 - c0, h):
-            scale(view("gz%d" % t, c0 + a, c0 + a + h), ow, view("mk", t, t + 1), idx=view("lw2", a // 16, (a + h) // 16))
+            scale(view("gz%d" % t, c0 + a, c0 + a + h), ow, view("mk", 4 * t + 1, 4 * t + 2), idx=view("lw2", a // 16, (a + h) // 16))
 
     def rupdate(t):
         L = 128 * (t + 2)
@@ -551,41 +566,47 @@ def rank_program(g, core, T, topo):
     pass12(1)
     for b in (0, 1):
         p4s(walk(0, psel_x(b), WIDE), "rr", 128 * b, 0)
-    for z in range(3):
+    for z in (1, 2):
         for b in (0, 1):
-            psel_z(b, z)
+            psel_z(b, z, "pz%d" % z)
     compare(0)
     for b in (1, 0):
-        p4s(walk(1, zlist(0, 128 * b), FINE), "an", 128 * b, 1)
+        p4s(walk(1, psel_z(b, 0, None, True), FINE), "an", 128 * b, 1)
     move(view("aq"), view("an", 128, 256))
     for t in range(3):
         b = t + 2
         append(t)
         if t:
-            tt(view("ne"), p4z(1 + t, walk(1 + t, zlist(t, 128 * (t + 1), view("ml")), FINE)), view("aq"), OP.not_equal)
+            tt(view("ne"), p4z(1 + t, walk(1 + t, matched(t), FINE)), view("aq"), OP.not_equal)
         else:
             tt(view("ne"), view("an"), view("aq"), OP.not_equal, idx=view("ml"))
         winner(t)
         if t == 2:
             break
         pass12(b)
-        gs = walk(0, psel_x(b), WIDE)
-        for z in range(t, 3):
-            psel_z(b, z)
+        gs = walk(0, psel_x(b), FINE)
+        psel_z(b, t, "pw%d" % t)
+        zs = psel_z(b, t + 1, "pz%d" % (t + 1), True)
         if t == 0:
+            psel_z(b, 2, "pz2")
             scale(view("gz0", 0, 256), view("an"), view("oh", 0, 1))
-            wpass(0, 256, 384, "pz0")
+            wpass(0, 256, 384)
         else:
-            wpass(1, 0, 512, "pz1")
+            move(view("pw1", 0, 384), view("pz1"))
+            wpass(1, 0, 512)
         rupdate(t)
         p4s(gs, "rr", 128 * b, 0, t)
         if t == 0:
-            wave(3, 0, 3)
+            ts(view("ex0", 0, 2048, 16), view("cst"), G16, OP.subtract, view("mk", 15, 16), OP.is_equal)
+            for k in (0, 1):
+                scale(view("sel", WSET * k, WSET * k + 2048, 256), view("zj", 15, 143, 16), view("mk", k, k + 1))
         compare(t + 1)
-        move(view("aq"), p4z(2 + t, walk(2 + t, zlist(t + 1, 128 * b), FINE)))
+        move(view("aq"), p4z(2 + t, walk(2 + t, zs, FINE)))
     in_order(view("pzn"), "pz2")
     in_order(view("res", 384, 1024), "rr")
-    wpass(2, 0, 512, "pzn")
+    for a in (0, 256):
+        move(view("pw2", a, a + 256), view("pzn", a, a + 256))
+    wpass(2, 0, 512)
 
     send(learner, view("resl"), view("res", 0, 896), "ares", 1.2, 2)
     bank = psum()
@@ -594,9 +615,9 @@ def rank_program(g, core, T, topo):
     tt(view("fin"), view(bank, 0, 36), view("cap"), OP.min)
     send(learner, view("finl"), view("fin"), "afin", 0.1, 2)
     do({"Y": a_dma([(T.ym[:], T.resl[::16, 0:384])], "dym", 0.1)}, [view("resl")], [])
-    i = do({"Y": a_dma([(T.yr[:], T.resl[:, 384:896])], "dyr", 0.7)}, [view("resl")], [])
-    j = do({"Y": a_dma([(T.yr[2::16, :], T.finl[:, 0:32])], "dy2", 0.1)}, [view("finl")], [])
-    ops[j]["deps"].add(i)
+    rows = [(max(0, a - 13), min(128, a + 2)) for a in range(0, 144, 16)]
+    do({"Y": a_dma([(T.yr[a:b, :], T.resl[a:b, 384:896]) for a, b in rows], "dyr", 0.7)}, [view("resl")], [])
+    do({"Y": a_dma([(T.yr[2::16, :], T.finl[:, 0:32])], "dy2", 0.1)}, [view("finl")], [])
     do({"S": a_dma([(T.ye[:], T.finl[:, 32:36])], "dye", 0.1)}, [view("finl")], [])
 
     if "p" not in PLAN:
@@ -622,8 +643,8 @@ def rank_program(g, core, T, topo):
             pos[q] += 1
             r.then_inc(T.sem[CSEM[q]], 1)
             tok[i] = (CSEM[q], pos[q])
-    for s in ("dym", "dy2", "dye"):
-        g.sync.wait_ge(T.sem[s], 16)
+    for s, n in (("dym", 1), ("dyr", len(rows)), ("dy2", 1), ("dye", 1)):
+        g.sync.wait_ge(T.sem[s], 16 * n)
     g.wait_ge(T.sem.sent, sent[0])
     for q in sorted(CSEM):
         g.wait_ge(T.sem[CSEM[q]], pos[q])

from concourse.mybir import AluOpType, AxisListType, ActivationFunctionType

OP = AluOpType
AF = ActivationFunctionType
CWS = [512] * 7 + [384, 128]
NCH = len(CWS)
EPS = 0.499969482421875
PARTS = 4
WSET, WCMP = 2064, 272
NBUF = 12
WIDE, FINE = 64, 32
SETS = [(1, 0), (2, 0), (0, 1), (1, 1), (2, 1), (0, 2), (0, 3), (1, 2), (2, 2), (1, 3), (2, 3)]
DIGITS = "0123456789abcdefghijklmnopqrstuvwxyzABCDEFGHIJKLMNOPQRSTUVWXYZ"
ORDER = "1s032k22001R1K3a2F092Y1p0f2V0l1v6o2o370r2D1y2R1E2J1C2t2x2M252z0c0i117m7C0o0u0x140D2b282e0J1W6r067q1H2h3377175X1a1Z0A1d0G0M7v1g30661T3m1j3o7W1N3s0P0V3i5A0S4q3u0Z4s4O2Q5w522s7K3y6l7N4v3G4j3S414C4Z3D4m7Z6P827a553P4g445R3J3V3M7z3A4y4a474E7R4d3Y867t887T586x4Q8h3f8k6J8q8cdg8f8u968o9c8G9a1m8wcfci4Hclco8I6f9g9r9jdj8Mcs8z5b6Admdp9l8C694T8P717d7g8R6M9u909x9p9Bcy6D8Ucv5e9DcA5hcD7F5qcG5U9G9M8X5F9S94cKcM9K4X6icT9Pb9b6dtblbfaTbcbobi5naWbr63dyaZaQdwbRcQc3bzd2cVb3bt9V9YbU60bwbLc6dBc9bO6ubCcc7HbFbXc03cbI74ekcYdLd4dad8eqewetdEezeCdIdTa7aaad4LendNeJeL5OeFeOdR5DeReUdXam6ceXdee5f7dZa1fWeig1ape2e9ebef6Y6Sg5f9f1agfiflg7gafogmfvgd5k5tfrfxgggkfAgvgTgWgZh2f3gpgzh6fDgtfQffh8gBfGa47jgIfJhIgKgFhbhehhfMhMhGgNhOhlhRgRhVi0hXjRasjThn5LfZicifk5i6iafSjWi3iuiW6GiQaBiriNixfciHiZj2iTiKja6Vii5IjgakjsiAk0iDjmjdjjk3jvjpjEjyjHo6jBj4kejKj7k8jNkbkzaEaHkRkwavkokhkCljlvkFlAlMkIilkLlykOaKlDkUkXl0lGl3lKlPkklSl6lVlZl9hqhthwaOmFm1azmHm4hzmLkqkum7sImalmlomNmdhCmgmTmQmjnznCmZmWn3mmipmpnFmBnInLsKnbn5n8msmvo9mynfnhlrodlcnOogoinknroloonRnnnwovnUnXoDoro1nuqioxqeoHoJoNoAlfoSpqphpnoPpep8pkqkpbp5oVsNquoYqnpKpNpEq2pHpWq8p2pyq5pZqCpsqrqFqbpBpvpQpTqwqAqXqUqIo4rcrorxr0r3r6r9rErArQrGrMrJrSrgqLrZs1rVsUs8s4sQrrsWqOqRsasdrusZt5sgsjsmrispt8sFssrmt2svsytztbsBtCtftlthtntqtwtutFtItLtOtRtUtX"

F, B, H, I, U = "float32", "bfloat16", "float16", "int32", "uint16"
SCRATCH = {}
for _n, _w, _d in [
        ("mti", 4096, I), ("xw", 4096, I), ("ow", 4096, I), ("inp", 72, I), ("inl", 72, I), ("inu", 48, U),
        ("res", 1024, F), ("resl", 896, F), ("fin", 36, F), ("finl", 36, F), ("cap", 36, F),
        ("pi", 8, I), ("ix", 24, F), ("qg", 128, B), ("pg", 128, B), ("io640", 640, F), ("c24", 24, F), ("cc", WCMP, F), ("ee", WCMP, B),
        ("one", 128, B), ("blk", 128, B), ("eye", 16, B), ("i128", 128, B), ("zj", 144, B), ("blkp", 128, B), ("tlo", 128, B),
        ("pmx", 128, B), ("blkpp", 128, B), ("blki", 128, B), ("b16", 128, B), ("d15", 128, B), ("low", 128, B), ("zb", 248, B),
        ("b8f", 8, F), ("keep", 384, B), ("nlneg", 8, H), ("own", 24, F), ("cnp", 8, F), ("neg1", 384, F), ("z8", 8, F), ("c15", 16, B),
        ("k32", 32, F), ("w16", 640, B), ("wdb", 16, B), ("code", 8, F), ("cb", 512, H), ("cmp", 11 * WCMP, B),
        ("ex0", 2048, B), ("row", 128, H), ("cst", 128, F),
        ("lm", 384, B), ("qsf", 24, F), ("kl", 8, U), ("qgt", 128, H), ("ql", 8, U), ("xi", 256, F),
        ("xl", 512, U), ("xk", 640, F), ("yy", 8192, H), ("gb", 2048 * NBUF, H), ("ls", 128 * 20, U),
        ("pw0", 384, H), ("pw1", 512, H), ("pw2", 512, H), ("zo", 144, B), ("pz1", 384, F), ("pz2", 512, F), ("pzn", 640, F),
        ("rr", 512, B), ("an", 256, B), ("r2", 384, B), ("rq2", 128, B), ("lhb", 1024, B),
        ("sc", 3072, F), ("nn", 8, F), ("top", 8, F), ("uu", 8, H), ("inc", 10, H), ("ww", 8, H), ("mn", 8, H), ("ml", 8, U),
        ("cnt", 4, H), ("pl", 24, U), ("num", 512, F), ("aq", 128, B), ("ne", 128, B), ("sm", 8, F), ("dd2", 16, B),
        ("oh", 4, F), ("ws", 12, B), ("mk", 16, F), ("lw", 32, U), ("gw", 512, H), ("lw2", 32, U),
        ("gz0", 384, B), ("gz1", 512, B), ("gz2", 512, B)]:
    SCRATCH[_n] = ("sbuf", [128, _w], _d)
SCRATCH["sel"] = ("sbuf", [128, len(SETS), WSET], B)
BANKS = ["bank%d" % _k for _k in range(8)]
for _n in BANKS:
    SCRATCH[_n] = ("psum", [128, 512], F)
SEMAPHORES = (["cv", "cs", "cp", "cg", "sent", "din", "din2", "ain", "ares", "afin", "dym", "dyr", "dy2", "dye"]
              + ["dmt%d" % h for h in range(NCH)] + ["wave%d" % h for h in range(4)] + ["dz%d" % h for h in range(len(SETS))])
CSEM = {"V": "cv", "S": "cs", "P": "cp", "G": "cg"}
PLAN = {}


def plan(ops):
    code = [62 * DIGITS.index(ORDER[k]) + DIGITS.index(ORDER[k + 1]) for k in range(0, len(ORDER), 2)]
    if len(code) != len(ops):
        code = [3 * i for i in range(len(ops))]
    order = [(x // 3, list(ops[x // 3]["alt"])[x % 3]) for x in code]
    users, bank_of, extra = {}, {}, {}
    for i, o in enumerate(ops):
        users.setdefault(o["ps"], []).append(i)
    togo, held, through = [0] * 8, [None] * 8, [0] * 8
    for n, (i, q) in enumerate(order):
        v = ops[i]["ps"]
        if v is not None:
            if v not in bank_of:
                k = min([k for k in range(8) if not togo[k]], key=lambda k: through[k])
                extra[i] = users[held[k]] if held[k] else []
                held[k], bank_of[v], togo[k] = v, k, len(users[v])
            togo[bank_of[v]] -= 1
            through[bank_of[v]] = n
    return order, bank_of, extra


def rank_program(g, core, T, topo):
    rank = T.rank_of(core)
    if rank is None:
        return
    queue = {"V": g.vector, "S": g.scalar, "P": g.tensor, "G": g, "Y": g.sync}
    ops = []
    wrote, readers = {}, {}
    nps = [0]

    def view(name, c0=0, c1=None, st=1):
        if c1 is None:
            c1 = SCRATCH[name][1][1]
        return (name, c0, c1, st, (c1 - c0 + st - 1) // st)

    def psum():
        nps[0] += 1
        return "#%d" % nps[0]

    def inps(v):
        return v[0][0] == "#"

    def ap(v):
        if v[0] == "sel":
            k = v[1] // WSET
            return T.sel[:, k, v[1] - k * WSET:v[2] - k * WSET:v[3]]
        t = T[BANKS[PLAN["p"][1][v[0]]]] if inps(v) else T[v[0]]
        return t[:, v[1]:v[2]] if v[3] == 1 else t[:, v[1]:v[2]:v[3]]

    def do(alt, reads, writes, free=False, after=()):
        i = len(ops)
        deps, soft = set(), set(after)
        for v in reads:
            for (a, b, j) in wrote.get(v[0], []):
                if a < v[2] and v[1] < b:
                    deps.add(j)
                elif inps(v):
                    soft.add(j)
            if inps(v):
                soft.update(j for (a, b, j) in readers.get(v[0], []))
        for v in writes:
            for (a, b, j) in wrote.get(v[0], []):
                if inps(v):
                    soft.add(j)
                elif a < v[2] and v[1] < b and not (free and ops[j]["free"]):
                    deps.add(j)
            for (a, b, j) in readers.get(v[0], []):
                if a < v[2] and v[1] < b:
                    deps.add(j)
                elif inps(v):
                    soft.add(j)
        ps = [v[0] for v in list(reads) + list(writes) if inps(v)]
        ops.append({"alt": alt, "deps": deps, "soft": soft - deps, "free": free, "ps": ps[0] if ps else None,
                    "nm": writes[0][:2] if writes else ("-", 0)})
        for v in writes:
            if not free:
                for d in (wrote, readers):
                    d[v[0]] = [r for r in d.get(v[0], []) if not (v[1] <= r[0] and r[1] <= v[2])]
            wrote.setdefault(v[0], []).append((v[1], v[2], i))
        for v in reads:
            readers.setdefault(v[0], []).append((v[1], v[2], i))
        return i

    def a_dma(pairs, sem, us):
        def fn(e):
            for o, i in pairs:
                e.dma_start(o, i).then_inc(T.sem[sem], 16)
        return (fn, (0.08 * len(pairs), 0, 0, 0, 0, us, 1), (sem, 16 * len(pairs)))

    def sca(s):
        return [s] if isinstance(s, tuple) else []

    def val(s):
        return ap(s) if isinstance(s, tuple) else s

    def two(*vs):
        return all(not inps(v) and SCRATCH[v[0]][2] in (B, H, U) for v in vs)

    def dv(n, half=False):
        return (0.03, max(64, n * (0.5 if half else 1.0)), 0, 0, 0, 0, 0)

    def dg(n):
        return (0.05, 0, n, 0, 0, 0, 0)

    def ind(v, idx):
        return ap(v) if idx is None else ap(v).indirect(ap(idx))

    def lst(idx):
        return [] if idx is None else [idx]

    def a_ts(out, in0, s1, op0, s2=None, op1=None, idx=None):
        w = dv(out[4], two(out, in0)) if idx is None else dg(out[4])
        if op1 is None:
            return (lambda e: e.tensor_scalar(ap(out), ind(in0, idx), val(s1), None, op0), w, None)
        return (lambda e: e.tensor_scalar(ap(out), ind(in0, idx), val(s1), val(s2), op0, op1), w, None)

    def a_act(out, in_, scale=1.0, bias=0.0, func=AF.Identity, idx=None):
        return (lambda e: e.activation(ap(out), ind(in_, idx), func, bias=val(bias), scale=val(scale)),
                (0.065, 0, out[4], 0, 0, 0, 0) if idx else (0.065, out[4], 0, 0, 0, 0, 0), None)

    def a_cp(out, in_, idx=None):
        return (lambda e: e.tensor_copy(ap(out), ind(in_, idx)), dv(out[4], two(out, in_)) if idx is None else dg(out[4]), None)

    def a_iota(out, pattern, base=0, cm=0):
        if SCRATCH[out[0]][2] == I:
            fn = lambda e: e.iota(ap(out), pattern, base, cm)
        else:
            fn = lambda e: e.iota(ap(out), pattern, base, cm, allow_small_or_imprecise_dtypes=True)
        return (fn, (0.13, 2 * out[4], 0, 0, 0, 0, 0), None)

    def a_fill(v, c):
        return (lambda e: e.memset(ap(v), float(c)), dv(v[4], two(v)), None)

    def ts(out, in0, s1, op0, s2=None, op1=None):
        do({"V": a_ts(out, in0, s1, op0, s2, op1)}, [in0] + sca(s1) + sca(s2), [out])

    def tt(out, in0, in1, op, idx=None):
        w = dg(out[4]) if idx else dv(out[4] * (1 if inps(in0) or inps(in1) else 2))
        do({"V": (lambda e: e.tensor_tensor(ap(out), ind(in0, idx), ap(in1), op), w, None)}, [in0, in1] + lst(idx), [out])

    def scatter(win, idx, in_):
        do({"V": (lambda e: e.tensor_copy(ap(win).indirect(ap(idx)), ap(in_)), (0.05, 0, 0, in_[4], 0, 0, 0), None)}, [in_, idx], [win])

    def scan(out, d0, d1, init, op0, op1):
        do({"V": (lambda e: e.tensor_tensor_scan(ap(out), ap(d0), ap(d1), val(init), op0, op1), dv(out[4]), None)}, [d0, d1] + sca(init), [out])

    def reduce(out, in_, op):
        do({"V": (lambda e: e.tensor_reduce(ap(out), ap(in_), AxisListType.X, op), dv(in_[4]), None)}, [in_], [out])

    def act(out, in_, scale=1.0, bias=0.0, func=AF.Identity):
        do({"S": a_act(out, in_, scale, bias, func)}, [in_] + sca(scale) + sca(bias), [out])

    def move(out, in_, idx=None):
        do({"S": a_act(out, in_, idx=idx), "V": a_cp(out, in_, idx)}, [in_] + lst(idx), [out])

    def scale(out, in_, col, free=False, idx=None):
        do({"S": a_act(out, in_, col, idx=idx), "V": a_ts(out, in_, col, OP.mult, idx=idx)}, [in_, col] + lst(idx), [out], free)

    def lin(out, in_, s, b=0.0, idx=None):
        do({"V": a_ts(out, in_, s, OP.mult, b, OP.add, idx), "S": a_act(out, in_, s, b, idx=idx)}, [in_] + sca(s) + sca(b) + lst(idx), [out])

    def step(out, idx):
        lin(out, xw, 1.0, -2048.0, idx)

    def states(out, in_, idx=None):
        lin(out, in_, 1.0, 2048.0, idx)

    def mms(out, pairs, parts=1):
        n = len(pairs)
        for m in range(parts):
            lo, hi = n * m // parts, n * (m + 1) // parts

            def fn(e, lo=lo, hi=hi):
                for k in range(lo, hi):
                    r = e.matmul(ap(out), ap(pairs[k][0]), ap(pairs[k][1]), k == 0, k == n - 1)
                return r
            do({"P": (fn, (0, 0, 0, 0, (hi - lo) * max(64, out[4]), 0, 0), None)}, [p for pr in pairs[lo:hi] for p in pr], [out])

    def iota(out, pattern, base=0, cm=0):
        do({"G": a_iota(out, pattern, base, cm)}, [], [out])

    def select(out, in_, pattern, op, fill, base, cm):
        do({"G": (lambda e: e.affine_select(ap(out), ap(in_), pattern, op, float(fill), base, cm), (0.17, 2 * out[4], 0, 0, 0, 0, 0), None)},
           [in_], [out])

    def const(v, c=0, early=False):
        alt = {"G": a_iota(v, [[0, v[4]]], c)}
        if early:
            alt["V"] = a_fill(v, c)
        do(alt, [], [v])

    nrk = len(T.cores)
    sent = [0]

    def send(dst, out, v, sem, us, kind, share=1):
        rid, pid, _ = topo.addr(dst)
        eng = topo.engines(core, dst)[::share]
        sent[0] += len(eng)
        do({"G": (lambda e: e.remote_dma(ap(out), ap(v), T.sem[sem], T.sem.sent, pid, rid, sum(1 << k for k in eng)),
                  (0.3, 0, 0, 0, 0, us, kind), (sem, len(eng)))}, [v], [out])
    owner, learner = T.cores[(rank + 1) % nrk], T.cores[(rank - 1) % nrk]

    do({"S": a_dma([(T.inp[:, 0:4], T.ex[:]), (T.inp[:, 4:16], T.zs[:]), (T.inp[:, 48:72], T.qs[:])], "din", 0.1)},
       [], [view("inp", 0, 16), view("inp", 48, 72)])
    last = [do({"Y": a_dma([(T.inp[:, 16:24], T.bk[:]), (T.inp[:, 24:48], T.qc[:])], "din2", 0.1)}, [], [view("inp", 16, 48)])]
    send(owner, view("inl"), view("inp"), "ain", 0.2, 3, 4)
    xw, ow = view("xw"), view("ow")
    a = 0
    for h in range(NCH):
        b = a + CWS[h]
        last = [do({"Y": a_dma([(T.mti[:, a:b], T.mt[:, a:b])], "dmt%d" % h, 5.2 * CWS[h] / 4096)}, [], [view("mti", a, b)], after=last)]
        x, v = view("xw", a, b), view("mti", a, b)
        do({"S": a_act(x, v, 0.0625, -0.46875), "V": a_ts(x, v, 4, OP.arith_shift_right)}, [v], [x])
        a = b
    for a in range(0, 4096, 512):
        ts(view("ow", a, a + 512), view("mti", a, a + 512), 15, OP.bitwise_and)

    def ix(k):
        return view("ix", k, k + 1)
    A_, PG2, G_, PI_, G16, A15, A32 = ix(0), ix(1), ix(2), ix(3), ix(4), ix(5), ix(6)
    iota(view("pi", 0, 1), [[0, 1]], 0, 1)
    iota(view("pi", 1, 2), [[0, 1]], 0, 2)
    ts(view("pi", 4, 6), view("pi", 0, 2), 15, OP.bitwise_and)
    ts(view("pi", 6, 8), view("pi", 0, 2), 4, OP.arith_shift_right)
    move(view("ix", 0, 4), view("pi", 4, 8))
    iota(view("qg"), [[1, 8], [0, 16]])
    iota(view("ee"), [[1, 17], [0, 16]])
    iota(view("cc"), [[0, 17], [16, 16]], 1, 1)
    iota(view("io640"), [[1, 640]])
    const(view("one"), 1, True)
    select(view("i128"), view("one"), [[-1, 128]], OP.is_equal, 0, 0, 1)
    ts(view("blk"), view("qg"), G_, OP.is_equal)
    ts(view("ee"), view("ee"), A_, OP.is_equal)
    iota(view("eye"), [[1, 16]])
    ts(view("eye"), view("eye"), A_, OP.is_equal)
    lin(G16, G_, 16.0, 1.0)
    const(view("zj"), 0, True)
    ts(view("zj", 15, 143, 16), view("qg", 0, 128, 16), G_, OP.is_equal)
    ts(view("b8f"), view("qg", 0, 128, 16), G_, OP.is_equal, -2048.0, OP.mult)

    def jj(i):
        return view("zj", 15 - i, 143 - i)

    def sel(kind, s, i):
        if kind == s == 0:
            return view("ex0", 128 * i, 128 * i + 128)
        c = WSET * SETS.index((kind, s))
        return view("sel", c + i, c + 2048, 16)

    def whole(k0, k1=None):
        return [view("sel", WSET * k, WSET * k + WSET) for k in range(k0, k1 or k0 + 1)]
    first = view("sel", 0, WSET // 4)
    do({"V": a_fill(first, 0)}, [], [first])
    for a in range(WSET // 4, 3 * WSET, WSET // 4):
        v = view("sel", a, a + WSET // 4)
        do({"V": a_fill(v, 0), "S": a_act(v, first), "G": a_iota(v, [[0, v[4]]])}, [first], [v])
    for a in range(10 * WSET, 11 * WSET, WSET // 4):
        const(view("sel", a, a + WSET // 4), 0, True)
    for s in range(4):
        c = WCMP * SETS.index((1, s))
        const(view("cmp", c, c + 2 * WCMP), 0, s < 2)
    move(view("inu"), view("inl", 0, 48))
    lin(view("code", 0, 4), view("inl", 0, 16, 4), 16.0, G16)
    tt(view("code", 4, 8), view("code", 0, 4), view("inl", 1, 16, 4), OP.add)

    def wave(n, k0, k1):
        last[0] = do({"Y": a_dma([(T.sel[16 * k:16 * k + 16, k0:k1, 256 * k:256 * k + WCMP], T.cmp[16 * k:16 * k + 16, WCMP * k0:WCMP * k1])
                                  for k in range(8)], "wave%d" % n, 0.15 * (k1 - k0))},
                     [view("cmp", WCMP * k0, WCMP * k1)], whole(k0, k1), after=last)

    def zeros(*sets):
        for k in sets:
            do({"Y": a_dma([(T.sel[:, k, :], T.sel[:, 10, :])], "dz%d" % k, 1.32)}, whole(10), whole(k), after=last)
    for s in range(4):
        cb, d = view("cb", 128 * s, 128 * s + 128), WCMP * SETS.index((1, s))
        scale(cb, view("blk"), view("code", 4 + s, 5 + s))
        if s:
            bank, c = view(psum(), 0, WCMP), WCMP * SETS.index((0, s))
            mms(bank, [(cb, view("ee"))])
            tt(view("cmp", c, c + WCMP), bank, view("cc"), OP.is_equal)
        else:
            bank = view(psum(), 0, 128)
            mms(bank, [(cb, view("i128"))])
            move(view("row"), bank)
            for a in range(16):
                ts(sel(0, 0, a), view("row"), view("cc", a, a + 1), OP.is_equal)
        move(view("cmp", d, d + 2 * WCMP, 17), view("eye"), idx=view("inu", 4 * s + 2, 4 * s + 4))
    zeros(3, 4)
    wave(0, 0, 3)
    wave(1, 3, 5)
    zeros(5, 6)
    wave(2, 5, 7)
    zeros(7, 8, 9)
    wave(3, 7, 11)

    move(view("lm"), view("eye"), idx=view("inu", 24, 48))
    lin(view("qsf", 8, 24), view("inl", 56, 72), 1.0 / 16384)
    move(view("wdb"), view("inl", 0, 16))
    for a in range(512, 1024, 256):
        const(view("res", a, a + 256), -1)
    for a in range(128, 640, 256):
        const(view("pzn", a, a + 256))
        const(view("xk", a, a + 256))
    const(view("cnt", 0, 1), 128)
    const(view("inc", 0, 2))
    const(view("neg1"), -1)
    const(view("z8"))
    const(view("zb"))
    const(view("b16"), 16)
    const(view("cap", 32, 36), 16)
    const(view("w16", 0, 512))
    const(view("w16", 512, 640), 16)
    iota(view("pg"), [[0, 16], [2, 8]])
    iota(view("c24"), [[16, 24]], 128)
    iota(view("c15"), [[-1, 16]], 15)
    iota(view("d15"), [[0, 8], [-1, 16]], 15)
    select(view("d15"), view("d15"), [[-1, 128]], OP.is_equal, 0, 0, 1)
    select(view("low"), view("d15"), [[-16, 8], [0, 16]], OP.is_ge, -256, 0, 1)
    select(view("low"), view("low"), [[16, 8], [0, 16]], OP.is_ge, -256, 15, -1)
    select(view("blki"), view("one"), [[0, 16], [-16, 8]], OP.is_ge, 0, 0, 1)
    select(view("blki"), view("blki"), [[0, 16], [16, 8]], OP.is_ge, 0, 15, -1)
    select(view("pmx"), view("one"), [[-1, 8], [-8, 16]], OP.is_equal, 0, 0, 1)
    for t in range(2):
        select(view("keep", 128 * t, 128 * t + 128), view("i128"), [[0, 8], [1, 16]], OP.not_equal, 0, -t, 0)
    select(view("keep", 256, 384), view("i128"), [[0, 8], [1, 16]], OP.is_ge, 0, -3, 0)
    ts(view("zb", 120, 128), view("qg", 0, 128, 16), G_, OP.is_equal)
    ts(view("blkpp"), view("pg"), PG2, OP.is_equal)
    ts(view("blkp"), view("qg"), 2.0, OP.mult, PG2, OP.is_equal)
    select(view("tlo"), view("blkp"), [[1, 8], [8, 16]], OP.is_gt, 0, 0, -1)
    iota(view("cst"), [[16, 16], [0, 8]], 1, 1)
    select(view("cst"), view("cst"), [[0, 16], [-16, 8]], OP.is_ge, -1, 0, 1)
    select(view("cst"), view("cst"), [[0, 16], [16, 8]], OP.is_ge, -1, 15, -1)
    lin(A15, A_, -1.0, 15.0)
    lin(A32, A_, 32.0)
    lin(view("k32"), view("io640", 0, 32), 1.0, A32)
    lin(view("own"), view("c24"), 1.0, PI_)
    lin(view("cnp"), view("own", 0, 8), 1.0, -639.0)
    lin(view("sm", 4, 5), A_, -1.0, 767.0)
    lin(view("nlneg"), view("c24", 0, 8), -1.0, view("sm", 4, 5))
    iota(view("num", 0, 128), [[1, 128]])

    turn = {"gb": 0, "ls": 0}

    def fresh(name, w):
        k = w * (turn[name] % (SCRATCH[name][1][1] // w))
        turn[name] += 1
        return k

    def pl(t):
        return view("pl", 8 * t, 8 * t + 8)

    def lookup(t, cnt):
        if t == 0:
            ts(view("kl"), view("inl", 48, 56), 1.0 / 128, OP.mult, -EPS, OP.add)
        else:
            ts(view("kl"), view("qsf", 8 * t, 8 * t + 8), cnt, OP.mult, -EPS, OP.add)
            scatter(view("xk"), pl(t - 1), view("xi", 128 * t - 128, 128 * t))
        tt(view("qgt"), view("xk") if t else view("xk", 0, 128), view("lm", 128 * t, 128 * t + 128), OP.mult, idx=view("kl"))
        bank = view(psum(), 0, 8)
        mms(bank, [(jj(i), view("qgt", i, 128, 16)) for i in range(16)])
        states(view("ql"), bank)

    def pass12(b):
        lst_ = view("inu", 16, 24) if b == 0 else view("ql")
        move(view("xl", 128 * b, 128 * b + 128), xw, lst_)
        if b < 3:
            step(view("xk", 0, 128) if b == 0 else view("xi", 128 * b - 128, 128 * b), lst_)
        for a in range(128 * b, 128 * b + 128, WIDE):
            step(view("yy", 16 * a, 16 * (a + WIDE)), view("xl", a, a + WIDE))

    def psel_x(b):
        out = fresh("ls", 128)
        for h in (0, 1):
            bank, c = view(psum(), 0, 64), 2048 * b + 1024 * h
            mms(bank, [(sel(0, 0, a), view("yy", c + a, c + 1024, 16)) for a in range(16)])
            states(view("ls", out + 64 * h, out + 64 * h + 64), bank)
        return out

    def psel_z(b, z, buf=None, walks=False):
        bank, out = view(psum(), 0, 128), None
        mms(bank, [(sel(0, 1 + z, a), view("yy", 2048 * b + a, 2048 * b + 2048, 16)) for a in range(16)], PARTS)
        if walks:
            out = fresh("ls", 128)
            states(view("ls", out, out + 128), bank)
        if buf:
            move(view(buf, 128 * b, 128 * b + 128), bank)
        return out

    def matched(t):
        out = fresh("ls", 128)
        states(view("ls", out, out + 128), view("pz%d" % t, 0, 128 * t + 256), view("ml"))
        return out

    def walk(s, src, w):
        mid, gb = fresh("ls", 128), fresh("gb", 2048)
        for h in (0, 1):
            bank, c = view(psum(), 0, 64), gb + 1024 * h
            for a in range(0, 64, w):
                step(view("gb", c + 16 * a, c + 16 * (a + w)), view("ls", src + 64 * h + a, src + 64 * h + a + w))
            mms(bank, [(sel(1, s, e), view("gb", c + e, c + 1024, 16)) for e in range(16)])
            states(view("ls", mid + 64 * h, mid + 64 * h + 64), bank)
        gb = fresh("gb", 2048)
        for a in range(0, 128, w):
            move(view("gb", gb + 16 * a, gb + 16 * (a + w)), ow, idx=view("ls", mid + a, mid + a + w))
        return gb

    def p4s(gb, out, c0, s, t=-1):
        for h in (0, 1):
            bank, c, o = view(psum(), 0, 64), gb + 1024 * h, c0 + 64 * h
            mms(bank, [(sel(2, s, e), view("gb", c + e, c + 1024, 16)) for e in range(16) if e != t]
                + ([(jj(t), view("gz%d" % t, o, o + 64))] if t >= 0 else []))
            move(view(out, o, o + 64), bank)

    def p4z(s, gb):
        bank, c = psum(), WSET * SETS.index((2, s))

        def fn(e):
            for k in range(16):
                r = e.matmul(ap(view(bank, k, 128, 16)), ap(view("gb", gb + k, gb + 2048, 16)), ap(view("sel", c + 17 * k, c + 2048, 256)), True, True)
            return r
        do({"P": (fn, (0, 0, 0, 0, 16 * 64, 0, 0), None)}, [view("gb", gb, gb + 2048)] + whole(c // WSET), [view(bank, 0, 128)])
        return view(bank, 0, 128)

    def compare(t):
        b, L = t + 1, 128 * (t + 1)
        q = view("rr", 128 * b, 128 * b + 128)
        act(view("r2", 0, L), view("rr", 0, L), scale=32.0, func=AF.Square)
        act(view("rq2"), q, scale=32.0, func=AF.Square)
        bank = view(psum(), 0, 8)
        mms(bank, [(view("zb", 120 - 8 * i, 248 - 8 * i), view("rq2", i, 128, 16)) for i in range(16)])
        tt(view("top"), view("own", 8 * t, 8 * t + 8), bank, OP.subtract)
        lin(view("nn"), bank, -1.0)
        for k in range(8):
            scale(view("lhb", k, 1024, 8), q, view("b8f", k, k + 1), free=True)
        for c in range(8):
            bank = view(psum(), 0, L)
            mms(bank, [(view("blki"), view("r2", 0, L)), (view("lhb", 128 * c, 128 * c + 128), view("rr", 0, L))])
            scan(view("sc", 384 * c, 384 * c + L), bank, view("neg1", 0, L), view("top", c, c + 1), OP.min, OP.add)

    def append(t):
        L = 128 * (t + 1)
        least = view("sc", L - 1, 3072, 384)
        bank = psum()
        cnt, tot = view(bank, 8, 9), view("inc", 9, 10)
        tt(view("uu"), least, view("nn"), OP.is_ge)
        tt(view("mn"), least, view("nn"), OP.subtract)
        scan(view("inc", 2, 10), view("uu"), view("z8"), 0.0, OP.add, OP.add)
        tt(view("ww"), view("uu"), view("cnp"), OP.mult)
        mms(cnt, [(view("i128"), view("cnt", t, t + 1)), (view("blkp"), tot)])
        mms(view(bank, 0, 8), [(view("blkp"), view("inc", 1, 9)), (view("tlo"), view("uu")), (view("i128"), view("nlneg")), (view("pmx"), view("ww"))])
        if t < 2:
            mms(view(bank, 9, 10), [(view("blkpp"), tot)])
        mb = view(psum(), 0, 8)
        mms(mb, [(view("pmx"), view("mn"))])
        move(pl(t), view(bank, 0, 8))
        if t < 2:
            lookup(t + 1, cnt)
            move(view("cnt", t + 1, t + 2), cnt)
            ts(view("cnp"), view("cnp"), view(bank, 9, 10), OP.add)
        else:
            ts(view("cap", 0, 32), view("k32"), cnt, OP.is_lt)
            lin(view("cap", 0, 32), view("cap", 0, 32), 17.0, -1.0)
        lin(view("ml"), mb, 1.0, float(L))
        move(view("num", L, L + 128), view("io640"), idx=pl(t))
        move(view("res", 128 * t, 128 * t + 128), view("num", 0, L + 128), idx=view("ml"))
        if t < 2:
            q = view("rr", L, L + 128)
            tt(q, view("w16"), q, OP.max, idx=pl(t))

    def in_order(win, src):
        move(view(win[0], win[1], win[1] + 128), view(src, 0, 128))
        for k in range(3):
            scatter(win, pl(k), view(src, 128 * k + 128, 128 * k + 256))

    def winner(t):
        mx, bank = view("sm", 1, 2), psum()
        if t:
            sc = view(bank, 128, 129)
            mms(view(bank, 0, 128), [(view("blk"), view("low")), (view("b16"), view("ne"))])
            mms(sc, [(view("d15"), view("one", 0, 1)), (view("ne"), view("b16", 0, 1))])
            reduce(mx, view(bank, 0, 128), OP.max)
        else:
            dc, sc = view("sm", 0, 1), view("sm", 2, 3)
            reduce(dc, view("ne"), OP.add)
            ts(view("dd2"), view("eye"), dc, OP.mult, 16.0, OP.mult)
            mms(view(bank, 0, 16), [(view("blk"), view("dd2")), (view("i128"), view("c15"))])
            lin(sc, dc, 16.0, A15)
            reduce(mx, view(bank, 0, 16), OP.max)
        oh, ws, bank = view("oh", t, t + 1), view("ws", 4 * t, 4 * t + 4), psum()
        ts(oh, sc, mx, OP.is_equal)
        scale(ws, view("wdb", 4 * t + 4, 4 * t + 8), oh)
        mms(view(bank, 0, 4), [(view("blk"), ws)])
        ts(view("mk", 4 * t, 4 * t + 2), view(bank, 2, 4), A_, OP.is_equal)
        ts(view("mk", 4 * t + 2, 4 * t + 3), view(bank, 2, 3), A_, OP.is_equal, -2048.0, OP.mult)
        scale(view("zo"), view("zj"), oh)
        if t == 0:
            ts(view("mk", 15, 16), view(bank, 0, 1), 16.0, OP.mult, view(bank, 1, 2), OP.add)

    def wpass(t, c0, c1):
        n = (c1 - c0) // 16
        h = (c1 - c0) // (2 if n > 16 else 1)
        bank, bank2 = view(psum(), 0, n), view(psum(), 0, n)
        mms(bank, [(view("zo", 15 - i, 143 - i), view("pw%d" % t, c0 + i, c1, 16)) for i in range(16)])
        states(view("lw", 0, n), bank)
        mk, mb = view("mk", 4 * t, 4 * t + 1), view("mk", 4 * t + 2, 4 * t + 3)
        for a in range(0, c1 - c0, h):
            lin(view("gw", a, a + h), xw, mk, mb, view("lw", a // 16, (a + h) // 16))
        mms(bank2, [(jj(i), view("gw", i, c1 - c0, 16)) for i in range(16)])
        states(view("lw2", 0, n), bank2)
        for a in range(0, c1 - c0, h):
            scale(view("gz%d" % t, c0 + a, c0 + a + h), ow, view("mk", 4 * t + 1, 4 * t + 2), idx=view("lw2", a // 16, (a + h) // 16))

    def rupdate(t):
        L = 128 * (t + 2)
        bank = view(psum(), 0, L)
        mms(bank, [(view("keep", 128 * t, 128 * t + 128), view("rr", 0, L)), (jj(t), view("gz%d" % t, 0, L))])
        move(view("rr", 0, L), bank)

    pass12(0)
    lookup(0, None)
    pass12(1)
    for b in (0, 1):
        p4s(walk(0, psel_x(b), WIDE), "rr", 128 * b, 0)
    for z in (1, 2):
        for b in (0, 1):
            psel_z(b, z, "pz%d" % z)
    compare(0)
    for b in (1, 0):
        p4s(walk(1, psel_z(b, 0, None, True), FINE), "an", 128 * b, 1)
    move(view("aq"), view("an", 128, 256))
    for t in range(3):
        b = t + 2
        append(t)
        if t:
            tt(view("ne"), p4z(1 + t, walk(1 + t, matched(t), FINE)), view("aq"), OP.not_equal)
        else:
            tt(view("ne"), view("an"), view("aq"), OP.not_equal, idx=view("ml"))
        winner(t)
        if t == 2:
            break
        pass12(b)
        gs = walk(0, psel_x(b), FINE)
        psel_z(b, t, "pw%d" % t)
        zs = psel_z(b, t + 1, "pz%d" % (t + 1), True)
        if t == 0:
            psel_z(b, 2, "pz2")
            scale(view("gz0", 0, 256), view("an"), view("oh", 0, 1))
            wpass(0, 256, 384)
        else:
            move(view("pw1", 0, 384), view("pz1"))
            wpass(1, 0, 512)
        rupdate(t)
        p4s(gs, "rr", 128 * b, 0, t)
        if t == 0:
            ts(view("ex0", 0, 2048, 16), view("cst"), G16, OP.subtract, view("mk", 15, 16), OP.is_equal)
            for k in (0, 1):
                scale(view("sel", WSET * k, WSET * k + 2048, 256), view("zj", 15, 143, 16), view("mk", k, k + 1))
        compare(t + 1)
        move(view("aq"), p4z(2 + t, walk(2 + t, zs, FINE)))
    in_order(view("pzn"), "pz2")
    in_order(view("res", 384, 1024), "rr")
    for a in (0, 256):
        move(view("pw2", a, a + 256), view("pzn", a, a + 256))
    wpass(2, 0, 512)

    send(learner, view("resl"), view("res", 0, 896), "ares", 1.2, 2)
    bank = psum()
    mms(view(bank, 32, 36), [(view("keep", 256, 384), view("wdb", 0, 4))] + [(jj(t), view("ws", 4 * t, 4 * t + 4)) for t in range(3)])
    mms(view(bank, 0, 32), [(jj(i), view("gz2", 32 * i, 32 * i + 32)) for i in range(16)])
    tt(view("fin"), view(bank, 0, 36), view("cap"), OP.min)
    send(learner, view("finl"), view("fin"), "afin", 0.1, 2)
    do({"Y": a_dma([(T.ym[:], T.resl[::16, 0:384])], "dym", 0.1)}, [view("resl")], [])
    rows = [(max(0, a - 13), min(128, a + 2)) for a in range(0, 144, 16)]
    do({"Y": a_dma([(T.yr[a:b, :], T.resl[a:b, 384:896]) for a, b in rows], "dyr", 0.7)}, [view("resl")], [])
    do({"Y": a_dma([(T.yr[2::16, :], T.finl[:, 0:32])], "dy2", 0.1)}, [view("finl")], [])
    do({"S": a_dma([(T.ye[:], T.finl[:, 32:36])], "dye", 0.1)}, [view("finl")], [])

    if "p" not in PLAN:
        PLAN["ops"] = ops
        PLAN["p"] = plan(ops)
    order, _, extra = PLAN["p"]
    pos = dict.fromkeys(queue, 0)
    seen = {q: {} for q in queue}
    run, tok = dict(order), {}
    for i, q in order:
        o = ops[i]
        want = {}
        for d in list(o["deps"]) + [d for d in o["soft"] if run[d] != q] + [d for d in extra.get(i, []) if run[d] + q != "PP"]:
            s, n = tok[d]
            want[s] = max(want.get(s, 0), n)
        for s in sorted(want):
            if seen[q].get(s, 0) < want[s]:
                queue[q].wait_ge(T.sem[s], want[s])
                seen[q][s] = want[s]
        r = o["alt"][q][0](queue[q])
        tok[i] = o["alt"][q][2]
        if tok[i] is None:
            pos[q] += 1
            r.then_inc(T.sem[CSEM[q]], 1)
            tok[i] = (CSEM[q], pos[q])
    for s, n in (("dym", 1), ("dyr", len(rows)), ("dy2", 1), ("dye", 1)):
        g.sync.wait_ge(T.sem[s], 16 * n)
    g.wait_ge(T.sem.sent, sent[0])
    for q in sorted(CSEM):
        g.wait_ge(T.sem[CSEM[q]], pos[q])
